import numpy as np, ml_dtypes
CORES = [2,3,42,43,82,83,122,123]
N = 8
BF = ml_dtypes.bfloat16
W, C, K, VISITS = 2048, 2048, 256, 4
LEV = np.arange(16).reshape(1, 1, 16, 1)
HC = 39 + 14 * LEV
UC = 5 + 10 * LEV
SIZES = np.array([1, 1, 2, 2, 3, 4, 6, 8, 16, 32, 64, 128, 256, 512, W, W]).reshape(1, 1, 16, 1)
def take(a, i):
    return np.take_along_axis(a, i, a.ndim - 1)
def cell(z):
    return (255 + np.add.reduce(HC * z, axis=2)) & (C - 1)
def first(keys):
    return np.unique(keys, return_index=True)[1]
def parts(rng, amp=12):
    pool = np.argsort(rng.random((8, 16, W)), axis=-1); pl = np.broadcast_to(pool[None], (N, 8, 16, W))
    fo = np.where(rng.random((N, 8, W)) < 0.6, np.arange(W), rng.integers(0, W, (N, 8, W)))
    la = take(pl, (rng.random((N, 8, 16, K)) * SIZES).astype(np.int64)); bk = take(pl, (rng.random((N, 8, 16, C)) * SIZES).astype(np.int64))
    cen = rng.integers(40, 216, (1, 8, 16, 1))
    far = rng.random((N, 8, 1, W)) < 0.06
    for q in range(N):
        for g in range(8):
            far[q, g, 0, fo[q, g, pool[g, :4, :2].reshape(-1)]] = False
    x = np.where(far, rng.integers(0, 256, (N, 8, 16, W)), cen + rng.integers(-amp, amp + 1, (N, 8, 16, W)))
    z = np.where(rng.random((N, 8, 1, K)) < 0.04, rng.integers(0, 256, (N, 8, 16, K)), cen + rng.integers(-amp, amp + 1, (N, 8, 16, K)))
    t = 235 - 4 * LEV + rng.integers(0, 4, (N, 8, 16, 1))
    c = cell(z); same = rng.random((N, 8, K)) < 0.15
    for q in range(N):
        for g in range(8):
            j = np.flatnonzero(same[q, g]); j = j[first(c[q, g, j])]
            bk[q, g][:, c[q, g, j]] = la[q, g][:, j]
    return x, fo, bk, la, z, t
def pack(x, fo, bk, la, z, t):
    return {"x": np.ascontiguousarray(x.reshape(N, 128, W)).astype(np.float32).astype(BF), "fw": np.ascontiguousarray(fo).astype(np.int32),
            "bk": np.ascontiguousarray(bk.reshape(N, 128, C)).astype(np.int32), "la": np.ascontiguousarray(la.reshape(N, 128, K)).astype(np.int32),
            "zz": np.ascontiguousarray(z.reshape(N, 128, K)).astype(np.float32).astype(BF), "th": np.ascontiguousarray(t.reshape(N, 128, 1)).astype(np.int32)}
def setup_inputs(rng):
    return pack(*parts(rng))
def setup_inputs_spread(rng):
    x = np.minimum((np.exp2(8 * rng.random((N, 8, 1, W))) * rng.random((N, 8, 16, W))).astype(np.int64), 255)
    z = np.minimum((np.exp2(8 * rng.random((N, 8, 1, K))) * rng.random((N, 8, 16, K))).astype(np.int64), 255)
    t = -np.sort(-np.minimum(np.exp2(12 * rng.random((N, 8, 16, 1))).astype(np.int64), 4080), axis=2)
    fo = rng.integers(0, W, (N, 8, W)); la = (W * rng.random((N, 8, 16, K)) ** 3).astype(np.int64); bk = (W * rng.random((N, 8, 16, C)) ** 3).astype(np.int64)
    return pack(x, fo, np.minimum(bk, W - 1), np.minimum(la, W - 1), z, t)
def setup_inputs_ends(rng):
    def both(n):
        k = rng.integers(0, 3, (N, 8, 1, n)); return np.where(k == 0, 0, np.where(k == 1, 255, 255 * rng.integers(0, 2, (N, 8, 16, n))))
    x, z = both(W), both(K)
    fo = (W - 1) * rng.integers(0, 2, (N, 8, W)); bk = (W - 1) * rng.integers(0, 2, (N, 8, 16, C)); la = (W - 1) * rng.integers(0, 2, (N, 8, 16, K))
    t = 4080 * (rng.random((N, 8, 16, 1)) < rng.choice(np.array([0.5, 0.8, 0.95]), (N, 8, 1, 1))).astype(np.int64)
    t[N - 1, 7] = 4080; t[:, 6] = 4080; t[:, 6, 15] = 0
    near = (255 * (16 - np.arange(16) // 2) - 1 + np.arange(16) % 2).reshape(16, 1)
    for g, o in ((3, 1), (5, -1)):
        z[:, g] = 255 * (np.argsort(rng.random((N, 16, K)), axis=1) < np.argsort(rng.random((N, 1, K)), axis=-1) % 17)
        t[:, g] = near[::o]
    x[:, 1::2, :, 0] = 0; x[:, 1::2, :, W - 1] = 255; fo[:, 1::2, 0] = 0; fo[:, 1::2, W - 1] = W - 1
    z[..., K - 1] = 0; la[..., K - 1] = W - 1; z[..., K - 2] = 255; la[..., K - 2] = 0
    bk[:, 1::2, :, 255] = 0; bk[:, 1::2, :, C - 1] = W - 1
    return pack(x, fo, bk, la, z, t)
def setup_inputs_corners(rng):
    x, fo, bk, la, z, t = parts(rng); a = np.arange(W)
    pat = [a, 0 * a, 0 * a + W - 1, np.maximum(a - 1, 0), W - 1 - a, (a + 1) % W, a ^ 1]
    kind = rng.integers(0, 4, (N, 8)); kind[0] = (1, 0, 2, 3, 1, 3, 0, 1)
    r = rng.random((N, 8, 1, K)); la = np.where(r < 0.1, 0, np.where(r < 0.2, W - 1, la))
    z[..., K - 1] = z[..., 0]; c = cell(z)
    for q in range(N):
        for g in range(8):
            i = (g + q) % 8
            if i < 7: fo[q, g] = pat[i]
            if kind[q, g] == 1: t[q, g] = 4080
            if kind[q, g] == 2: t[q, g] = 0
            if kind[q, g] == 3: t[q, g] = np.where(LEV[0, 0] < rng.integers(1, 16), 4080, 0)
            for j in rng.permutation(K)[:8]:
                bk[q, g][:, c[q, g, j]] = la[q, g][:, j]; bk[q, g, 15, c[q, g, j]] = rng.integers(0, W)
    return pack(x, fo, bk, la, z, t)
def setup_inputs_crowd(rng):
    x, fo, bk, la, z, t = parts(rng)
    for q in range(N):
        for g in range(8):
            k = g % 4; j = K - 1 if q == 0 else int(rng.integers(0, K))
            if k != 3: z[q, g] = z[q, g][:, :1].copy(); la[q, g] = la[q, g][:, :1].copy()
            if k == 2: t[q, g] = 0
            else: fo[q, g] = np.arange(W); la[q, g, 0] = W - 1; t[q, g, 0] = 4080
            c = (255 + np.add.reduce(HC[0, 0] * z[q, g], axis=0)) & (C - 1)
            if k in (0, 1): bk[q, g][:, c[0]] = la[q, g][:, 0]; bk[q, g, 0, c[0]] = rng.integers(0, W - 1)
            if k == 3: bk[q, g, 0] = rng.integers(0, W - 1, C)
            if k == 1 or (k == 3 and q % 2 == 1): la[q, g][:, j] = bk[q, g][:, c[j]]
    return pack(x, fo, bk, la, z, t)
def setup_inputs_ties(rng):
    x, fo, bk, la, z, t = parts(rng, 1)
    t = -np.sort(-rng.integers(14, 25, (N, 8, 16, 1)), axis=2)
    for g in (2, 6):
        mid = rng.integers(40, 216, (16, 1)); fo[:, g] = np.arange(W)
        x[:, g] = mid + rng.integers(-1, 2, (N, 16, W)); z[:, g] = mid + rng.integers(-1, 2, (N, 16, K))
    t[:, 2] = 22 - LEV[0, 0] // 2
    for q in range(N):
        a = rng.integers(0, W - 1, (16, 1)); la[q, 2] = a; bk[q, 2] = a
        x[q, 2, :, W - 1] = x[q, 2, :, int(a[0, 0])]
        j = rng.permutation(K)[:1 + q % 3]; la[q, 2, 0, j] = W - 1; z[q, 2][:, j] = x[q, 2, :, W - 1:]
    la[:, 6] = rng.integers(0, W, (N, 16, K)); bk[:, 6] = rng.integers(0, W, (N, 16, C)); t[:, 6] = 9
    return pack(x, fo, bk, la, z, t)
def check_inputs(d):
    bad = []
    for k, hi in (("x", 255), ("fw", W - 1), ("bk", W - 1), ("la", W - 1), ("zz", 255), ("th", 4080)):
        v = np.asarray(d[k]).astype(np.float64)
        if not (np.min(v) >= 0 and np.max(v) <= hi): bad.append("range of " + k)
        elif np.any(v != np.floor(v)): bad.append("whole numbers of " + k)
    return bad
def reference(x, fw, bk, la, zz, th):
    X = x.astype(np.float32).astype(np.int32).reshape(N, 8, 16, W); Z = zz.astype(np.float32).astype(np.int32).reshape(N, 8, 16, K)
    F = fw.astype(np.int64).reshape(N, 8, W); B = bk.astype(np.int64).reshape(N, 8, 16, C); L = la.astype(np.int64).reshape(N, 8, 16, K)
    T = th.astype(np.int64).reshape(N, 8, 16, 1); A = np.zeros((N, 8, 1, 1), np.int64)
    for v in range(VISITS):
        if v > 0:
            s = 1 + (v - 1) % (N - 1); L = np.roll(L, s, axis=0); Z = np.roll(Z, s, axis=0)
        L = take(F, L.reshape(N, 8, 16 * K)).reshape(N, 8, 16, K)
        c = cell(Z)
        G = take(F, take(B, c[:, :, None, :]).reshape(N, 8, 16 * K)).reshape(N, 8, 16, K)
        d = np.add.reduce(np.abs(take(X, L.reshape(N, 8, 1, 16 * K)).reshape(N, 8, 16, 16, K) - Z[:, :, :, None, :]), axis=2)
        e = np.add.reduce(np.abs(take(X, G.reshape(N, 8, 1, 16 * K)).reshape(N, 8, 16, 16, K) - Z[:, :, :, None, :]), axis=2)
        fail = d > T + (A & 15); ks = np.where(np.any(fail, axis=2), np.argmax(fail, axis=2), 16)
        good = (G != L) & (e <= T); m = np.where(np.any(good, axis=2), np.argmax(good, axis=2), 16)
        merge = m < ks
        u = ((255 + np.add.reduce(UC * Z, axis=2)) & 1023)[:, :, None, :]
        new = np.where(LEV >= ks[:, :, None, :], (((L * u) >> 5) + L + 613 * LEV) & (W - 1), L)
        w = np.take_along_axis(new, np.minimum(ks, 15)[:, :, None, :], 2)
        val = np.where(ks[:, :, None, :] < 16, Z, (take(X, w) + Z) >> 1)
        mm = np.minimum(m, 15)[:, :, None, :]; gm = np.take_along_axis(G, mm, 2); lm = np.take_along_axis(L, mm, 2)
        hi = np.maximum(gm, lm)[:, :, 0]; lo = np.minimum(gm, lm)[:, :, 0]
        Z = np.where(m[:, :, None, :] < 16, (Z + take(X, gm)) >> 1, Z)
        for q in range(N):
            for g in range(8):
                j = first(w[q, g, 0]); X[q, g][:, w[q, g, 0, j]] = val[q, g][:, j]
                j = first(c[q, g]); B[q, g][:, c[q, g, j]] = new[q, g][:, j]
                j = np.flatnonzero(merge[q, g]); j = j[first(hi[q, g, j])]; F[q, g, hi[q, g, j]] = lo[q, g, j]
        A = np.add.reduce(merge.astype(np.int64), axis=2)[:, :, None, None]
        L = new
    return {"yx": X.reshape(N, 128, W).astype(np.float32).astype(BF), "yf": F.astype(np.float32), "yb": B.reshape(N, 128, C).astype(np.float32),
            "yl": L.reshape(N, 128, K).astype(np.float32), "yz": Z.reshape(N, 128, K).astype(np.float32).astype(BF)}

@@ -1,0 +1,610 @@
+from concourse.bass import DstId, RemoteDMATransfer
+from concourse.mybir import dt, AluOpType, AxisListType, ActivationFunctionType
+
+W, K, VISITS = 2048, 256, 4
+BIG = float(2 ** 17)
+ROUND = 1.5 * 2 ** 23
+XO, DO, ZO = W, 2 * W, 2 * W + 32
+F32, BF16, I32, U16, F16 = "float32", "bfloat16", "int32", "uint16", "float16"
+
+SCRATCH = {
+    "pL": ("psum", [128, 2, 256], F32), "pG": ("psum", [128, 2, 512], F32), "pA": ("psum", [128, 512], F32),
+    "pB": ("psum", [128, 512], F32), "pC": ("psum", [128, 512], F32), "pD": ("psum", [128, 512], F32),
+    "pS": ("psum", [128, 512], F32),
+}
+
+
+def _sb(dtype, **kw):
+    for n, s in kw.items():
+        SCRATCH[n] = ("sbuf", [128] + (list(s) if isinstance(s, tuple) else [s]), dtype)
+
+
+_sb(BF16, tab=ZO + K, xf=W, hh=W, gm=8192, gh=8192, zrep=4096, v1=(16, 32), fl=256,
+    z0=K, z1=K, z2=K, z3=K, zs0=K, zs1=K, zs2=K, zs3=K,
+    ones=128, idb=128, rz=256, r8=96, selz=144, pair=128, fi=128, mb=512, ol1=512, ol2=512, og1=384, og2=128,
+    nm=16, a15=256, blkn=128, cu=32, lb=32)
+_sb(F32, bt=W + 32, ident=128, blk=128, maske=256, ri=128, re_=128, rw=8, seg=512, rst=512, stp=256, ck=256, zl=16,
+    cols=16, tf=256, urep=256, kf=512, ss=256, sg=512, nw=256, nk=256, sq=256, cc=256, zb=256,
+    uw=256, uh=256, uc=256, ew=256, eh=256, ec=256, ez=256, ev=256, sm=160, pr=512, s2=128, fo=128)
+_sb(I32, bi=W, fi2=128, li=K, ti=8, ia=256, ib=256, rr=256, qi=128, ai=128)
+_sb(U16, l0=K, l1=K, l2=K, l3=K, ls0=K, ls1=K, ls2=K, fw16=128, bc=K, ex=16, exl=16, o1=32, o2=32, oc=16, oz=16, ov=16)
+_sb(BF16, ul=256)
+_sb(F16, h1=256, h2=256)
+
+SEMAPHORES = (["pe", "dve", "act", "pool", "sent"] + ["d%d" % i for i in range(24)]
+              + ["al%d" % i for i in range(1, VISITS)] + ["az%d" % i for i in range(1, VISITS)])
+SAME_QUEUE_WAW = True
+SPLIT = (512, 6, 10)
+A = AluOpType
+FN = ActivationFunctionType
+
+
+def rank_program(g, core, T, topo):
+    rank = T.rank_of(core)
+    if rank is None:
+        return
+    n_ranks = len(T.cores)
+    ops = []
+    ndma = [0]
+
+    def V(name, *idx, part=slice(None)):
+        shape = SCRATCH[name][1][1:]
+        full = list(idx) + [slice(None)] * (len(shape) - len(idx))
+        lo = hi = 0
+        stride = 1
+        for d in range(len(shape) - 1, -1, -1):
+            r = range(shape[d])[full[d]]
+            if isinstance(r, int):
+                lo += r * stride; hi += r * stride
+            else:
+                lo += r[0] * stride; hi += r[-1] * stride
+            stride *= shape[d]
+        if SCRATCH[name][0] == "psum":
+            lo, hi = lo // 512 * 512, hi // 512 * 512 + 511
+        return {"ap": T[name][(part,) + tuple(full)], "reg": [(name, lo, hi + 1)], "also": []}
+
+    def S(a, b, s=1):
+        return slice(a, b, s)
+
+    def ind(win, off):
+        return {"ap": win["ap"].indirect(off["ap"]), "reg": win["reg"], "also": off["reg"]}
+
+    def rec(eng, fn, outs, ins, sem=None, count=1, ext=False):
+        w, r = [], []
+        for o in outs:
+            w += o["reg"]; r += o["also"]
+        for i in ins:
+            if isinstance(i, dict):
+                r += i["reg"] + i["also"]
+        ops.append({"eng": eng, "fn": fn, "w": w, "r": r, "sem": sem, "count": count, "ext": ext})
+
+    def ap(x):
+        return x["ap"] if isinstance(x, dict) else x
+
+    def tt(o, a, b, op):
+        rec("dve", lambda: g.vector.tensor_tensor(ap(o), ap(a), ap(b), op), [o], [a, b])
+
+    def ts(o, a, s1, op0, s2=None, op1=None):
+        if op1 is None:
+            rec("dve", lambda: g.vector.tensor_scalar(ap(o), ap(a), ap(s1), None, op0), [o], [a, s1])
+        else:
+            rec("dve", lambda: g.vector.tensor_scalar(ap(o), ap(a), ap(s1), ap(s2), op0, op1), [o], [a, s1, s2])
+
+    def cp(o, a):
+        rec("dve", lambda: g.vector.tensor_copy(ap(o), ap(a)), [o], [a])
+
+    def ms(o, c):
+        rec("dve", lambda: g.vector.memset(ap(o), c), [o], [])
+
+    def scan(o, d0, d1, init, op0, op1):
+        rec("dve", lambda: g.vector.tensor_tensor_scan(ap(o), ap(d0), ap(d1), init, op0, op1), [o], [d0, d1])
+
+    def act(o, a, func=FN.Identity, bias=0.0, scale=1.0):
+        rec("act", lambda: g.scalar.activation(ap(o), ap(a), func, bias=ap(bias), scale=ap(scale)), [o], [a, bias, scale])
+
+    def mm(o, l, r, start, stop):
+        rec("pe", lambda: g.tensor.matmul(ap(o), ap(l), ap(r), start, stop), [o], [l, r])
+
+    def iota(o, pat, base, cm):
+        small = SCRATCH[o["reg"][0][0]][2] != I32
+        if small:
+            rec("pool", lambda: g.iota(ap(o), pat, base, cm, allow_small_or_imprecise_dtypes=True), [o], [])
+        else:
+            rec("pool", lambda: g.iota(ap(o), pat, base, cm), [o], [])
+
+    def asel(o, a, pat, op, fill, base, cm):
+        rec("pool", lambda: g.affine_select(ap(o), ap(a), pat, op, fill, base, cm), [o], [a])
+
+    def dma(q, o, a):
+        sem = "d%d" % ndma[0]
+        ndma[0] += 1
+        e = {"sync": g.sync, "act": g.scalar, "pool": g}[q]
+        rec(q, lambda: e.dma_start(ap(o), ap(a)), [o] if isinstance(o, dict) else [], [a], sem=sem, count=16)
+
+    def lanes_mask(src, dst):
+        eng = [e for e in topo.engines(src, dst) if all(e in topo.engines(src, c) for c in T.cores if c != src)]
+        return sum(1 << e for e in eng), len(eng)
+
+    nsent = [0]
+
+    def send(src, land, sem, v):
+        s = 1 + (v - 1) % (n_ranks - 1)
+        dst = T.cores[(rank + s) % n_ranks]
+        rid, pid, _ = topo.addr(dst)
+        mask, n = lanes_mask(core, dst)
+        nsent[0] += n
+        rec("pool", lambda: g.remote_dma(T[land][:], T[src][:], T.sem[sem], T.sem.sent, pid, rid, mask), [], [V(src)], sem="")
+
+    def arrive(land, sem, v):
+        s = 1 + (v - 1) % (n_ranks - 1)
+        n = lanes_mask(T.cores[(rank - s) % n_ranks], core)[1]
+        rec("ext", None, [V(land)], [], sem=sem, count=n, ext=True)
+
+    col = lambda i: V("cols", S(i, i + 1))
+    sm = lambda i, n=1: V("sm", S(16 * i, 16 * (i + n)))
+    qi = lambda i, n=1: V("qi", S(16 * i, 16 * (i + n)))
+
+    dma("sync", V("fi2"), T.fw[:])
+    dma("act", V("z0"), T.zz[:])
+    dma("sync", V("tab", S(XO, XO + W)), T.x[:])
+    dma("act", V("li"), T.la[:])
+    dma("act", V("ti", S(0, 1)), T.th[:])
+    ms(V("tab", S(0, W)), 0.0)
+    dma("act", V("bi"), T.bk[:])
+
+    iota(V("ia", S(0, 1)), [[0, 1]], 0, 1)
+    ms(V("ident"), 1.0)
+    ms(V("ones"), 1.0)
+    asel(V("blk"), V("ident"), [[-16, 8], [0, 16]], A.is_ge, 0.0, 0, 1)
+    asel(V("blk"), V("blk"), [[16, 8], [0, 16]], A.is_ge, 0.0, 15, -1)
+    asel(V("ident"), V("ident"), [[-1, 128]], A.is_equal, 0.0, 0, 1)
+    ts(V("ai"), V("fi2"), 255, A.bitwise_and)
+    ts(V("qi"), V("fi2"), 1792, A.bitwise_and)
+    cp(V("fl", S(0, 128)), V("ai"))
+    cp(V("fl", S(128, 256)), V("qi"))
+    dma("sync", V("tab", S(0, W), part=S(8, 128, 16)), V("fl", S(0, 128)))
+    dma("sync", V("tab", S(0, W), part=S(9, 128, 16)), V("fl", S(128, 256)))
+    ts(V("ib", S(0, 1)), V("ia", S(0, 1)), 15, A.bitwise_and)
+    cp(col(0), V("ib", S(0, 1)))
+    ts(col(1), col(0), 8.0, A.is_lt)
+    ts(col(2), col(0), 7.5, A.is_gt)
+    ts(col(3), col(0), 9.5, A.is_lt)
+    tt(col(2), col(2), col(3), A.mult)
+    blk8 = V("blk", S(0, 128, 16))
+    ms(V("selz"), 0.0)
+    ts(V("selz", S(15, 143, 16)), blk8, col(2), A.mult)
+    asel(V("tf", S(0, 128)), V("blk"), [[-16, 8], [-2, 16]], A.is_ge, 0.0, 0, 1)
+    asel(V("pair"), V("tf", S(0, 128)), [[16, 8], [2, 16]], A.is_ge, 0.0, 1, -1)
+    iota(V("ia", S(16, 32)), [[1, 16]], 0, 0)
+    iota(V("zl"), [[128, 2], [0, 8]], ZO - XO, 1)
+    iota(V("kf", S(0, 256)), [[0, 16], [1, 16]], 0, 0)
+    ts(V("fi"), V("ident"), col(2), A.mult)
+    ts(col(4), col(1), -256.0, A.mult)
+    ts(col(5), col(0), 14.0, A.mult, 39.0, A.add)
+    ts(col(6), col(0), 20.0, A.mult, 10.0, A.add)
+    ts(col(7), col(0), float(DO), A.add)
+    ts(col(8), col(0), float(DO + 16), A.add)
+    ts(col(9), col(0), float(W + 16), A.add)
+    ts(col(10), col(0), 9.0, A.is_equal, 16.0, A.mult)
+    ts(col(11), col(0), -4096.0, A.mult, 65536.0, A.add)
+    r8 = lambda i, n=1: V("r8", S(8 * i, 8 * (i + n)))
+    ts(r8(0), blk8, 2 * BIG, A.mult)
+    ts(r8(1), blk8, -2 * BIG, A.mult)
+    ts(r8(2), blk8, col(1), A.mult, -BIG, A.mult)
+    ts(r8(3), blk8, col(2), A.mult, -1.0, A.mult)
+    cp(V("idb"), V("ident"))
+    ts(r8(5), blk8, col(1), A.mult, BIG, A.mult)
+    ts(r8(6), blk8, col(2), A.mult)
+    ts(r8(7), blk8, col(2), A.mult)
+    ts(r8(8), blk8, col(5), A.mult)
+    ts(r8(9), blk8, col(6), A.mult)
+    cp(V("l0"), V("li"))
+    cp(V("ex"), V("ia", S(16, 32)))
+    ts(V("exl"), V("ia", S(16, 32)), col(10), A.add)
+    ts(V("rz", S(0, 128)), V("blk"), -BIG, A.mult)
+    ts(V("rz", S(128, 256)), V("blk"), BIG, A.mult)
+    ms(V("cu", S(0, 16)), 255.0)
+    ms(V("cu", S(16, 32)), 510.0)
+    cp(V("rw"), blk8)
+    ts(V("maske"), V("kf", S(0, 256)), col(0), A.is_equal)
+    ts(V("ti", S(1, 2)), V("ti", S(0, 1)), 2048.0, A.add)
+    ts(V("ti", S(2, 3)), V("ti", S(1, 2)), 127, A.bitwise_and)
+    ts(V("ti", S(3, 4)), V("ti", S(1, 2)), 8064, A.bitwise_and)
+    cp(V("cols", S(12, 14)), V("ti", S(2, 4)))
+    ts(col(14), col(12), 1.0, A.add)
+    ts(col(12), col(12), 0.5, A.add)
+    for nm_ in ("ol1", "ol2", "og1", "og2"):
+        ms(V(nm_), 0.0)
+    for h in range(2):
+        ts(V("ol1", S(256 * h, 256 * h + 128)), V("ident"), col(13), A.mult, -BIG, A.mult)
+        ts(V("ol2", S(256 * h, 256 * h + 128)), V("ident"), col(12), A.mult, -BIG, A.mult)
+    ts(V("og1", S(0, 128)), V("ident"), col(13), A.mult, BIG, A.mult)
+    ts(V("og1", S(128, 256)), V("ident"), col(11), A.mult)
+    ts(V("og2", S(0, 128)), V("ident"), col(14), A.mult, BIG, A.mult)
+
+    def late_constants():
+        kk = V("kf", S(0, 256))
+        act(V("ri"), V("ident"), FN.Identity, scale=1.0 / 64)
+        act(V("re_"), V("blk"), FN.Identity, scale=-1.0 / 64)
+        act(V("ck"), kk, FN.Identity, scale=613.0 * 32)
+        ms(V("ri", S(15, 128, 16)), 0.0)
+        ms(V("re_", S(15, 128, 16)), 0.0)
+        ts(V("mb", S(0, 256)), kk, col(0), A.is_ge, 128.0, A.mult)
+        ms(V("stp"), 4096.0)
+        ms(V("seg"), 1.0)
+        ms(V("rst"), 0.0)
+        ms(V("mb", S(15, 256, 16)), 0.0)
+        ms(V("stp", S(0, 256, 16)), -1e9)
+        ms(V("seg", S(0, 512, 16)), 0.0)
+        ms(V("rst", S(15, 512, 16)), 1.0)
+        act(V("mb", S(256, 512)), V("mb", S(0, 256)), FN.Copy)
+        asel(V("blkn"), V("ones"), [[-1, 8], [0, 16]], A.is_equal, 0.0, 0, 1)
+        ts(V("blkn"), V("blkn"), -BIG, A.mult)
+
+    def spread_z(v, levels, eng):
+        a = V("z%d" % v)
+        for k in levels:
+            o = dict(V("zrep", S(k, 4096, 16)), reg=[("zrep", k, k + 1)])
+            if eng == "act":
+                act(o, a, FN.Copy)
+            elif eng == "dve":
+                cp(o, a)
+            else:
+                asel(o, a, [[0, K]], A.is_ge, 0.0, 0, 0)
+
+    def fw_mm(wrapped):
+        for p in range(16):
+            rhs = V("tab", S(p, W, 16)) if wrapped else V("tab", S(128 * p, 128 * p + 128))
+            mm(V("pD", S(0, 128)), V("selz", S(15 - p, 143 - p)), rhs, p == 0, p == 15)
+
+    hbank = [V("pA"), V("pB"), V("pG", 0), V("pG", 1)]
+    XW = V("tab", S(XO, XO + W))
+
+    def xf_part(a, b, eng):
+        src = ind(XW, V("fw16", S(a // 16, b // 16)))
+        if eng == "dve":
+            cp(V("xf", S(a, b)), src)
+        else:
+            act(V("xf", S(a, b)), src, FN.Copy)
+
+    def h_mm(j):
+        mm(hbank[j], V("fi"), V("tab", S(512 * j, 512 * j + 512)), True, False)
+        mm(hbank[j], V("pair"), V("xf", S(512 * j, 512 * j + 512)), False, True)
+
+    def h_cp(j):
+        act(V("hh", S(512 * j, 512 * j + 512)), hbank[j], FN.Identity, bias=col(4))
+
+    def cell_mm(v):
+        mm(V("pC", S(288, 320)), V("idb"), V("cu"), True, False)
+        for wh in range(2):
+            for h in range(2):
+                o = 288 + 16 * wh + 8 * h
+                mm(V("pC", S(o, o + 8)), V("z%d" % v, S(128 * h, 128 * h + 128)), r8(8 + wh), False, wh + h == 2)
+
+    def cell_act():
+        y1, y2 = V("s2", S(64, 96)), V("s2", S(96, 128))
+        act(y1, V("pC", S(288, 320)), FN.Identity, bias=2.0 ** -12 - 0.5, scale=1 / 2048)
+        act(y2, y1, FN.Identity, bias=ROUND)
+        act(y1, y2, FN.Identity, bias=2048 * ROUND, scale=-2048.0)
+
+    def cell_small():
+        tt(sm(0, 2), V("pC", S(288, 320)), V("s2", S(64, 96)), A.add)
+
+    def e_op(name, src):
+        tt(V(name), ind(src, V("ex")), V("maske"), A.mult)
+
+    def u_op(name, src):
+        act(V(name), ind(src, V("ex")), FN.Copy)
+
+    def w_mm(name, ps, o):
+        for h in range(2):
+            mm(V(ps, S(o + 8 * h, o + 8 * h + 8)), V(name, S(128 * h, 128 * h + 128)), V("rw"), True, True)
+
+    def dif_open(ps, n):
+        mm(V(ps, S(0, n)), V("idb"), V("mb", S(0, n)), True, False)
+
+    def dif_mm(e, u, ps, o, stop):
+        for name, rhs in ((e, "re_"), (u, "ri")):
+            for h in range(2):
+                mm(V(ps, S(o + 128 * h, o + 128 * h + 128)), V(name, S(128 * h, 128 * h + 128)), V(rhs), False,
+                   stop and name == u and h == 1)
+
+    def contest(ps, n, wv, dcol):
+        scan(V("pr", S(0, 256 * n)), V(ps, S(0, 256 * n)), V("rst", S(0, 256 * n)), 1.0, A.mult, A.add)
+        ts(V("s2", S(0, 16 * n)), V("pr", S(14, 256 * n, 16)), 0.0, A.is_equal, dcol, A.mult)
+        tt(V("s2", S(32, 32 + 16 * n)), wv, V("s2", S(0, 16 * n)), A.max)
+
+    def open_l(v):
+        mm(V("pL"), V("ones"), V("ol1"), True, False)
+        mm(V("pL"), V("ones"), V("ol2"), False, False)
+        for h in range(2):
+            mm(V("pL", h, S(0, 128)), V("z%d" % v, S(128 * h, 128 * h + 128)), V("rz", S(0, 128)), False, False)
+            if v > 0:
+                for i in range(2):
+                    mm(V("pL", h, S(0, 128)), V("a15", S(128 * i, 128 * i + 128), part=S(0, 8)), V("blkn", part=S(0, 8)), False, False)
+
+    def open_g(v):
+        for h in range(2):
+            mm(V("pG", h, S(0, 384)), V("ones"), V("og1"), True, False)
+            mm(V("pG", h, S(0, 128)), V("ones"), V("og2", S(0, 128)), False, False)
+            mm(V("pG", h, S(0, 128)), V("z%d" % v, S(128 * h, 128 * h + 128)), V("rz", S(128, 256)), False, False)
+
+    def offs(v, side, h):
+        return V("l%d" % v if side == 0 else "bc", S(128 * h, 128 * h + 128))
+
+    def g_max(v, side, h):
+        o = 4096 * side + 2048 * h
+        tt(V("gm", S(o, o + 2048)), ind(V("xf"), offs(v, side, h)),
+           dict(V("zrep", S(2048 * h, 2048 * h + 2048)), reg=[("zrep", 0, 16)]), A.max)
+
+    def g_h(v, side, h):
+        o = 4096 * side + 2048 * h
+        act(V("gh", S(o, o + 2048)), ind(V("hh"), offs(v, side, h)), FN.Copy)
+
+    def m_mm(side, h):
+        o = 4096 * side + 2048 * h
+        for k in range(16):
+            mm(V("pG" if side else "pL", h, S(k, 128, 16)), V("gm", S(o + k, o + 2048, 16)), r8(side), False, False)
+
+    def hl_mm(h):
+        o = 2048 * h
+        for k in range(16):
+            mm(V("pL", h, S(k, 256, 16)), V("gh", S(o + k, o + 2048, 16)), r8(2, 2), False, h == 1 and k == 15)
+
+    def hd_mm(h):
+        o = 2048 * h
+        for k in range(16):
+            mm(V("pG", h, S(256 + k, 384, 16)), V("gh", S(o + k, o + 2048, 16)), r8(3), False, False)
+
+    def hg_mm(h):
+        o = 4096 + 2048 * h
+        for k in range(16):
+            mm(V("pG", h, S(k, 384, 16)), V("gh", S(o + k, o + 2048, 16)), r8(5, 3), False, k == 15)
+
+    both = S(0, 2)
+    Lp, Dp = V("pL", both, S(128, 256)), V("pL", both, S(0, 128))
+    L15 = V("pL", both, S(143, 256, 16))
+    S15 = V("ss", S(15, 256, 16))
+    SG, SL = V("sg", S(15, 256, 16)), V("sg", S(271, 512, 16))
+    scr = V("pS", S(0, 256))
+
+    def l_side():
+        tt(scr, Lp, V("urep"), A.mult)
+        tt(V("ia"), V("ck"), scr, A.subtract)
+        ts(V("rr"), V("ia"), 5, A.arith_shift_right, 2047, A.bitwise_and)
+        tt(V("kf", S(0, 256)), Dp, V("rr"), A.min)
+        scan(V("ss"), V("stp"), V("kf", S(0, 256)), 0.0, A.add, A.max)
+        tt(scr, Lp, V("ss"), A.max)
+        ts(sm(3), S15, 1.0, A.add, 4096.0, A.mult)
+        ts(sm(9), S15, -4096.0, A.max, 6144.0, A.add)
+        ts(sm(5), V("pS", S(15, 256, 16)), -1.0, A.mult)
+        tt(V("nw"), scr, V("rr"), A.min)
+        tt(qi(4), sm(5), S15, A.max)
+        tt(sm(3), sm(3), V("zl"), A.min)
+        ts(qi(5), qi(4), 2047, A.bitwise_and)
+        tt(sm(4), sm(5), sm(3), A.max)
+        cp(sm(2), qi(5))
+
+    def newk_mm():
+        for h in range(2):
+            hs = S(128 * h, 128 * h + 128)
+            mm(V("pC", hs), V("nw", hs), V("ident"), True, True)
+
+    def halve(hname, off, out):
+        tt(V(hname), ind(V("tab", S(XO, ZO + K)), V(off)), V("zb"), A.add)
+        ts(out, V(hname), 0.5, A.mult, -1024.0, A.add)
+
+    Ep, Gp, Fp = V("pG", both, S(0, 128)), V("pG", both, S(128, 256)), V("pG", both, S(256, 384))
+
+    def g_square():
+        act(V("sq"), Fp, FN.Square, scale=512.0)
+
+    def g_side():
+        tt(V("cc"), Ep, V("sq"), A.min)
+        tt(V("kf", S(0, 256)), Gp, V("cc"), A.min)
+        tt(V("kf", S(256, 512)), V("kf", S(0, 256)), Fp, A.subtract)
+        scan(V("sg"), V("seg"), V("kf"), 0.0, A.mult, A.max)
+        tt(qi(0), SG, V("zl"), A.max)
+        tt(qi(1), SG, SL, A.max)
+        ts(qi(3), qi(0), 4095, A.bitwise_and)
+        tt(qi(2), SG, SL, A.min)
+        e_op("ez", qi(3))
+        w_mm("ez", "pC", 256)
+        tt(V("nm"), SG, sm(9), A.is_le)
+        ts(qi(4, 2), qi(1, 2), 2047, A.bitwise_and)
+        ts(sm(5), V("nm"), col(7), A.mult)
+        cp(V("lb", S(16, 32)), qi(5))
+        tt(sm(6), qi(4), sm(5), A.max)
+        cp(V("oz"), V("pC", S(256, 272)))
+        u_op("uh", sm(6))
+        tt(V("lb", S(0, 16)), qi(5), V("lb", S(16, 32)), A.subtract)
+        act(V("ul"), ind(V("lb"), V("exl")), FN.Copy)
+
+    def lo_mm():
+        for h in range(2):
+            mm(V("pL", 0, S(128 * h, 128 * h + 128)), V("ul", S(128 * h, 128 * h + 128)), V("idb"), True, True)
+
+    def count_merges():
+        for h in range(2):
+            mm(V("pC", S(384, 512), part=S(0, 8)), V("nm", S(8 * h, 8 * h + 8)), V("ones"), h == 0, h == 1)
+        ps, y1, y2 = V("pC", S(384, 512), part=S(0, 8)), V("fo", part=S(0, 8)), V("tf", S(0, 128), part=S(0, 8))
+        act(y1, ps, FN.Identity, bias=16 - 15 / 32, scale=-1 / 16)
+        act(V("a15", S(0, 128), part=S(0, 8)), ps, FN.Identity, bias=256.0, scale=-1.0)
+        act(y2, y1, FN.Identity, bias=ROUND)
+        act(V("a15", S(128, 256), part=S(0, 8)), y2, FN.Identity, bias=16 * ROUND, scale=-16.0)
+
+    def scatter_b(a, b):
+        for c in range(b - 1, a - 1, -1):
+            cp(ind(V("bt"), V("o2", S(2 * c, 2 * c + 1))), V("nk", S(16 * c, 16 * c + 16)))
+
+    def scatter_fx():
+        for c in range(15, -1, -1):
+            cp(ind(V("tab", S(0, ZO)), V("o1", S(2 * c, 2 * c + 2))), V("v1", c))
+
+    XS, ZP, ZA = SPLIT
+    for v in range(VISITS):
+        last = v == VISITS - 1
+        z = V("z%d" % v)
+        if v > 0:
+            arrive("l%d" % v, "al%d" % v, v)
+            arrive("z%d" % v, "az%d" % v, v)
+        spread_z(v, range(0, ZP), "pool")
+        spread_z(v, range(ZP, ZA), "act")
+        cell_mm(v)
+        cell_act()
+        fw_mm(True)
+        if v > 0:
+            scatter_b(8, 16)
+        cp(V("fw16"), V("pD", S(0, 128)))
+        xf_part(XS, W, "act")
+        if v > 0:
+            scatter_b(0, 8)
+        spread_z(v, range(ZA, 16), "dve")
+        cell_small()
+        if XS:
+            xf_part(0, XS, "dve")
+        e_op("ec", sm(0))
+        for j in range(4):
+            h_mm(j)
+            h_cp(j)
+        w_mm("ec", "pD", 320)
+        open_l(v)
+        if v == 0:
+            cp(V("bt", S(0, W)), V("bi"))
+        g_max(v, 0, 0)
+        cp(V("oc"), V("pD", S(320, 336)))
+        cp(V("bc"), ind(V("bt", S(0, W)), V("oc")))
+        g_h(v, 0, 0)
+        m_mm(0, 0)
+        open_g(v)
+        g_max(v, 0, 1)
+        if v == 0:
+            late_constants()
+        act(V("urep"), ind(sm(1), V("ex")), FN.Identity, bias=32.0, scale=0.5)
+        u_op("uc", sm(0))
+        g_h(v, 0, 1)
+        m_mm(0, 1)
+        hl_mm(0)
+        hd_mm(0)
+        dif_open("pA", 512)
+        dif_mm("ec", "uc", "pA", 0, False)
+        g_max(v, 1, 0)
+        act(V("zb"), z, FN.Identity, bias=2047.5)
+        act(V("tab", S(ZO, ZO + K)), z, FN.Copy)
+        g_h(v, 1, 0)
+        m_mm(1, 0)
+        hl_mm(1)
+        hd_mm(1)
+        g_max(v, 1, 1)
+        g_h(v, 1, 1)
+        m_mm(1, 1)
+        hg_mm(0)
+        l_side()
+        newk_mm()
+        hg_mm(1)
+        u_op("uw", sm(2))
+        e_op("ew", sm(2))
+        e_op("ev", sm(4))
+        g_square()
+        act(V("nk"), V("pC", S(0, 256)), FN.Abs)
+        w_mm("ev", "pD", 352)
+        w_mm("ew", "pD", 336)
+        dif_mm("ew", "uw", "pA", 256, True)
+        dif_open("pB", 256)
+        if last:
+            dma("sync", T.yl[:], V("nk"))
+            contest("pA", 2, V("pD", S(320, 352)), col(9))
+            cp(V("o2", S(0, 32, 2)), V("s2", S(32, 48)))
+            ts(V("o1", S(1, 32, 2)), V("s2", S(48, 64)), float(XO), A.add)
+            scatter_b(0, 16)
+            dma("sync", T.yb[:], V("bt", S(0, W)))
+        g_side()
+        e_op("eh", sm(6))
+        halve("h1", "oz", V("zs%d" % v))
+        if not last:
+            send("zs%d" % v, "z%d" % (v + 1), "az%d" % (v + 1), v + 1)
+            cp(V("ls%d" % v), V("nk"))
+            send("ls%d" % v, "l%d" % (v + 1), "al%d" % (v + 1), v + 1)
+        else:
+            dma("act", T.yz[:], V("zs%d" % v))
+        w_mm("eh", "pD", 368)
+        dif_mm("eh", "uh", "pB", 0, True)
+        lo_mm()
+        act(V("v1", S(0, 16), S(0, 16)), V("pL", 0), FN.Copy)
+        cp(V("ov"), V("pD", S(352, 368)))
+        if not last:
+            count_merges()
+            contest("pA", 2, V("pD", S(320, 352)), col(9))
+            cp(V("o2", S(0, 32, 2)), V("s2", S(32, 48)))
+            ts(V("o1", S(1, 32, 2)), V("s2", S(48, 64)), float(XO), A.add)
+        halve("h2", "ov", V("v1", S(0, 16), S(16, 32)))
+        contest("pB", 1, V("pD", S(368, 384)), col(7))
+        cp(V("o1", S(0, 32, 2)), V("s2", S(32, 48)))
+        scatter_fx()
+    dma("act", T.yx[:], XW)
+    fw_mm(False)
+    cp(V("fo"), V("pD", S(0, 128)))
+    dma("sync", T.yf[:], V("fo"))
+
+    def meet(a, b):
+        return a[0] == b[0] and a[1] < b[2] and b[1] < a[2]
+
+    hist = {}
+    for i, o in enumerate(ops):
+        deps = set()
+        own = o["sem"] is None
+        for reg, wr in [(r, False) for r in o["r"]] + [(r, True) for r in o["w"]]:
+            ps = SCRATCH[reg[0]][0] == "psum"
+            for j, reg2, wr2 in hist.get(reg[0], []):
+                if not meet(reg, reg2):
+                    continue
+                p = ops[j]
+                same = own and p["sem"] is None and p["eng"] == o["eng"]
+                if same:
+                    need = o["eng"] != "pe" and ((wr2 and not wr) or (SAME_QUEUE_WAW and (wr or wr2)))
+                else:
+                    need = wr or wr2 or ps
+                if need and j != i:
+                    deps.add(j)
+        o["deps"] = deps
+        for reg, wr in [(r, False) for r in o["r"]] + [(r, True) for r in o["w"]]:
+            hist.setdefault(reg[0], []).append((i, reg, wr))
+        for j in deps:
+            ops[j]["inc"] = True
+    tally = {}
+    for o in ops:
+        if o["sem"] is None:
+            if o.get("inc"):
+                tally[o["eng"]] = tally.get(o["eng"], 0) + 1
+            o["tick"] = (o["eng"], tally.get(o["eng"], 0))
+        else:
+            o["tick"] = (o["sem"], o["count"])
+    queue = {"pe": g.tensor, "dve": g.vector, "act": g.scalar, "pool": g, "sync": g.sync}
+    known = {e: {} for e in queue}
+    for o in ops:
+        if o["ext"]:
+            o["clock"] = {}
+            continue
+        kn = known[o["eng"]]
+        for j in sorted(o["deps"], reverse=True):
+            p = ops[j]
+            s, n = p["tick"]
+            if s == "" or kn.get(s, 0) >= n:
+                continue
+            queue[o["eng"]].wait_ge(T.sem[s], n)
+            kn[s] = n
+            for s2, n2 in p["clock"].items():
+                if kn.get(s2, 0) < n2:
+                    kn[s2] = n2
+        o["clock"] = dict(kn)
+        ins = o["fn"]()
+        if o["sem"] is None:
+            if o.get("inc"):
+                ins.then_inc(T.sem[o["eng"]], 1)
+        elif o["sem"]:
+            ins.then_inc(T.sem[o["sem"]], 16)
+    for e, n in tally.items():
+        g.wait_ge(T.sem[e], n)
+    for i in range(ndma[0]):
+        g.wait_ge(T.sem["d%d" % i], 16)
+    g.wait_ge(T.sem.sent, nsent[0])

@@ -35,6 +35,9 @@ SEMAPHORES = (["pe", "dve", "act", "pool", "sent"] + ["d%d" % i for i in range(2
               + ["al%d" % i for i in range(1, VISITS)] + ["az%d" % i for i in range(1, VISITS)])
 SAME_QUEUE_WAW = True
 SPLIT = (512, 6, 10)
+LAT, HOLD, AHEAD = 90.0, 0.2, 1000.0
+EARLY = (6000.0, 3000.0)
+MEMO = {}
 A = AluOpType
 FN = ActivationFunctionType
 
@@ -51,38 +54,62 @@ def rank_program(g, core, T, topo):
         shape = SCRATCH[name][1][1:]
         full = list(idx) + [slice(None)] * (len(shape) - len(idx))
         lo = hi = 0
-        stride = 1
+        stride = n = 1
         for d in range(len(shape) - 1, -1, -1):
             r = range(shape[d])[full[d]]
             if isinstance(r, int):
                 lo += r * stride; hi += r * stride
             else:
-                lo += r[0] * stride; hi += r[-1] * stride
+                lo += r[0] * stride; hi += r[-1] * stride; n *= len(r)
             stride *= shape[d]
         if SCRATCH[name][0] == "psum":
             lo, hi = lo // 512 * 512, hi // 512 * 512 + 511
-        return {"ap": T[name][(part,) + tuple(full)], "reg": [(name, lo, hi + 1)], "also": []}
+        return {"ap": T[name][(part,) + tuple(full)], "reg": [(name, lo, hi + 1)], "also": [], "n": n,
+                "rows": len(range(128)[part]), "size": 4 if SCRATCH[name][2] in (F32, I32) else 2}
 
     def S(a, b, s=1):
         return slice(a, b, s)
 
     def ind(win, off):
-        return {"ap": win["ap"].indirect(off["ap"]), "reg": win["reg"], "also": off["reg"]}
+        return dict(win, ap=win["ap"].indirect(off["ap"]), also=off["reg"], n=16 * off["n"])
 
-    def rec(eng, fn, outs, ins, sem=None, count=1, ext=False):
+    def rec(eng, fn, outs, ins, sem=None, count=1, ext=False, two=False, to=None):
         w, r = [], []
         for o in outs:
             w += o["reg"]; r += o["also"]
         for i in ins:
             if isinstance(i, dict):
                 r += i["reg"] + i["also"]
-        ops.append({"eng": eng, "fn": fn, "w": w, "r": r, "sem": sem, "count": count, "ext": ext})
+        sides = [x for x in outs + ins if isinstance(x, dict)]
+        n = max([x["n"] for x in outs] + [0])
+        if ext:
+            cost = 0.0
+        elif sem == "":
+            cost = 4000.0
+        elif sem is not None:
+            cost = 2000.0 + sides[0]["n"] * sides[0]["rows"] * sides[0]["size"] / 200.0
+        elif eng == "pe":
+            cost = max(64, ins[1]["n"]) * (4 if ins[1]["size"] == 4 else 1) * 0.5
+        elif eng == "pool":
+            cost = 170.0 + 2 * n
+        elif outs[0]["also"]:
+            cost = 50.0 + 3.8 * n
+        elif any(x["also"] for x in sides):
+            cost = 55.0 + 1.55 * n
+        else:
+            full = [x for x in ins if isinstance(x, dict) and x["n"] == n]
+            if eng == "dve" and all(x["size"] == 2 for x in outs + full):
+                n = n / 2
+            if two and SCRATCH[full[0]["reg"][0][0]][0] == SCRATCH[full[1]["reg"][0][0]][0]:
+                n = 2 * n
+            cost = 55.0 + max(64, n)
+        ops.append({"eng": eng, "fn": fn, "w": w, "r": r, "sem": sem, "count": count, "ext": ext, "cost": cost, "to": to})
 
     def ap(x):
         return x["ap"] if isinstance(x, dict) else x
 
     def tt(o, a, b, op):
-        rec("dve", lambda: g.vector.tensor_tensor(ap(o), ap(a), ap(b), op), [o], [a, b])
+        rec("dve", lambda: g.vector.tensor_tensor(ap(o), ap(a), ap(b), op), [o], [a, b], two=True)
 
     def ts(o, a, s1, op0, s2=None, op1=None):
         if op1 is None:
@@ -133,7 +160,7 @@ def rank_program(g, core, T, topo):
         rid, pid, _ = topo.addr(dst)
         mask, n = lanes_mask(core, dst)
         nsent[0] += n
-        rec("pool", lambda: g.remote_dma(T[land][:], T[src][:], T.sem[sem], T.sem.sent, pid, rid, mask), [], [V(src)], sem="")
+        rec("pool", lambda: g.remote_dma(T[land][:], T[src][:], T.sem[sem], T.sem.sent, pid, rid, mask), [], [V(src)], sem="", to=sem)
 
     def arrive(land, sem, v):
         s = 1 + (v - 1) % (n_ranks - 1)
@@ -150,7 +177,6 @@ def rank_program(g, core, T, topo):
     dma("act", V("li"), T.la[:])
     dma("act", V("ti", S(0, 1)), T.th[:])
     ms(V("tab", S(0, W)), 0.0)
-    dma("act", V("bi"), T.bk[:])
 
     iota(V("ia", S(0, 1)), [[0, 1]], 0, 1)
     ms(V("ident"), 1.0)
@@ -164,6 +190,7 @@ def rank_program(g, core, T, topo):
     cp(V("fl", S(128, 256)), V("qi"))
     dma("sync", V("tab", S(0, W), part=S(8, 128, 16)), V("fl", S(0, 128)))
     dma("sync", V("tab", S(0, W), part=S(9, 128, 16)), V("fl", S(128, 256)))
+    dma("sync", V("bi"), T.bk[:])
     ts(V("ib", S(0, 1)), V("ia", S(0, 1)), 15, A.bitwise_and)
     cp(col(0), V("ib", S(0, 1)))
     ts(col(1), col(0), 8.0, A.is_lt)
@@ -251,6 +278,7 @@ def rank_program(g, core, T, topo):
                 cp(o, a)
             else:
                 asel(o, a, [[0, K]], A.is_ge, 0.0, 0, 0)
+            ops[-1]["chain"] = "z" + eng
 
     def fw_mm(wrapped):
         for p in range(16):
@@ -336,10 +364,12 @@ def rank_program(g, core, T, topo):
         o = 4096 * side + 2048 * h
         tt(V("gm", S(o, o + 2048)), ind(V("xf"), offs(v, side, h)),
            dict(V("zrep", S(2048 * h, 2048 * h + 2048)), reg=[("zrep", 0, 16)]), A.max)
+        ops[-1]["chain"] = "gm"
 
     def g_h(v, side, h):
         o = 4096 * side + 2048 * h
         act(V("gh", S(o, o + 2048)), ind(V("hh"), offs(v, side, h)), FN.Copy)
+        ops[-1]["chain"] = "gh"
 
     def m_mm(side, h):
         o = 4096 * side + 2048 * h
@@ -467,13 +497,16 @@ def rank_program(g, core, T, topo):
         for j in range(4):
             h_mm(j)
             h_cp(j)
+            ops[-1]["chain"] = "gh"
         w_mm("ec", "pD", 320)
         open_l(v)
         if v == 0:
-            cp(V("bt", S(0, W)), V("bi"))
+            for j in range(4):
+                cp(V("bt", S(512 * j, 512 * j + 512)), V("bi", S(512 * j, 512 * j + 512)))
         g_max(v, 0, 0)
         cp(V("oc"), V("pD", S(320, 336)))
         cp(V("bc"), ind(V("bt", S(0, W)), V("oc")))
+        ops[-1]["early"] = EARLY[0] if v else 0.0
         g_h(v, 0, 0)
         m_mm(0, 0)
         open_g(v)
@@ -523,6 +556,7 @@ def rank_program(g, core, T, topo):
         halve("h1", "oz", V("zs%d" % v))
         if not last:
             send("zs%d" % v, "z%d" % (v + 1), "az%d" % (v + 1), v + 1)
+            ops[-1]["early"] = EARLY[1] + (0.0 if v else 3000.0)
             cp(V("ls%d" % v), V("nk"))
             send("ls%d" % v, "l%d" % (v + 1), "al%d" % (v + 1), v + 1)
         else:
@@ -548,6 +582,93 @@ def rank_program(g, core, T, topo):
 
     def meet(a, b):
         return a[0] == b[0] and a[1] < b[2] and b[1] < a[2]
+
+    def arrange(ops):
+        n = len(ops)
+        pre = [dict() for _ in range(n)]
+        seen, lastq, sends = {}, {}, {}
+        for i, o in enumerate(ops):
+            for reg, wr in [(r, False) for r in o["r"]] + [(r, True) for r in o["w"]]:
+                ps = SCRATCH[reg[0]][0] == "psum"
+                for j, reg2, wr2 in seen.get(reg[0], []):
+                    if j != i and meet(reg, reg2):
+                        same = ops[j]["eng"] == o["eng"]
+                        if same and o["eng"] == "pe":
+                            pre[i][j] = 0.0
+                        elif wr or wr2 or (ps and not same):
+                            pre[i][j] = LAT
+            for reg, wr in [(r, False) for r in o["r"]] + [(r, True) for r in o["w"]]:
+                old = seen.get(reg[0], [])
+                if wr:
+                    old = [e for e in old if not (reg[1] <= e[1][1] and e[1][2] <= reg[2])]
+                seen[reg[0]] = old + [(i, reg, wr)]
+            if o.get("chain"):
+                if o["chain"] in lastq:
+                    pre[i].setdefault(lastq[o["chain"]], 0.0)
+                lastq[o["chain"]] = i
+            if o["ext"]:
+                pre[i][sends[o["sem"]]] = 0.0
+            elif o["sem"] is not None:
+                if o["eng"] in lastq:
+                    pre[i].setdefault(lastq[o["eng"]], None)
+                lastq[o["eng"]] = i
+                if o["sem"] == "":
+                    sends[o["to"]] = i
+        suc = [[] for _ in range(n)]
+        for i in range(n):
+            for j in pre[i]:
+                suc[j].append(i)
+        rest = [0.0] * n
+        for i in range(n - 1, -1, -1):
+            rest[i] = ops[i]["cost"] + ops[i].get("early", 0.0) + max([0.0] + [rest[k] + (pre[k][i] or 0.0) - (ops[i]["cost"] if pre[k][i] is None else 0.0) for k in suc[i]])
+        left = [len(p) for p in pre]
+        ready_at = [0.0] * n
+        ready = {}
+        for i in range(n):
+            if not left[i]:
+                ready.setdefault(ops[i]["eng"], []).append(i)
+        free, wires, order = {}, [0.0], []
+        while len(order) < n:
+            best = None
+            for e, lst in ready.items():
+                if lst:
+                    t = max(free.get(e, 0.0), min(ready_at[i] for i in lst))
+                    if best is None or t < best[0]:
+                        best = (t, e)
+            t, e = best
+            wait = None
+            for now in sorted((i for i in ready[e] if ready_at[i] <= t), key=lambda i: (-rest[i], i)):
+                soon = [i for i in ready[e] if t < ready_at[i] < t + min(HOLD * ops[now]["cost"], 600.0)
+                        and rest[i] > rest[now] + AHEAD and e != "ext"]
+                if not soon:
+                    break
+                wait = wait or soon
+            else:
+                now = max(wait, key=lambda i: rest[i])
+                t = ready_at[now]
+            ready[e].remove(now)
+            order.append(now)
+            o = ops[now]
+            if o["sem"] is None or o["ext"]:
+                end = t + o["cost"]
+                free[e] = end if not o["ext"] else 0.0
+            else:
+                free[e] = t + 100.0
+                if o["sem"]:
+                    wires[0] = max(wires[0], t + 1000.0) + o["cost"] - 2000.0
+                    end = wires[0] + 1000.0
+                else:
+                    end = t + o["cost"]
+            for k in suc[now]:
+                ready_at[k] = max(ready_at[k], t if pre[k][now] is None else end + pre[k][now])
+                left[k] -= 1
+                if not left[k]:
+                    ready.setdefault(ops[k]["eng"], []).append(k)
+        return order
+
+    if "order" not in MEMO:
+        MEMO["order"] = arrange(ops)
+    ops = [ops[i] for i in MEMO["order"]]
 
     hist = {}
     for i, o in enumerate(ops):

@@ -4,7 +4,7 @@ from concourse.mybir import dt, AluOpType, AxisListType, ActivationFunctionType
 W, K, VISITS = 2048, 256, 4
 BIG = float(2 ** 17)
 ROUND = 1.5 * 2 ** 23
-XO, DO, ZO = W, 2 * W, 2 * W + 32
+XO, ZO = W + 48, 2 * W + 80
 F32, BF16, I32, U16, F16 = "float32", "bfloat16", "int32", "uint16", "float16"
 
 SCRATCH = {
@@ -19,24 +19,28 @@ def _sb(dtype, **kw):
         SCRATCH[n] = ("sbuf", [128] + (list(s) if isinstance(s, tuple) else [s]), dtype)
 
 
-_sb(BF16, tab=ZO + K, xf=W, hh=W, gm=8192, gh=8192, zrep=4096, v1=(16, 32), fl=256,
+_sb(BF16, tab=ZO + K, xf=W, hh=W, gm=8192, gh=8192, zrep=4096, vf=256, vx=256, mbf=392, fl=256,
     z0=K, z1=K, z2=K, z3=K, zs0=K, zs1=K, zs2=K, zs3=K,
     ones=128, idb=128, rz=256, r8=96, selz=144, pair=128, fi=128, mb=512, ol1=512, ol2=512, og1=384, og2=128,
     nm=16, a15=256, blkn=128, cu=32, lb=32)
 _sb(F32, bt=W + 32, ident=128, blk=128, maske=256, ri=128, re_=128, rw=8, seg=512, rst=512, stp=256, ck=256, zl=16,
     cols=16, tf=256, urep=256, kf=512, ss=256, sg=512, nw=256, nk=256, sq=256, cc=256, zb=256,
-    uw=256, uh=256, uc=256, ew=256, eh=256, ec=256, ez=256, ev=256, sm=160, pr=512, s2=128, fo=128)
+    uw=256, uh=256, uc=256, ew=256, eh=256, ec=256, ez=256, ev=256, sm=160, pr=512, s2=128, s3=32, fo=128,
+    ri2=68, re2=68, rsf=392, prf=392, s4=16)
 _sb(I32, bi=W, fi2=128, li=K, ti=8, ia=256, ib=256, rr=256, qi=128, ai=128)
-_sb(U16, l0=K, l1=K, l2=K, l3=K, ls0=K, ls1=K, ls2=K, fw16=128, bc=K, ex=16, exl=16, o1=32, o2=32, oc=16, oz=16, ov=16)
+_sb(U16, l0=K, l1=K, l2=K, l3=K, ls0=K, ls1=K, ls2=K, fw16=128, bc=K, ex=16, exl=16, o1=16, o2=32, o3=32, oc=16, oz=16, ov=16)
 _sb(BF16, ul=256)
 _sb(F16, h1=256, h2=256)
 
 SEMAPHORES = (["pe", "dve", "act", "pool", "sent"] + ["d%d" % i for i in range(24)]
               + ["al%d" % i for i in range(1, VISITS)] + ["az%d" % i for i in range(1, VISITS)])
 SAME_QUEUE_WAW = True
-SPLIT = (512, 6, 10)
-LAT, HOLD, AHEAD = 90.0, 0.2, 1000.0
-EARLY = (6000.0, 3000.0)
+SPLIT = (768, 6, 10)
+LAT, HOLD, AHEAD = 200.0, 0.3, 1000.0
+EARLY = (6000.0, 3000.0, 4000.0, 3000.0, 0.0, 0.0)
+PIECES = (1, 1, 1, 1)
+HDVE, XP = (), 2048
+RATE = (0.85, 40.0, 1.15, 2.6, 1024)
 MEMO = {}
 A = AluOpType
 FN = ActivationFunctionType
@@ -89,20 +93,20 @@ def rank_program(g, core, T, topo):
         elif sem is not None:
             cost = 2000.0 + sides[0]["n"] * sides[0]["rows"] * sides[0]["size"] / 200.0
         elif eng == "pe":
-            cost = max(64, ins[1]["n"]) * (4 if ins[1]["size"] == 4 else 1) * 0.5
+            cost = max(64, ins[1]["n"]) * (4 if ins[1]["size"] == 4 else 1) * RATE[0] / 2
         elif eng == "pool":
-            cost = 170.0 + 2 * n
+            cost = 170.0 + 2 * n * RATE[0]
         elif outs[0]["also"]:
-            cost = 50.0 + 3.8 * n
+            cost = 50.0 + RATE[3] * n
         elif any(x["also"] for x in sides):
-            cost = 55.0 + 1.55 * n
+            cost = 55.0 + RATE[2] * n
         else:
             full = [x for x in ins if isinstance(x, dict) and x["n"] == n]
             if eng == "dve" and all(x["size"] == 2 for x in outs + full):
                 n = n / 2
             if two and SCRATCH[full[0]["reg"][0][0]][0] == SCRATCH[full[1]["reg"][0][0]][0]:
                 n = 2 * n
-            cost = 55.0 + max(64, n)
+            cost = RATE[1] + max(64, n) * RATE[0]
         ops.append({"eng": eng, "fn": fn, "w": w, "r": r, "sem": sem, "count": count, "ext": ext, "cost": cost, "to": to})
 
     def ap(x):
@@ -184,12 +188,11 @@ def rank_program(g, core, T, topo):
     asel(V("blk"), V("ident"), [[-16, 8], [0, 16]], A.is_ge, 0.0, 0, 1)
     asel(V("blk"), V("blk"), [[16, 8], [0, 16]], A.is_ge, 0.0, 15, -1)
     asel(V("ident"), V("ident"), [[-1, 128]], A.is_equal, 0.0, 0, 1)
-    ts(V("ai"), V("fi2"), 255, A.bitwise_and)
-    ts(V("qi"), V("fi2"), 1792, A.bitwise_and)
-    cp(V("fl", S(0, 128)), V("ai"))
-    cp(V("fl", S(128, 256)), V("qi"))
+    cp(V("fl", S(128, 256)), V("fi2"))
+    tt(V("fl", S(0, 128)), V("fi2"), V("fl", S(128, 256)), A.subtract)
     dma("sync", V("tab", S(0, W), part=S(8, 128, 16)), V("fl", S(0, 128)))
-    dma("sync", V("tab", S(0, W), part=S(9, 128, 16)), V("fl", S(128, 256)))
+    dma("act", V("tab", S(0, W), part=S(9, 128, 16)), V("fl", S(128, 256)))
+    ops[-1]["apart"] = ops[-2]["apart"] = True
     dma("sync", V("bi"), T.bk[:])
     ts(V("ib", S(0, 1)), V("ia", S(0, 1)), 15, A.bitwise_and)
     cp(col(0), V("ib", S(0, 1)))
@@ -205,34 +208,41 @@ def rank_program(g, core, T, topo):
     iota(V("ia", S(16, 32)), [[1, 16]], 0, 0)
     iota(V("zl"), [[128, 2], [0, 8]], ZO - XO, 1)
     iota(V("kf", S(0, 256)), [[0, 16], [1, 16]], 0, 0)
-    ts(V("fi"), V("ident"), col(2), A.mult)
-    ts(col(4), col(1), -256.0, A.mult)
-    ts(col(5), col(0), 14.0, A.mult, 39.0, A.add)
-    ts(col(6), col(0), 20.0, A.mult, 10.0, A.add)
-    ts(col(7), col(0), float(DO), A.add)
-    ts(col(8), col(0), float(DO + 16), A.add)
-    ts(col(9), col(0), float(W + 16), A.add)
+    def lin(o, a, scale, bias=0.0):
+        act(o, a, FN.Identity, bias=bias, scale=scale)
+
+    def fill(o, c):
+        iota(o, [[0, o["n"]]], c, 0)
+
+    lin(V("fi"), V("ident"), col(2))
+    lin(col(4), col(1), -256.0)
+    lin(col(5), col(0), 14.0, 39.0)
+    lin(col(6), col(0), 20.0, 10.0)
+    ts(V("ib", S(1, 2)), V("ia", S(0, 1)), 31, A.bitwise_and)
+    ts(col(7), V("ib", S(1, 2)), float(W + 16), A.add)
+    lin(col(9), col(0), 1.0, float(W + 16))
+    lin(col(15), col(0), 1.0, float(W + 32))
+    lin(col(8), col(2), -1.0)
     ts(col(10), col(0), 9.0, A.is_equal, 16.0, A.mult)
-    ts(col(11), col(0), -4096.0, A.mult, 65536.0, A.add)
+    lin(col(11), col(0), -4096.0, 65536.0)
     r8 = lambda i, n=1: V("r8", S(8 * i, 8 * (i + n)))
-    ts(r8(0), blk8, 2 * BIG, A.mult)
-    ts(r8(1), blk8, -2 * BIG, A.mult)
-    ts(r8(2), blk8, col(1), A.mult, -BIG, A.mult)
-    ts(r8(3), blk8, col(2), A.mult, -1.0, A.mult)
+    lin(V("rz", S(0, 128)), V("blk"), -BIG)
+    lin(V("rz", S(128, 256)), V("blk"), BIG)
+    lin(r8(0), blk8, 2 * BIG)
+    lin(r8(1), blk8, -2 * BIG)
+    lin(r8(2), V("rz", S(0, 128, 16)), col(1))
+    lin(r8(3), blk8, col(8))
     cp(V("idb"), V("ident"))
-    ts(r8(5), blk8, col(1), A.mult, BIG, A.mult)
-    ts(r8(6), blk8, col(2), A.mult)
-    ts(r8(7), blk8, col(2), A.mult)
+    lin(r8(5), V("rz", S(128, 256, 16)), col(1))
+    lin(r8(6), blk8, col(2))
+    lin(r8(7), blk8, col(2))
     ts(r8(8), blk8, col(5), A.mult)
     ts(r8(9), blk8, col(6), A.mult)
     cp(V("l0"), V("li"))
     cp(V("ex"), V("ia", S(16, 32)))
     ts(V("exl"), V("ia", S(16, 32)), col(10), A.add)
-    ts(V("rz", S(0, 128)), V("blk"), -BIG, A.mult)
-    ts(V("rz", S(128, 256)), V("blk"), BIG, A.mult)
-    ms(V("cu", S(0, 16)), 255.0)
-    ms(V("cu", S(16, 32)), 510.0)
-    cp(V("rw"), blk8)
+    iota(V("cu"), [[255, 2], [0, 16]], 255, 0)
+    lin(V("rw"), blk8, 1.0)
     ts(V("maske"), V("kf", S(0, 256)), col(0), A.is_equal)
     ts(V("ti", S(1, 2)), V("ti", S(0, 1)), 2048.0, A.add)
     ts(V("ti", S(2, 3)), V("ti", S(1, 2)), 127, A.bitwise_and)
@@ -254,19 +264,29 @@ def rank_program(g, core, T, topo):
         act(V("ri"), V("ident"), FN.Identity, scale=1.0 / 64)
         act(V("re_"), V("blk"), FN.Identity, scale=-1.0 / 64)
         act(V("ck"), kk, FN.Identity, scale=613.0 * 32)
-        ms(V("ri", S(15, 128, 16)), 0.0)
-        ms(V("re_", S(15, 128, 16)), 0.0)
+        fill(V("ri", S(15, 128, 16)), 0)
+        fill(V("re_", S(15, 128, 16)), 0)
         ts(V("mb", S(0, 256)), kk, col(0), A.is_ge, 128.0, A.mult)
-        ms(V("stp"), 4096.0)
-        ms(V("seg"), 1.0)
-        ms(V("rst"), 0.0)
-        ms(V("mb", S(15, 256, 16)), 0.0)
-        ms(V("stp", S(0, 256, 16)), -1e9)
-        ms(V("seg", S(0, 512, 16)), 0.0)
-        ms(V("rst", S(15, 512, 16)), 1.0)
+        fill(V("ri2"), 0)
+        fill(V("re2"), 0)
+        for j in range(4):
+            lin(V("ri2", S(17 * j, 17 * j + 16)), V("ident", S(32 * j, 32 * j + 16)), 1.0 / 64)
+            lin(V("re2", S(17 * j, 17 * j + 16)), V("blk", S(32 * j + 16, 32 * j + 32)), -1.0 / 64)
+        fill(V("rsf"), 0)
+        fill(V("rsf", S(15, 256, 16)), 1)
+        fill(V("rsf", S(272, 392, 17)), 1)
+        fill(V("mbf", S(256, 392)), 0)
+        fill(V("stp"), 4096)
+        fill(V("seg"), 1)
+        fill(V("rst"), 0)
+        fill(V("mb", S(15, 256, 16)), 0)
+        fill(V("stp", S(0, 256, 16)), -16000000)
+        fill(V("seg", S(0, 512, 16)), 0)
+        fill(V("rst", S(15, 512, 16)), 1)
         act(V("mb", S(256, 512)), V("mb", S(0, 256)), FN.Copy)
+        act(V("mbf", S(0, 256)), V("mb", S(0, 256)), FN.Copy)
         asel(V("blkn"), V("ones"), [[-1, 8], [0, 16]], A.is_equal, 0.0, 0, 1)
-        ts(V("blkn"), V("blkn"), -BIG, A.mult)
+        lin(V("blkn"), V("blkn"), -BIG)
 
     def spread_z(v, levels, eng):
         a = V("z%d" % v)
@@ -289,18 +309,26 @@ def rank_program(g, core, T, topo):
     XW = V("tab", S(XO, XO + W))
 
     def xf_part(a, b, eng):
-        src = ind(XW, V("fw16", S(a // 16, b // 16)))
-        if eng == "dve":
-            cp(V("xf", S(a, b)), src)
-        else:
-            act(V("xf", S(a, b)), src, FN.Copy)
+        cuts = [a] + [c for c in range(XP, W, XP) if a < c < b] + [b]
+        for a, b in zip(cuts, cuts[1:]):
+            src = ind(XW, V("fw16", S(a // 16, b // 16)))
+            if eng == "dve":
+                cp(V("xf", S(a, b)), src)
+            else:
+                act(V("xf", S(a, b)), src, FN.Copy)
 
     def h_mm(j):
         mm(hbank[j], V("fi"), V("tab", S(512 * j, 512 * j + 512)), True, False)
         mm(hbank[j], V("pair"), V("xf", S(512 * j, 512 * j + 512)), False, True)
 
     def h_cp(j):
-        act(V("hh", S(512 * j, 512 * j + 512)), hbank[j], FN.Identity, bias=col(4))
+        if j in HDVE:
+            ts(V("hh", S(512 * j, 512 * j + 512)), hbank[j], col(4), A.add)
+            ops[-1]["chain"] = "gm"
+            ops[-1]["early"] = EARLY[5]
+        else:
+            act(V("hh", S(512 * j, 512 * j + 512)), hbank[j], FN.Identity, bias=col(4))
+            ops[-1]["chain"] = "gh"
 
     def cell_mm(v):
         mm(V("pC", S(288, 320)), V("idb"), V("cu"), True, False)
@@ -361,10 +389,12 @@ def rank_program(g, core, T, topo):
         return V("l%d" % v if side == 0 else "bc", S(128 * h, 128 * h + 128))
 
     def g_max(v, side, h):
-        o = 4096 * side + 2048 * h
-        tt(V("gm", S(o, o + 2048)), ind(V("xf"), offs(v, side, h)),
-           dict(V("zrep", S(2048 * h, 2048 * h + 2048)), reg=[("zrep", 0, 16)]), A.max)
-        ops[-1]["chain"] = "gm"
+        n = PIECES[2 * side + h]
+        for j in range(n):
+            a, b = 128 * h + 128 * j // n, 128 * h + 128 * (j + 1) // n
+            tt(V("gm", S(4096 * side + 16 * a, 4096 * side + 16 * b)), ind(V("xf"), V("bc" if side else "l%d" % v, S(a, b))),
+               dict(V("zrep", S(16 * a, 16 * b)), reg=[("zrep", 0, 16)]), A.max)
+            ops[-1]["chain"] = "gm"
 
     def g_h(v, side, h):
         o = 4096 * side + 2048 * h
@@ -405,6 +435,7 @@ def rank_program(g, core, T, topo):
         tt(V("kf", S(0, 256)), Dp, V("rr"), A.min)
         scan(V("ss"), V("stp"), V("kf", S(0, 256)), 0.0, A.add, A.max)
         tt(scr, Lp, V("ss"), A.max)
+        ops[-1]["early"] = EARLY[2]
         ts(sm(3), S15, 1.0, A.add, 4096.0, A.mult)
         ts(sm(9), S15, -4096.0, A.max, 6144.0, A.add)
         ts(sm(5), V("pS", S(15, 256, 16)), -1.0, A.mult)
@@ -467,13 +498,34 @@ def rank_program(g, core, T, topo):
         for c in range(b - 1, a - 1, -1):
             cp(ind(V("bt"), V("o2", S(2 * c, 2 * c + 1))), V("nk", S(16 * c, 16 * c + 16)))
 
-    def scatter_fx():
+    def scatter_x():
         for c in range(15, -1, -1):
-            cp(ind(V("tab", S(0, ZO)), V("o1", S(2 * c, 2 * c + 2))), V("v1", c))
+            cp(ind(V("tab", S(XO, ZO)), V("o3", S(2 * c, 2 * c + 1))), V("vx", S(16 * c, 16 * c + 16)))
+
+    def scatter_f():
+        for r in range(7, -1, -1):
+            cp(ind(V("tab", S(0, XO)), V("o1", S(2 * r, 2 * r + 2))), V("vf", S(32 * r, 32 * r + 32)))
+
+    def contest_f():
+        scan(V("prf"), V("pB", S(0, 392)), V("rsf"), 1.0, A.mult, A.add)
+        ts(dict(V("s4", S(0, 16, 2)), reg=[("s4", 0, 1)]), V("prf", S(14, 256, 32)), 0.0, A.is_equal, col(9), A.mult)
+        ts(dict(V("s4", S(1, 16, 2)), reg=[("s4", 1, 2)]), V("prf", S(30, 256, 32)), 0.0, A.is_equal, col(15), A.mult)
+        ts(V("s3", S(16, 24)), V("prf", S(271, 392, 17)), 0.0, A.is_equal, col(15), A.mult)
+        tt(V("s3", S(0, 16)), V("pD", S(368, 384)), V("s4"), A.max)
+        tt(V("s3", S(1, 16, 2)), V("s3", S(1, 16, 2)), V("s3", S(16, 24)), A.max)
+        cp(V("o1", S(0, 16)), V("s3", S(0, 16)))
+
+    def dif_f():
+        for name, rhs, far in (("eh", "re_", "re2"), ("uh", "ri", "ri2")):
+            for h in range(2):
+                hs = S(128 * h, 128 * h + 128)
+                mm(V("pB", hs), V(name, hs), V(rhs), False, False)
+                mm(V("pB", S(256 + 68 * h, 324 + 68 * h)), V(name, hs), V(far), False, name == "uh" and h == 1)
 
     XS, ZP, ZA = SPLIT
     for v in range(VISITS):
         last = v == VISITS - 1
+        XS = SPLIT[0] if v else RATE[4]
         z = V("z%d" % v)
         if v > 0:
             arrive("l%d" % v, "al%d" % v, v)
@@ -497,7 +549,6 @@ def rank_program(g, core, T, topo):
         for j in range(4):
             h_mm(j)
             h_cp(j)
-            ops[-1]["chain"] = "gh"
         w_mm("ec", "pD", 320)
         open_l(v)
         if v == 0:
@@ -543,14 +594,15 @@ def rank_program(g, core, T, topo):
         w_mm("ev", "pD", 352)
         w_mm("ew", "pD", 336)
         dif_mm("ew", "uw", "pA", 256, True)
-        dif_open("pB", 256)
+        mm(V("pB", S(0, 392)), V("idb"), V("mbf"), True, False)
         if last:
             dma("sync", T.yl[:], V("nk"))
             contest("pA", 2, V("pD", S(320, 352)), col(9))
             cp(V("o2", S(0, 32, 2)), V("s2", S(32, 48)))
-            ts(V("o1", S(1, 32, 2)), V("s2", S(48, 64)), float(XO), A.add)
+            cp(V("o3", S(0, 32, 2)), V("s2", S(48, 64)))
             scatter_b(0, 16)
             dma("sync", T.yb[:], V("bt", S(0, W)))
+            ops[-1]["early"] = EARLY[3]
         g_side()
         e_op("eh", sm(6))
         halve("h1", "oz", V("zs%d" % v))
@@ -562,19 +614,21 @@ def rank_program(g, core, T, topo):
         else:
             dma("act", T.yz[:], V("zs%d" % v))
         w_mm("eh", "pD", 368)
-        dif_mm("eh", "uh", "pB", 0, True)
+        dif_f()
         lo_mm()
-        act(V("v1", S(0, 16), S(0, 16)), V("pL", 0), FN.Copy)
+        act(V("vf"), V("pL", 0), FN.Copy)
         cp(V("ov"), V("pD", S(352, 368)))
         if not last:
             count_merges()
             contest("pA", 2, V("pD", S(320, 352)), col(9))
             cp(V("o2", S(0, 32, 2)), V("s2", S(32, 48)))
-            ts(V("o1", S(1, 32, 2)), V("s2", S(48, 64)), float(XO), A.add)
-        halve("h2", "ov", V("v1", S(0, 16), S(16, 32)))
-        contest("pB", 1, V("pD", S(368, 384)), col(7))
-        cp(V("o1", S(0, 32, 2)), V("s2", S(32, 48)))
-        scatter_fx()
+            cp(V("o3", S(0, 32, 2)), V("s2", S(48, 64)))
+            ops[-1]["early"] = EARLY[4]
+        halve("h2", "ov", V("vx"))
+        ops[-1]["early"] = EARLY[4]
+        scatter_x()
+        contest_f()
+        scatter_f()
     dma("act", T.yx[:], XW)
     fw_mm(False)
     cp(V("fo"), V("pD", S(0, 128)))
@@ -591,7 +645,7 @@ def rank_program(g, core, T, topo):
             for reg, wr in [(r, False) for r in o["r"]] + [(r, True) for r in o["w"]]:
                 ps = SCRATCH[reg[0]][0] == "psum"
                 for j, reg2, wr2 in seen.get(reg[0], []):
-                    if j != i and meet(reg, reg2):
+                    if j != i and meet(reg, reg2) and not (o.get("apart") and ops[j].get("apart")):
                         same = ops[j]["eng"] == o["eng"]
                         if same and o["eng"] == "pe":
                             pre[i][j] = 0.0
@@ -599,7 +653,7 @@ def rank_program(g, core, T, topo):
                             pre[i][j] = LAT
             for reg, wr in [(r, False) for r in o["r"]] + [(r, True) for r in o["w"]]:
                 old = seen.get(reg[0], [])
-                if wr:
+                if wr and not o.get("apart"):
                     old = [e for e in old if not (reg[1] <= e[1][1] and e[1][2] <= reg[2])]
                 seen[reg[0]] = old + [(i, reg, wr)]
             if o.get("chain"):
@@ -677,7 +731,7 @@ def rank_program(g, core, T, topo):
         for reg, wr in [(r, False) for r in o["r"]] + [(r, True) for r in o["w"]]:
             ps = SCRATCH[reg[0]][0] == "psum"
             for j, reg2, wr2 in hist.get(reg[0], []):
-                if not meet(reg, reg2):
+                if not meet(reg, reg2) or (o.get("apart") and ops[j].get("apart")):
                     continue
                 p = ops[j]
                 same = own and p["sem"] is None and p["eng"] == o["eng"]

@@ -21,25 +21,26 @@ def _sb(dtype, **kw):
 
 _sb(BF16, tab=ZO + K, xf=W, hh=W, gm=8192, gh=8192, zrep=4096, vf=256, vx=256, mbf=392, fl=256,
     z0=K, z1=K, z2=K, z3=K, zs0=K, zs1=K, zs2=K, zs3=K,
-    ones=128, idb=128, rz=256, r8=96, selz=144, pair=128, fi=128, mb=512, ol1=512, ol2=512, og1=384, og2=128,
+    ones=128, idb=128, rz=256, r8=104, idn=128, pen=512, selz=144, pair=128, fi=128, mb=512, ol1=512, ol2=512, og1=256, ok=512, og2=128,
     nm=16, a15=256, blkn=128, cu=32, lb=32)
-_sb(F32, bt=W + 32, ident=128, blk=128, maske=256, ri=128, re_=128, rw=8, seg=512, rst=512, stp=256, ck=256, zl=16,
-    cols=16, tf=256, urep=256, kf=512, ss=256, sg=512, nw=256, nk=256, sq=256, cc=256, zb=256,
+_sb(F32, bf=W, ident=128, blk=128, maske=256, ri=128, re_=128, rw=8, seg=256, rst=512, stp=256, ck=256, zl=16,
+    cols=16, tf=256, urep=256, kf=256, ss=256, sg=(2, 256), nw=256, nk=256, sq=256, zb=256,
     uw=256, uh=256, uc=256, ew=256, eh=256, ec=256, ez=256, ev=256, sm=160, pr=512, s2=128, s3=32, fo=128,
     ri2=68, re2=68, rsf=392, prf=392, s4=16)
-_sb(I32, bi=W, fi2=128, li=K, ti=8, ia=256, ib=256, rr=256, qi=128, ai=128)
-_sb(U16, l0=K, l1=K, l2=K, l3=K, ls0=K, ls1=K, ls2=K, fw16=128, bc=K, ex=16, exl=16, o1=16, o2=32, o3=32, oc=16, oz=16, ov=16)
+_sb(I32, bt=W + 32, fi2=128, li=K, ti=8, ia=256, ib=256, rr=256, qi=128, ai=128)
+_sb(U16, l0=K, l1=K, l2=K, l3=K, ls0=K, ls1=K, ls2=K, fw16=128, bc=K, ex=16, exl=16, o1=16, o2=64, oc=16, oz=16, ov=16)
 _sb(BF16, ul=256)
 _sb(F16, h1=256, h2=256)
 
 SEMAPHORES = (["pe", "dve", "act", "pool", "sent"] + ["d%d" % i for i in range(24)]
               + ["al%d" % i for i in range(1, VISITS)] + ["az%d" % i for i in range(1, VISITS)])
 SAME_QUEUE_WAW = True
-SPLIT = (768, 6, 10)
+SPLIT = (1024, 7, 14)
 LAT, HOLD, AHEAD = 200.0, 0.3, 1000.0
-EARLY = (6000.0, 3000.0, 4000.0, 3000.0, 0.0, 0.0)
-PIECES = (1, 1, 1, 1)
-HDVE, XP = (), 2048
+EARLY = (6000.0, 3000.0, 3000.0, 2000.0, 2000.0, 3000.0, 6000.0)
+PIECES = (1, 1, 1, 4)
+HDVE, XP = (), 512
+WEAVE = True
 RATE = (0.85, 40.0, 1.15, 2.6, 1024)
 MEMO = {}
 A = AluOpType
@@ -193,7 +194,7 @@ def rank_program(g, core, T, topo):
     dma("sync", V("tab", S(0, W), part=S(8, 128, 16)), V("fl", S(0, 128)))
     dma("act", V("tab", S(0, W), part=S(9, 128, 16)), V("fl", S(128, 256)))
     ops[-1]["apart"] = ops[-2]["apart"] = True
-    dma("sync", V("bi"), T.bk[:])
+    dma("sync", V("bt", S(0, W)), T.bk[:])
     ts(V("ib", S(0, 1)), V("ia", S(0, 1)), 15, A.bitwise_and)
     cp(col(0), V("ib", S(0, 1)))
     ts(col(1), col(0), 8.0, A.is_lt)
@@ -256,7 +257,9 @@ def rank_program(g, core, T, topo):
         ts(V("ol1", S(256 * h, 256 * h + 128)), V("ident"), col(13), A.mult, -BIG, A.mult)
         ts(V("ol2", S(256 * h, 256 * h + 128)), V("ident"), col(12), A.mult, -BIG, A.mult)
     ts(V("og1", S(0, 128)), V("ident"), col(13), A.mult, BIG, A.mult)
-    ts(V("og1", S(128, 256)), V("ident"), col(11), A.mult)
+    for j in range(4):
+        lin(V("ok", S(128 * j, 128 * j + 128)), V("ident"), col(11))
+    lin(V("idn"), V("ident"), -1.0)
     ts(V("og2", S(0, 128)), V("ident"), col(14), A.mult, BIG, A.mult)
 
     def late_constants():
@@ -281,7 +284,7 @@ def rank_program(g, core, T, topo):
         fill(V("rst"), 0)
         fill(V("mb", S(15, 256, 16)), 0)
         fill(V("stp", S(0, 256, 16)), -16000000)
-        fill(V("seg", S(0, 512, 16)), 0)
+        fill(V("seg", S(0, 256, 16)), 0)
         fill(V("rst", S(15, 512, 16)), 1)
         act(V("mb", S(256, 512)), V("mb", S(0, 256)), FN.Copy)
         act(V("mbf", S(0, 256)), V("mb", S(0, 256)), FN.Copy)
@@ -381,7 +384,9 @@ def rank_program(g, core, T, topo):
 
     def open_g(v):
         for h in range(2):
-            mm(V("pG", h, S(0, 384)), V("ones"), V("og1"), True, False)
+            mm(V("pG", h, S(0, 256)), V("ones"), V("og1", S(0, 256)), True, False)
+            if h == 0:
+                mm(V("pB"), V("ones"), V("ok"), True, False)
             mm(V("pG", h, S(0, 128)), V("ones"), V("og2", S(0, 128)), False, False)
             mm(V("pG", h, S(0, 128)), V("z%d" % v, S(128 * h, 128 * h + 128)), V("rz", S(128, 256)), False, False)
 
@@ -414,18 +419,21 @@ def rank_program(g, core, T, topo):
     def hd_mm(h):
         o = 2048 * h
         for k in range(16):
-            mm(V("pG", h, S(256 + k, 384, 16)), V("gh", S(o + k, o + 2048, 16)), r8(3), False, False)
+            mm(V("pG", h, S(128 + k, 256, 16)), V("gh", S(o + k, o + 2048, 16)), r8(3), False, False)
+            mm(V("pB", S(256 * h + 128 + k, 256 * h + 256, 16)), V("gh", S(o + k, o + 2048, 16)), r8(6), False, False)
 
     def hg_mm(h):
         o = 4096 + 2048 * h
         for k in range(16):
-            mm(V("pG", h, S(k, 384, 16)), V("gh", S(o + k, o + 2048, 16)), r8(5, 3), False, k == 15)
+            mm(V("pG", h, S(k, 256, 16)), V("gh", S(o + k, o + 2048, 16)), r8(5, 2), False, k == 15)
+        for k in range(16):
+            mm(V("pB", S(256 * h + k, 256 * h + 128, 16)), V("gh", S(o + k, o + 2048, 16)), r8(6), False, False)
 
     both = S(0, 2)
     Lp, Dp = V("pL", both, S(128, 256)), V("pL", both, S(0, 128))
     L15 = V("pL", both, S(143, 256, 16))
     S15 = V("ss", S(15, 256, 16))
-    SG, SL = V("sg", S(15, 256, 16)), V("sg", S(271, 512, 16))
+    SG, SL = V("sg", both, S(15, 128, 16)), V("sg", both, S(143, 256, 16))
     scr = V("pS", S(0, 256))
 
     def l_side():
@@ -436,8 +444,9 @@ def rank_program(g, core, T, topo):
         scan(V("ss"), V("stp"), V("kf", S(0, 256)), 0.0, A.add, A.max)
         tt(scr, Lp, V("ss"), A.max)
         ops[-1]["early"] = EARLY[2]
-        ts(sm(3), S15, 1.0, A.add, 4096.0, A.mult)
-        ts(sm(9), S15, -4096.0, A.max, 6144.0, A.add)
+        lin(sm(3), S15, 4096.0, 4096.0)
+        act(sm(8), S15, FN.Relu, bias=4096.0)
+        lin(sm(9), sm(8), 1.0, 2048.0)
         ts(sm(5), V("pS", S(15, 256, 16)), -1.0, A.mult)
         tt(V("nw"), scr, V("rr"), A.min)
         tt(qi(4), sm(5), S15, A.max)
@@ -455,16 +464,21 @@ def rank_program(g, core, T, topo):
         tt(V(hname), ind(V("tab", S(XO, ZO + K)), V(off)), V("zb"), A.add)
         ts(out, V(hname), 0.5, A.mult, -1024.0, A.add)
 
-    Ep, Gp, Fp = V("pG", both, S(0, 128)), V("pG", both, S(128, 256)), V("pG", both, S(256, 384))
+    Ep, Fp = V("pG", both, S(0, 128)), V("pG", both, S(128, 256))
 
     def g_square():
         act(V("sq"), Fp, FN.Square, scale=512.0)
+        act(V("pen", S(0, 256)), Ep, FN.Relu, bias=BIG, scale=-1.0)
+        act(V("pen", S(256, 512)), V("sq"), FN.Relu, bias=BIG, scale=-1.0)
+        for h in range(2):
+            for i in range(2):
+                for wh in range(2):
+                    mm(V("pB", S(256 * h + 128 * wh, 256 * h + 128 * wh + 128)), V("idn"),
+                       V("pen", S(256 * i + 128 * h, 256 * i + 128 * h + 128)), False, h + i + wh == 3)
 
     def g_side():
-        tt(V("cc"), Ep, V("sq"), A.min)
-        tt(V("kf", S(0, 256)), Gp, V("cc"), A.min)
-        tt(V("kf", S(256, 512)), V("kf", S(0, 256)), Fp, A.subtract)
-        scan(V("sg"), V("seg"), V("kf"), 0.0, A.mult, A.max)
+        for h in range(2):
+            scan(V("sg", h), V("seg"), V("pB", S(256 * h, 256 * h + 256)), 0.0, A.mult, A.max)
         tt(qi(0), SG, V("zl"), A.max)
         tt(qi(1), SG, SL, A.max)
         ts(qi(3), qi(0), 4095, A.bitwise_and)
@@ -500,7 +514,7 @@ def rank_program(g, core, T, topo):
 
     def scatter_x():
         for c in range(15, -1, -1):
-            cp(ind(V("tab", S(XO, ZO)), V("o3", S(2 * c, 2 * c + 1))), V("vx", S(16 * c, 16 * c + 16)))
+            cp(ind(V("tab", S(XO, ZO)), V("o2", S(32 + 2 * c, 33 + 2 * c))), V("vx", S(16 * c, 16 * c + 16)))
 
     def scatter_f():
         for r in range(7, -1, -1):
@@ -511,16 +525,16 @@ def rank_program(g, core, T, topo):
         ts(dict(V("s4", S(0, 16, 2)), reg=[("s4", 0, 1)]), V("prf", S(14, 256, 32)), 0.0, A.is_equal, col(9), A.mult)
         ts(dict(V("s4", S(1, 16, 2)), reg=[("s4", 1, 2)]), V("prf", S(30, 256, 32)), 0.0, A.is_equal, col(15), A.mult)
         ts(V("s3", S(16, 24)), V("prf", S(271, 392, 17)), 0.0, A.is_equal, col(15), A.mult)
-        tt(V("s3", S(0, 16)), V("pD", S(368, 384)), V("s4"), A.max)
+        tt(V("s3", S(0, 16)), V("pC", S(272, 288)), V("s4"), A.max)
         tt(V("s3", S(1, 16, 2)), V("s3", S(1, 16, 2)), V("s3", S(16, 24)), A.max)
         cp(V("o1", S(0, 16)), V("s3", S(0, 16)))
 
     def dif_f():
-        for name, rhs, far in (("eh", "re_", "re2"), ("uh", "ri", "ri2")):
+        for name, rhs, far in (("uh", "ri", "ri2"), ("eh", "re_", "re2")):
             for h in range(2):
                 hs = S(128 * h, 128 * h + 128)
                 mm(V("pB", hs), V(name, hs), V(rhs), False, False)
-                mm(V("pB", S(256 + 68 * h, 324 + 68 * h)), V(name, hs), V(far), False, name == "uh" and h == 1)
+                mm(V("pB", S(256 + 68 * h, 324 + 68 * h)), V(name, hs), V(far), False, name == "eh" and h == 1)
 
     XS, ZP, ZA = SPLIT
     for v in range(VISITS):
@@ -546,16 +560,14 @@ def rank_program(g, core, T, topo):
         if XS:
             xf_part(0, XS, "dve")
         e_op("ec", sm(0))
-        for j in range(4):
+        for j in (0, 2, 1, 3):
             h_mm(j)
             h_cp(j)
         w_mm("ec", "pD", 320)
         open_l(v)
-        if v == 0:
-            for j in range(4):
-                cp(V("bt", S(512 * j, 512 * j + 512)), V("bi", S(512 * j, 512 * j + 512)))
         g_max(v, 0, 0)
         cp(V("oc"), V("pD", S(320, 336)))
+        ops[-1]["early"] = 0.0 if v else EARLY[0]
         cp(V("bc"), ind(V("bt", S(0, W)), V("oc")))
         ops[-1]["early"] = EARLY[0] if v else 0.0
         g_h(v, 0, 0)
@@ -579,11 +591,18 @@ def rank_program(g, core, T, topo):
         m_mm(1, 0)
         hl_mm(1)
         hd_mm(1)
+        n0 = len(ops)
         g_max(v, 1, 1)
+        n1 = len(ops)
+        l_side()
+        if WEAVE:
+            pieces, steps = ops[n0:n1], ops[n1:]
+            for o in steps[:len(pieces)]:
+                o["chain"] = "gm"
+            ops[n0:] = [o for pair in zip(steps, pieces) for o in pair] + steps[len(pieces):]
         g_h(v, 1, 1)
         m_mm(1, 1)
         hg_mm(0)
-        l_side()
         newk_mm()
         hg_mm(1)
         u_op("uw", sm(2))
@@ -591,38 +610,45 @@ def rank_program(g, core, T, topo):
         e_op("ev", sm(4))
         g_square()
         act(V("nk"), V("pC", S(0, 256)), FN.Abs)
+        if not last:
+            cp(V("ls%d" % v), V("nk"))
+            send("ls%d" % v, "l%d" % (v + 1), "al%d" % (v + 1), v + 1)
+            ops[-1]["early"] = 0.0 if v else EARLY[6]
         w_mm("ev", "pD", 352)
         w_mm("ew", "pD", 336)
         dif_mm("ew", "uw", "pA", 256, True)
-        mm(V("pB", S(0, 392)), V("idb"), V("mbf"), True, False)
         if last:
             dma("sync", T.yl[:], V("nk"))
             contest("pA", 2, V("pD", S(320, 352)), col(9))
-            cp(V("o2", S(0, 32, 2)), V("s2", S(32, 48)))
-            cp(V("o3", S(0, 32, 2)), V("s2", S(48, 64)))
+            cp(V("o2", S(0, 64, 2)), V("s2", S(32, 64)))
             scatter_b(0, 16)
-            dma("sync", T.yb[:], V("bt", S(0, W)))
-            ops[-1]["early"] = EARLY[3]
+            for j in range(4):
+                js = S(512 * j, 512 * j + 512)
+                for i in range(2):
+                    half = S(512 * j + 256 * i, 512 * j + 256 * i + 256)
+                    cp(V("bf", half), V("bt", half))
+                dma("sync", T.yb[:, js], V("bf", js))
+                ops[-1]["early"] = EARLY[3]
         g_side()
         e_op("eh", sm(6))
         halve("h1", "oz", V("zs%d" % v))
+        if last:
+            ops[-2]["early"] = EARLY[5]
         if not last:
             send("zs%d" % v, "z%d" % (v + 1), "az%d" % (v + 1), v + 1)
-            ops[-1]["early"] = EARLY[1] + (0.0 if v else 3000.0)
-            cp(V("ls%d" % v), V("nk"))
-            send("ls%d" % v, "l%d" % (v + 1), "al%d" % (v + 1), v + 1)
+            ops[-1]["early"] = EARLY[1]
         else:
             dma("act", T.yz[:], V("zs%d" % v))
-        w_mm("eh", "pD", 368)
+        mm(V("pB", S(0, 392)), V("idb"), V("mbf"), True, False)
         dif_f()
+        w_mm("eh", "pC", 272)
         lo_mm()
         act(V("vf"), V("pL", 0), FN.Copy)
         cp(V("ov"), V("pD", S(352, 368)))
         if not last:
             count_merges()
             contest("pA", 2, V("pD", S(320, 352)), col(9))
-            cp(V("o2", S(0, 32, 2)), V("s2", S(32, 48)))
-            cp(V("o3", S(0, 32, 2)), V("s2", S(48, 64)))
+            cp(V("o2", S(0, 64, 2)), V("s2", S(32, 64)))
             ops[-1]["early"] = EARLY[4]
         halve("h2", "ov", V("vx"))
         ops[-1]["early"] = EARLY[4]

@@ -1,16 +1,18 @@
+import numpy as np
 from concourse.bass import DstId, RemoteDMATransfer
 from concourse.mybir import dt, AluOpType, AxisListType, ActivationFunctionType
 
 W, K, VISITS = 2048, 256, 4
-BIG = float(2 ** 17)
+BIG = float(2 ** 20)
 ROUND = 1.5 * 2 ** 23
-XO, ZO = W + 48, 2 * W + 80
+R64, R4096 = 64 * ROUND, 4096 * ROUND
+RANK, SINK = float(2 ** 20), float(2 ** 33)
+BO, WW, HW = W + 72, W + 72, W + 256
 F32, BF16, I32, U16, F16 = "float32", "bfloat16", "int32", "uint16", "float16"
 
 SCRATCH = {
-    "pL": ("psum", [128, 2, 256], F32), "pG": ("psum", [128, 2, 512], F32), "pA": ("psum", [128, 512], F32),
-    "pB": ("psum", [128, 512], F32), "pC": ("psum", [128, 512], F32), "pD": ("psum", [128, 512], F32),
-    "pS": ("psum", [128, 512], F32),
+    "pz": ("psum", [128, 2, 512], F32), "pL": ("psum", [128, 2, 256], F32), "pG": ("psum", [128, 2, 512], F32),
+    "pA": ("psum", [128, 512], F32), "pC": ("psum", [128, 512], F32), "pD": ("psum", [128, 512], F32),
 }
 
 
@@ -19,29 +21,26 @@ def _sb(dtype, **kw):
         SCRATCH[n] = ("sbuf", [128] + (list(s) if isinstance(s, tuple) else [s]), dtype)
 
 
-_sb(BF16, tab=ZO + K, xf=W, hh=W, gm=8192, gh=8192, zrep=4096, vf=256, vx=256, mbf=392, fl=256,
-    z0=K, z1=K, z2=K, z3=K, zs0=K, zs1=K, zs2=K, zs3=K,
-    ones=128, idb=128, rz=256, r8=104, idn=128, pen=512, selz=144, pair=128, fi=128, mb=512, ol1=512, ol2=512, og1=256, ok=512, og2=128,
-    nm=16, a15=256, blkn=128, cu=32, lb=32)
-_sb(F32, bf=W, ident=128, blk=128, maske=256, ri=128, re_=128, rw=8, seg=256, rst=512, stp=256, ck=256, zl=16,
-    cols=16, tf=256, urep=256, kf=256, ss=256, sg=(2, 256), nw=256, nk=256, sq=256, zb=256,
-    uw=256, uh=256, uc=256, ew=256, eh=256, ec=256, ez=256, ev=256, sm=160, pr=512, s2=128, s3=32, fo=128,
-    ri2=68, re2=68, rsf=392, prf=392, s4=16)
-_sb(I32, bt=W + 32, fi2=128, li=K, ti=8, ia=256, ib=256, rr=256, qi=128, ai=128)
-_sb(U16, l0=K, l1=K, l2=K, l3=K, ls0=K, ls1=K, ls2=K, fw16=128, bc=K, ex=16, exl=16, o1=16, o2=64, oc=16, oz=16, ov=16)
-_sb(BF16, ul=256)
-_sb(F16, h1=256, h2=256)
+_sb(BF16, ft=WW + 8, ipart=W, ilo=W, vf=K, xin=BO, i512=1024, vxo=256, fl=256, zin=K,
+    z0=K, z1=K, z2=K, z3=K, zs0=K, zs1=K, zs2=K, zs3=K, y2=256, fp=256, cst=512,
+    ones=128, idb=128, idn=128, idh=128, i64=128, dq=128, rz=256, r8=16, pen=(2, 256), selz=144, rst=384, sd=384, pr=768,
+    ol1=512, ol2=128, og1=512, og2=384, sgn=32, a15=256, blkn=128, cu=32, cb=32)
+_sb(F32, xb=2 * BO, w0=WW, w1=WW, gl=2 * HW, gg=2 * HW, nl=256, vx=256, vw=256, ident=128, blk=128, maske=256,
+    rl=16, rg=24, rs2=256, stp=256, ck=256, cols=32, tf=256, urep=256, kf=256, ss=264, num=W, sel0=144, g8=8,
+    sg=520, gq=256, y1=256, sq=256, sm=136, s3=32, s4=32)
+_sb(I32, bt=W, fi2=128, li=K, ti=8, ia=256, ib=256, rr=256, qi=32, qc=96, qa=128, qj=(2, 2, 8))
+_sb(U16, l0=K, l1=K, l2=K, l3=K, ls0=K, ls1=K, ls2=K, fw16=128, bc=K, o1=16, o3=32, lists=80, own=24)
+LISTS = ("ex", "oc", "oz", "ov", "ol")
+_sb(F16, ri=192, lq=256, wq=256, uw=256, uh=256, uc=256, gm=8192, nw=256, idq=128, idf=128, ec=256, ew=256, ev=128, eh=256, el=128, ez=128, rm=16, re_=192, rw=8,
+    sel=240, selv=240, hx=K, hz=K, xh=W)
 
 SEMAPHORES = (["pe", "dve", "act", "pool", "sent"] + ["d%d" % i for i in range(24)]
               + ["al%d" % i for i in range(1, VISITS)] + ["az%d" % i for i in range(1, VISITS)])
 SAME_QUEUE_WAW = True
-SPLIT = (1024, 7, 14)
-LAT, HOLD, AHEAD = 200.0, 0.3, 1000.0
-EARLY = (6000.0, 3000.0, 3000.0, 2000.0, 2000.0, 3000.0, 6000.0)
-PIECES = (1, 1, 1, 4)
-HDVE, XP = (), 512
-WEAVE = True
-RATE = (0.85, 40.0, 1.15, 2.6, 1024)
+LAT, PASSES, SHAKE = 170.0, 6000, (1000.0, 3000.0, 0.05, 60.0, 0.3)
+DMA = (1300.0, 700.0, 100.0, 200.0)
+RATE = (0.85, 40.0, 1.25, 2.6)
+CFG = {"gp": (64, 32, 32, 32), "gdve": (64, 0, 0, 0), "cut": (128, 128), "wp": 512, "wdve": 1024, "w0dve": 1024, "pur": "dve", "pen": ("act", "dve"), "gq": ("act", "act"), "early": {}, "first": (), "ftab": True}
 MEMO = {}
 A = AluOpType
 FN = ActivationFunctionType
@@ -56,6 +55,8 @@ def rank_program(g, core, T, topo):
     ndma = [0]
 
     def V(name, *idx, part=slice(None)):
+        if name in LISTS:
+            return V("lists", slice(16 * LISTS.index(name), 16 * LISTS.index(name) + 16))
         shape = SCRATCH[name][1][1:]
         full = list(idx) + [slice(None)] * (len(shape) - len(idx))
         lo = hi = 0
@@ -92,9 +93,9 @@ def rank_program(g, core, T, topo):
         elif sem == "":
             cost = 4000.0
         elif sem is not None:
-            cost = 2000.0 + sides[0]["n"] * sides[0]["rows"] * sides[0]["size"] / 200.0
+            cost = DMA[2] + sides[0]["n"] * sides[0]["rows"] * sides[0]["size"] / DMA[3]
         elif eng == "pe":
-            cost = max(64, ins[1]["n"]) * (4 if ins[1]["size"] == 4 else 1) * RATE[0] / 2
+            cost = 8.0 + max(min(64, ins[0]["n"]), ins[1]["n"]) * (4 if ins[1]["size"] == 4 else 1) * RATE[0] / 2
         elif eng == "pool":
             cost = 170.0 + 2 * n * RATE[0]
         elif outs[0]["also"]:
@@ -134,8 +135,18 @@ def rank_program(g, core, T, topo):
     def act(o, a, func=FN.Identity, bias=0.0, scale=1.0):
         rec("act", lambda: g.scalar.activation(ap(o), ap(a), func, bias=ap(bias), scale=ap(scale)), [o], [a, bias, scale])
 
-    def mm(o, l, r, start, stop):
-        rec("pe", lambda: g.tensor.matmul(ap(o), ap(l), ap(r), start, stop), [o], [l, r])
+    def mm(o, l, r, start=False, strict=False):
+        end = [False]
+        rec("pe", lambda: g.tensor.matmul(ap(o), ap(l), ap(r), start, end[0]), [o], [l, r])
+        ops[-1].update(end=end, start=start, adds=not (start or strict))
+
+    def join(k):
+        part = ops[-k:]
+        del ops[-k:]
+        for a, b in zip(part, part[1:]):
+            a["end"][0] = b["start"]
+        ops.append(dict(part[-1], fn=lambda: [o["fn"]() for o in part][-1], r=[x for o in part for x in o["r"]],
+                        cost=sum(o["cost"] for o in part), start=part[0]["start"], adds=all(o["adds"] for o in part)))
 
     def iota(o, pat, base, cm):
         small = SCRATCH[o["reg"][0][0]][2] != I32
@@ -147,11 +158,10 @@ def rank_program(g, core, T, topo):
     def asel(o, a, pat, op, fill, base, cm):
         rec("pool", lambda: g.affine_select(ap(o), ap(a), pat, op, fill, base, cm), [o], [a])
 
-    def dma(q, o, a):
+    def dma(o, a):
         sem = "d%d" % ndma[0]
         ndma[0] += 1
-        e = {"sync": g.sync, "act": g.scalar, "pool": g}[q]
-        rec(q, lambda: e.dma_start(ap(o), ap(a)), [o] if isinstance(o, dict) else [], [a], sem=sem, count=16)
+        rec("sync", lambda: g.sync.dma_start(ap(o), ap(a)), [o] if isinstance(o, dict) else [], [a], sem=sem, count=16)
 
     def lanes_mask(src, dst):
         eng = [e for e in topo.engines(src, dst) if all(e in topo.engines(src, c) for c in T.cores if c != src)]
@@ -172,16 +182,55 @@ def rank_program(g, core, T, topo):
         n = lanes_mask(T.cores[(rank - s) % n_ranks], core)[1]
         rec("ext", None, [V(land)], [], sem=sem, count=n, ext=True)
 
+    def early(name, n=1):
+        for o in ops[-n:]:
+            o["early"] = CFG["early"].get(name, 0.0)
+
+    def chain(name):
+        ops[-1]["chain"] = name
+
+    named = {}
+
+    def name(n):
+        named[n] = ops[-1]
+        for a, b in CFG["first"]:
+            if n in (a, b) and a in named and b in named:
+                named[b].setdefault("behind", []).append(named[a])
+
+    def lin(o, a, scale, bias=0.0):
+        act(o, a, FN.Identity, bias=bias, scale=scale)
+
+    def either(first, second):
+        first()
+        second()
+        b = ops.pop()
+        ops[-1]["alt"] = {k: b[k] for k in ("eng", "fn", "cost")}
+
+    def mov(o, a, bias=0.0, scale=1.0, on="dve"):
+        if scale != 1.0:
+            d = lambda: ts(o, a, scale, A.mult, bias, A.add)
+        elif isinstance(bias, dict) or bias:
+            d = lambda: ts(o, a, bias, A.add)
+        else:
+            d = lambda: cp(o, a)
+        s = lambda: lin(o, a, scale, bias)
+        either(*((d, s) if on == "dve" else (s, d)))
+
+    def fill(o, c):
+        iota(o, [[0, o["n"]]], c, 0)
+
     col = lambda i: V("cols", S(i, i + 1))
     sm = lambda i, n=1: V("sm", S(16 * i, 16 * (i + n)))
-    qi = lambda i, n=1: V("qi", S(16 * i, 16 * (i + n)))
+    both = S(0, 2)
+    half = lambda name, h: V(name, S(128 * h, 128 * h + 128))
 
-    dma("sync", V("fi2"), T.fw[:])
-    dma("act", V("z0"), T.zz[:])
-    dma("sync", V("tab", S(XO, XO + W)), T.x[:])
-    dma("act", V("li"), T.la[:])
-    dma("act", V("ti", S(0, 1)), T.th[:])
-    ms(V("tab", S(0, W)), 0.0)
+    dma(V("fi2"), T.fw[:])
+    for a in (0, W // 2):
+        dma(V("xin", S(a, a + W // 2)), T.x[:, a:a + W // 2])
+    dma(V("zin"), T.zz[:])
+    dma(V("li"), T.la[:])
+    dma(V("ti", S(0, 1)), T.th[:])
+    ms(V("ft", S(0, W)), 0.0)
 
     iota(V("ia", S(0, 1)), [[0, 1]], 0, 1)
     ms(V("ident"), 1.0)
@@ -189,476 +238,491 @@ def rank_program(g, core, T, topo):
     asel(V("blk"), V("ident"), [[-16, 8], [0, 16]], A.is_ge, 0.0, 0, 1)
     asel(V("blk"), V("blk"), [[16, 8], [0, 16]], A.is_ge, 0.0, 15, -1)
     asel(V("ident"), V("ident"), [[-1, 128]], A.is_equal, 0.0, 0, 1)
+    iota(V("i512", S(0, 512)), [[16, 32], [0, 16]], 0, 0)
+    iota(V("i512", S(512, 1024)), [[0, 32], [1, 16]], 0, 0)
     cp(V("fl", S(128, 256)), V("fi2"))
     tt(V("fl", S(0, 128)), V("fi2"), V("fl", S(128, 256)), A.subtract)
-    dma("sync", V("tab", S(0, W), part=S(8, 128, 16)), V("fl", S(0, 128)))
-    dma("act", V("tab", S(0, W), part=S(9, 128, 16)), V("fl", S(128, 256)))
+    dma(V("ft", S(0, W), part=S(8, 128, 16)), V("fl", S(0, 128)))
+    dma(V("ft", S(0, W), part=S(9, 128, 16)), V("fl", S(128, 256)))
     ops[-1]["apart"] = ops[-2]["apart"] = True
-    dma("sync", V("bt", S(0, W)), T.bk[:])
+    dma(V("bt"), T.bk[:])
     ts(V("ib", S(0, 1)), V("ia", S(0, 1)), 15, A.bitwise_and)
     cp(col(0), V("ib", S(0, 1)))
-    ts(col(1), col(0), 8.0, A.is_lt)
+    ts(col(1), col(0), 0.0, A.is_equal)
     ts(col(2), col(0), 7.5, A.is_gt)
     ts(col(3), col(0), 9.5, A.is_lt)
     tt(col(2), col(2), col(3), A.mult)
     blk8 = V("blk", S(0, 128, 16))
     ms(V("selz"), 0.0)
     ts(V("selz", S(15, 143, 16)), blk8, col(2), A.mult)
-    asel(V("tf", S(0, 128)), V("blk"), [[-16, 8], [-2, 16]], A.is_ge, 0.0, 0, 1)
-    asel(V("pair"), V("tf", S(0, 128)), [[16, 8], [2, 16]], A.is_ge, 0.0, 1, -1)
+    ts(V("dq"), V("ident"), col(1), A.mult, 1 / 64, A.mult)
+    lin(V("i64"), V("ident"), 64.0)
+    for j in range(4):
+        lin(col(16 + j), col(1), 8.0 * j - 16)
     iota(V("ia", S(16, 32)), [[1, 16]], 0, 0)
-    iota(V("zl"), [[128, 2], [0, 8]], ZO - XO, 1)
-    iota(V("kf", S(0, 256)), [[0, 16], [1, 16]], 0, 0)
-    def lin(o, a, scale, bias=0.0):
-        act(o, a, FN.Identity, bias=bias, scale=scale)
-
-    def fill(o, c):
-        iota(o, [[0, o["n"]]], c, 0)
-
-    lin(V("fi"), V("ident"), col(2))
-    lin(col(4), col(1), -256.0)
-    lin(col(5), col(0), 14.0, 39.0)
-    lin(col(6), col(0), 20.0, 10.0)
-    ts(V("ib", S(1, 2)), V("ia", S(0, 1)), 31, A.bitwise_and)
-    ts(col(7), V("ib", S(1, 2)), float(W + 16), A.add)
-    lin(col(9), col(0), 1.0, float(W + 16))
-    lin(col(15), col(0), 1.0, float(W + 32))
-    lin(col(8), col(2), -1.0)
-    ts(col(10), col(0), 9.0, A.is_equal, 16.0, A.mult)
-    lin(col(11), col(0), -4096.0, 65536.0)
-    r8 = lambda i, n=1: V("r8", S(8 * i, 8 * (i + n)))
-    lin(V("rz", S(0, 128)), V("blk"), -BIG)
-    lin(V("rz", S(128, 256)), V("blk"), BIG)
-    lin(r8(0), blk8, 2 * BIG)
-    lin(r8(1), blk8, -2 * BIG)
-    lin(r8(2), V("rz", S(0, 128, 16)), col(1))
-    lin(r8(3), blk8, col(8))
+    iota(V("kf"), [[0, 16], [1, 16]], 0, 0)
+    iota(V("cu"), [[255, 2], [0, 16]], 255, 0)
+    lin(V("z0"), V("zin"), 64.0)
+    lin(col(5), col(0), 14.0 / 64, 39.0 / 64)
+    lin(col(6), col(0), 20.0 / 64, 10.0 / 64)
+    lin(col(8), col(1), 64.0)
+    lin(col(11), col(0), -RANK, 15 * RANK)
+    lin(V("rz", S(0, 128)), V("blk"), -BIG / 64)
+    lin(V("rz", S(128, 256)), V("blk"), BIG / 64)
+    ts(V("rm", S(0, 8)), blk8, BIG / 32, A.mult)
+    ts(V("rm", S(8, 16)), blk8, -BIG / 32, A.mult)
+    lin(V("rl", S(0, 8)), blk8, -BIG / 64)
+    lin(V("rg", S(16, 24)), blk8, BIG / 64)
+    lin(V("rg", S(8, 16)), blk8, col(8))
+    lin(V("rg", S(0, 8)), blk8, col(8))
+    lin(V("rl", S(8, 16)), V("rg", S(8, 16)), -1.0)
     cp(V("idb"), V("ident"))
-    lin(r8(5), V("rz", S(128, 256, 16)), col(1))
-    lin(r8(6), blk8, col(2))
-    lin(r8(7), blk8, col(2))
-    ts(r8(8), blk8, col(5), A.mult)
-    ts(r8(9), blk8, col(6), A.mult)
+    ts(V("r8", S(0, 8)), blk8, col(5), A.mult)
+    ts(V("r8", S(8, 16)), blk8, col(6), A.mult)
     cp(V("l0"), V("li"))
     cp(V("ex"), V("ia", S(16, 32)))
-    ts(V("exl"), V("ia", S(16, 32)), col(10), A.add)
-    iota(V("cu"), [[255, 2], [0, 16]], 255, 0)
-    lin(V("rw"), blk8, 1.0)
-    ts(V("maske"), V("kf", S(0, 256)), col(0), A.is_equal)
-    ts(V("ti", S(1, 2)), V("ti", S(0, 1)), 2048.0, A.add)
-    ts(V("ti", S(2, 3)), V("ti", S(1, 2)), 127, A.bitwise_and)
-    ts(V("ti", S(3, 4)), V("ti", S(1, 2)), 8064, A.bitwise_and)
+    cp(V("rw"), blk8)
+    ts(V("maske"), V("kf"), col(0), A.is_equal)
+    ts(V("ti", S(2, 3)), V("ti", S(0, 1)), 127, A.bitwise_and)
+    ts(V("ti", S(3, 4)), V("ti", S(0, 1)), 8064, A.bitwise_and)
     cp(V("cols", S(12, 14)), V("ti", S(2, 4)))
-    ts(col(14), col(12), 1.0, A.add)
     ts(col(12), col(12), 0.5, A.add)
-    for nm_ in ("ol1", "ol2", "og1", "og2"):
-        ms(V(nm_), 0.0)
     for h in range(2):
         ts(V("ol1", S(256 * h, 256 * h + 128)), V("ident"), col(13), A.mult, -BIG, A.mult)
-        ts(V("ol2", S(256 * h, 256 * h + 128)), V("ident"), col(12), A.mult, -BIG, A.mult)
-    ts(V("og1", S(0, 128)), V("ident"), col(13), A.mult, BIG, A.mult)
-    for j in range(4):
-        lin(V("ok", S(128 * j, 128 * j + 128)), V("ident"), col(11))
+        lin(V("ol1", S(256 * h + 128, 256 * h + 256)), V("ident"), -1024.0)
+    ts(V("ol2"), V("ident"), col(12), A.mult, -BIG, A.mult)
+    lin(V("og2", S(256, 384)), V("ol1", S(0, 128)), -1.0)
+    lin(V("og2", S(0, 128)), V("ident"), 1024.0)
+    lin(V("og2", S(128, 256)), V("ident"), 1024.0)
+    lin(V("og1", S(256, 384)), V("ol2"), -1.0)
+    lin(V("og1", S(0, 128)), V("ident"), col(11))
+    lin(V("og1", S(128, 256)), V("ident"), col(11))
     lin(V("idn"), V("ident"), -1.0)
-    ts(V("og2", S(0, 128)), V("ident"), col(14), A.mult, BIG, A.mult)
 
     def late_constants():
-        kk = V("kf", S(0, 256))
-        act(V("ri"), V("ident"), FN.Identity, scale=1.0 / 64)
-        act(V("re_"), V("blk"), FN.Identity, scale=-1.0 / 64)
-        act(V("ck"), kk, FN.Identity, scale=613.0 * 32)
-        fill(V("ri", S(15, 128, 16)), 0)
-        fill(V("re_", S(15, 128, 16)), 0)
-        ts(V("mb", S(0, 256)), kk, col(0), A.is_ge, 128.0, A.mult)
-        fill(V("ri2"), 0)
-        fill(V("re2"), 0)
+        kk = V("kf")
+        cp(V("idq"), V("ident"))
+        lin(V("ck"), kk, 613.0 * 32)
+        lin(V("idh"), V("ident"), 0.5)
+        fill(V("tf", S(0, 192)), 1)
+        asel(V("y1", S(0, 192)), V("tf", S(0, 192)), [[-32, 4], [-16, 3], [1, 16]], A.is_equal, 0.0, -15, 1)
+        asel(V("sq", S(0, 192)), V("tf", S(0, 192)), [[-32, 4], [-16, 3], [1, 16]], A.is_equal, 0.0, 17, 1)
         for j in range(4):
-            lin(V("ri2", S(17 * j, 17 * j + 16)), V("ident", S(32 * j, 32 * j + 16)), 1.0 / 64)
-            lin(V("re2", S(17 * j, 17 * j + 16)), V("blk", S(32 * j + 16, 32 * j + 32)), -1.0 / 64)
-        fill(V("rsf"), 0)
-        fill(V("rsf", S(15, 256, 16)), 1)
-        fill(V("rsf", S(272, 392, 17)), 1)
-        fill(V("mbf", S(256, 392)), 0)
+            lin(V("ri", S(48 * j, 48 * j + 32)), V("y1", S(48 * j, 48 * j + 32)), 1.0)
+            lin(V("ri", S(48 * j + 32, 48 * j + 48)), V("sq", S(48 * j + 32, 48 * j + 48)), 1.0)
+            lin(V("re_", S(48 * j, 48 * j + 32)), V("blk", S(32 * j, 32 * j + 32)), -1.0)
+            lin(V("re_", S(48 * j + 32, 48 * j + 48)), V("blk", S(32 * j + 16, 32 * j + 32)), -1.0)
+        iota(V("pr", S(0, 384)), [[0, 24], [-1, 16]], 15, 0)
+        ts(V("rst"), V("pr", S(0, 384)), col(0), A.is_equal, 4096.0, A.mult)
+        asel(V("rst"), V("rst"), [[0, 8], [1, 3], [0, 16]], A.not_equal, 0.0, -2, 0)
         fill(V("stp"), 4096)
-        fill(V("seg"), 1)
-        fill(V("rst"), 0)
-        fill(V("mb", S(15, 256, 16)), 0)
+        lin(V("wq"), kk, 0.0)
+        lin(V("idf"), V("ident"), -1.0)
         fill(V("stp", S(0, 256, 16)), -16000000)
-        fill(V("seg", S(0, 256, 16)), 0)
-        fill(V("rst", S(15, 512, 16)), 1)
-        act(V("mb", S(256, 512)), V("mb", S(0, 256)), FN.Copy)
-        act(V("mbf", S(0, 256)), V("mb", S(0, 256)), FN.Copy)
         asel(V("blkn"), V("ones"), [[-1, 8], [0, 16]], A.is_equal, 0.0, 0, 1)
         lin(V("blkn"), V("blkn"), -BIG)
+        cp(col(4), V("ia", S(0, 1)))
+        ts(V("ib", S(1, 2)), V("ia", S(0, 1)), 31, A.bitwise_and)
+        cp(col(7), V("ib", S(1, 2)))
+        lin(col(14), col(0), 2.0, float(W + 2))
+        lin(col(15), col(0), 2.0, float(W + 34))
+        lin(col(10), col(0), 9.0, W / 2 + 8)
+        lin(col(20), col(0), 16.0, 15.0 - 8 * 1040)
+        lin(col(21), col(4), -7.0, W / 2 - 7)
+        lin(col(22), col(21), -2 * RANK)
+        lin(V("sel"), V("kf", S(0, 240)), 0.0)
+        lin(V("sel", S(112, 128)), V("maske", S(0, 16)), 1.0)
+        lin(V("selv"), V("sel"), col(21))
+        ts(V("ib", S(2, 3)), V("ia", S(0, 1)), 7, A.bitwise_and)
+        ts(V("ib", S(3, 4)), V("ia", S(0, 1)), 4, A.arith_shift_right)
+        ts(V("ib", S(4, 5)), V("ia", S(0, 1)), 3, A.arith_shift_right, 1, A.bitwise_and)
+        tt(col(24), V("ib", S(2, 3)), V("ib", S(3, 4)), A.is_equal)
+        cp(col(25), V("ib", S(4, 5)))
+        for i, (first, per_g, per_h, filler) in enumerate(((15, 16, 128, 256), (143, 16, 256, 512), (112, 1, 8, 128))):
+            lin(col(26), col(25), float(per_h), float(first - filler))
+            lin(V("g8"), V("kf", S(0, 8)), float(per_g), col(26))
+            ts(V("own", S(8 * i, 8 * i + 8)), V("g8"), col(24), A.mult, float(filler), A.add)
+        lin(V("ss", S(256, 264)), blk8, 0.0, -0.5)
+        lin(V("sg", S(512, 520)), blk8, 0.0)
+        lin(V("sm", S(128, 136)), blk8, 0.0)
+        lin(V("sel0"), V("kf", S(0, 144)), 0.0)
+        lin(V("sel0", S(15, 143, 16)), blk8, col(8))
+        lin(col(23), col(7), 2.0, W + 2 - RANK)
+        fill(V("rs2"), 2 ** 23)
+        lin(V("rs2"), V("rs2"), 4.0)
+        lin(V("rs2", S(0, 128, 16)), blk8, 0.0, col(23))
+        lin(V("rs2", S(128, 256, 16)), blk8, 0.0, col(22))
+        iota(V("cb", S(0, 16)), [[HW, 2], [256, 8]], 0, 0)
+        iota(V("cb", S(16, 32)), [[HW, 2], [144, 8]], 0, 0)
+        for i, c in enumerate((R64, -R64)):
+            lin(V("cst", S(256 * i, 256 * i + 256)), V("maske"), 0.0, c)
+        iota(V("num"), [[1, W]], 0, 0)
+        if CFG["ftab"]:
+            iota(V("ipart"), [[16, 128], [0, 16]], 0, 0)
+            iota(V("ilo"), [[0, 128], [1, 16]], 0, 0)
+            dma(V("ipart", part=S(8, 128, 16)), V("ilo", part=S(8, 128, 16)))
 
-    def spread_z(v, levels, eng):
-        a = V("z%d" % v)
-        for k in levels:
-            o = dict(V("zrep", S(k, 4096, 16)), reg=[("zrep", k, k + 1)])
-            if eng == "act":
-                act(o, a, FN.Copy)
-            elif eng == "dve":
-                cp(o, a)
-            else:
-                asel(o, a, [[0, K]], A.is_ge, 0.0, 0, 0)
-            ops[-1]["chain"] = "z" + eng
+    XW, BW = V("xb", S(0, W)), V("xb", S(BO, BO + W))
 
-    def fw_mm(wrapped):
+    def first_x():
+        banks = [V("pA"), V("pC"), V("pG", 0), V("pG", 1)]
+        for j in range(4):
+            mm(banks[j], V("dq"), V("i512", S(0, 512)), True, False)
+            mm(banks[j], V("dq"), V("i512", S(512, 1024)), False, False)
+        for j in range(4):
+            js = S(512 * j, 512 * j + 512)
+            mm(banks[j], V("i64"), V("xin", js), False, True)
+            mov(V("xb", js), banks[j], col(16 + j), on="act" if j % 2 else "dve")
+
+    def forwards(v):
+        ps = V("pC" if v else "pD", S(0, 128))
+        v = 0 if CFG["ftab"] else v
         for p in range(16):
-            rhs = V("tab", S(p, W, 16)) if wrapped else V("tab", S(128 * p, 128 * p + 128))
-            mm(V("pD", S(0, 128)), V("selz", S(15 - p, 143 - p)), rhs, p == 0, p == 15)
+            mm(ps, V("sel0" if v else "selz", S(15 - p, 143 - p)), V("w%d" % (v % 2) if v else "ft", S(p, W, 16)), p == 0)
+            if p % 2:
+                join(2)
+                chain("f")
+        if v:
+            mov(V("fi2"), ps, 1024.0)
+            ts(V("fi2"), V("fi2"), 2047, A.bitwise_and)
+        mov(V("fw16"), V("fi2") if v else ps)
 
-    hbank = [V("pA"), V("pB"), V("pG", 0), V("pG", 1)]
-    XW = V("tab", S(XO, XO + W))
+    def w_gather(v, by_dve, table):
+        for a in range(0, W, CFG["wp"]):
+            b = a + CFG["wp"]
+            o, src = V("w%d" % (v % 2), S(a, b)), ind(table, V("fw16", S(a // 16, b // 16)))
+            mov(o, src, on="dve" if a < by_dve else "act")
 
-    def xf_part(a, b, eng):
-        cuts = [a] + [c for c in range(XP, W, XP) if a < c < b] + [b]
-        for a, b in zip(cuts, cuts[1:]):
-            src = ind(XW, V("fw16", S(a // 16, b // 16)))
-            if eng == "dve":
-                cp(V("xf", S(a, b)), src)
-            else:
-                act(V("xf", S(a, b)), src, FN.Copy)
-
-    def h_mm(j):
-        mm(hbank[j], V("fi"), V("tab", S(512 * j, 512 * j + 512)), True, False)
-        mm(hbank[j], V("pair"), V("xf", S(512 * j, 512 * j + 512)), False, True)
-
-    def h_cp(j):
-        if j in HDVE:
-            ts(V("hh", S(512 * j, 512 * j + 512)), hbank[j], col(4), A.add)
-            ops[-1]["chain"] = "gm"
-            ops[-1]["early"] = EARLY[5]
-        else:
-            act(V("hh", S(512 * j, 512 * j + 512)), hbank[j], FN.Identity, bias=col(4))
-            ops[-1]["chain"] = "gh"
-
-    def cell_mm(v):
-        mm(V("pC", S(288, 320)), V("idb"), V("cu"), True, False)
+    def cell_part(v):
+        ps = V("pD", S(128, 160))
+        mm(ps, V("idb"), V("cu"), True, False)
         for wh in range(2):
             for h in range(2):
-                o = 288 + 16 * wh + 8 * h
-                mm(V("pC", S(o, o + 8)), V("z%d" % v, S(128 * h, 128 * h + 128)), r8(8 + wh), False, wh + h == 2)
-
-    def cell_act():
-        y1, y2 = V("s2", S(64, 96)), V("s2", S(96, 128))
-        act(y1, V("pC", S(288, 320)), FN.Identity, bias=2.0 ** -12 - 0.5, scale=1 / 2048)
-        act(y2, y1, FN.Identity, bias=ROUND)
-        act(y1, y2, FN.Identity, bias=2048 * ROUND, scale=-2048.0)
-
-    def cell_small():
-        tt(sm(0, 2), V("pC", S(288, 320)), V("s2", S(64, 96)), A.add)
+                o = 128 + 16 * wh + 8 * h
+                mm(V("pD", S(o, o + 8)), half("z%d" % v, h), V("r8", S(8 * wh, 8 * wh + 8)))
+        join(5)
+        mov(V("qc", S(0, 32)), ps)
+        ts(V("qc", S(32, 64)), V("qc", S(0, 32)), 2047, A.bitwise_and)
 
     def e_op(name, src):
         tt(V(name), ind(src, V("ex")), V("maske"), A.mult)
 
     def u_op(name, src):
-        act(V(name), ind(src, V("ex")), FN.Copy)
+        mov(V(name), ind(src, V("ex")), on="act")
 
-    def w_mm(name, ps, o):
+    def w_mm(name, o):
         for h in range(2):
-            mm(V(ps, S(o + 8 * h, o + 8 * h + 8)), V(name, S(128 * h, 128 * h + 128)), V("rw"), True, True)
+            mm(V("pD", S(o + 8 * h, o + 8 * h + 8)), half(name, h), V("rw"), True)
+        join(2)
 
-    def dif_open(ps, n):
-        mm(V(ps, S(0, n)), V("idb"), V("mb", S(0, n)), True, False)
+    def own_mm(name, i, win, o, sel="sel", base=None, **kw):
+        act(V(name), ind(V(win), V("own", S(8 * i, 8 * i + 8))), **kw)
+        if base is not None:
+            mm(V("pD", S(o, o + 16)), V("idb"), V("cb", S(base, base + 16)), True)
+        for j in range(8):
+            mm(V("pD", S(o, o + 16)), V(sel, S(112 - 16 * j, 240 - 16 * j)), V(name, S(16 * j, 16 * j + 16)), base is None and j == 0)
+        join(8 if base is None else 9)
 
-    def dif_mm(e, u, ps, o, stop):
-        for name, rhs in ((e, "re_"), (u, "ri")):
+    def dif(e, u, o, *bank):
+        for h in range(2):
+            mm(V(*bank, S(192 * h, 192 * h + 192)), half(e, h), V("re_"), True)
+            mm(V(*bank, S(192 * h, 192 * h + 192)), half(u, h), V("ri"))
+        join(4)
+        act(V("sd"), V(*bank, S(0, 384)), FN.Abs)
+        scan(V("pr", S(o, o + 384)), V("sd"), V("rst"), 1.0, A.min, A.max)
+
+    def open_z(v):
+        for h in range(2):
+            for j in range(4):
+                mm(V("pz", h, S(j, 512, 4)), V("idb"), half("z%d" % v, h), True)
+            join(4)
+        for name in ("gl", "gg"):
             for h in range(2):
-                mm(V(ps, S(o + 128 * h, o + 128 * h + 128)), V(name, S(128 * h, 128 * h + 128)), V(rhs), False,
-                   stop and name == u and h == 1)
-
-    def contest(ps, n, wv, dcol):
-        scan(V("pr", S(0, 256 * n)), V(ps, S(0, 256 * n)), V("rst", S(0, 256 * n)), 1.0, A.mult, A.add)
-        ts(V("s2", S(0, 16 * n)), V("pr", S(14, 256 * n, 16)), 0.0, A.is_equal, dcol, A.mult)
-        tt(V("s2", S(32, 32 + 16 * n)), wv, V("s2", S(0, 16 * n)), A.max)
+                asel(V(name, S(HW * h + W + 1, HW * h + HW, 2)), half("z%d" % v, h), [[0, 128]], A.is_ge, 0.0, 0, 0)
 
     def open_l(v):
-        mm(V("pL"), V("ones"), V("ol1"), True, False)
-        mm(V("pL"), V("ones"), V("ol2"), False, False)
+        d = [V("pL", h, S(0, 128)) for h in range(2)]
+        mm(V("pL"), V("ones"), V("ol1"), True)
         for h in range(2):
-            mm(V("pL", h, S(0, 128)), V("z%d" % v, S(128 * h, 128 * h + 128)), V("rz", S(0, 128)), False, False)
-            if v > 0:
+            mm(d[h], V("ones"), V("ol2"))
+        join(3)
+        for h in range(2):
+            mm(d[h], half("z%d" % v, h), V("rz", S(0, 128)))
+        join(2)
+        if v > 0:
+            for h in range(2):
                 for i in range(2):
-                    mm(V("pL", h, S(0, 128)), V("a15", S(128 * i, 128 * i + 128), part=S(0, 8)), V("blkn", part=S(0, 8)), False, False)
+                    mm(d[h], V("a15", S(128 * i, 128 * i + 128), part=S(0, 8)), V("blkn", part=S(0, 8)))
+            join(4)
 
-    def open_g(v):
-        for h in range(2):
-            mm(V("pG", h, S(0, 256)), V("ones"), V("og1", S(0, 256)), True, False)
-            if h == 0:
-                mm(V("pB"), V("ones"), V("ok"), True, False)
-            mm(V("pG", h, S(0, 128)), V("ones"), V("og2", S(0, 128)), False, False)
-            mm(V("pG", h, S(0, 128)), V("z%d" % v, S(128 * h, 128 * h + 128)), V("rz", S(128, 256)), False, False)
+    def open_g(v, h):
+        mm(V("pG", h, S(128, 512)), V("ones"), V("og2"), True)
+        mm(V("pG", h, S(384, 512)), V("ones"), V("og1", S(256, 384)))
+        mm(V("pG", h, S(384, 512)), half("z%d" % v, h), V("rz", S(128, 256)))
+        join(3)
 
-    def offs(v, side, h):
-        return V("l%d" % v if side == 0 else "bc", S(128 * h, 128 * h + 128))
+    def gather(v, side, h):
+        n = CFG["gp"][2 * side + 1 - h]
+        for a in range(0, 128, n):
+            o = V("gg" if side else "gl", S(HW * h + 16 * a, HW * h + 16 * (a + n)))
+            src = ind(V("w%d" % (v % 2), S(0, W)), V("bc" if side else "l%d" % v, S(128 * h + a, 128 * h + a + n)))
+            if a < CFG["gdve"][2 * side + 1 - h]:
+                mov(o, src)
+            else:
+                act(o, src, FN.Copy)
+                chain("gh")
 
-    def g_max(v, side, h):
-        n = PIECES[2 * side + h]
-        for j in range(n):
-            a, b = 128 * h + 128 * j // n, 128 * h + 128 * (j + 1) // n
-            tt(V("gm", S(4096 * side + 16 * a, 4096 * side + 16 * b)), ind(V("xf"), V("bc" if side else "l%d" % v, S(a, b))),
-               dict(V("zrep", S(16 * a, 16 * b)), reg=[("zrep", 0, 16)]), A.max)
-            ops[-1]["chain"] = "gm"
-
-    def g_h(v, side, h):
+    def gm(side, h, k, step, a=0, b=128):
         o = 4096 * side + 2048 * h
-        act(V("gh", S(o, o + 2048)), ind(V("hh"), offs(v, side, h)), FN.Copy)
-        ops[-1]["chain"] = "gh"
+        i = 2 * (8 * side + 4 * h + k % 4)
+        return dict(V("gm", S(o + 16 * a + k, o + 16 * b, step)), reg=[("gm", i + (a > 0), i + 1 + (b == 128))])
 
-    def m_mm(side, h):
-        o = 4096 * side + 2048 * h
-        for k in range(16):
-            mm(V("pG" if side else "pL", h, S(k, 128, 16)), V("gm", S(o + k, o + 2048, 16)), r8(side), False, False)
+    def g_max(side, h, j, a=0, b=128):
+        tt(gm(side, h, j, 4, a, b), V("gg" if side else "gl", S(HW * h + 16 * a + j, HW * h + 16 * b, 4)), V("pz", h, S(4 * a, 4 * b)), A.max)
+        chain("gm")
+        name("max%d%d%d" % (side, h, j))
 
-    def hl_mm(h):
-        o = 2048 * h
-        for k in range(16):
-            mm(V("pL", h, S(k, 256, 16)), V("gh", S(o + k, o + 2048, 16)), r8(2, 2), False, h == 1 and k == 15)
+    def x_mm(side, h, ks, a=0, b=128):
+        for k in ks:
+            mm(V("pG", h, S(128 + k, 512, 16), part=S(a, b)) if side else V("pL", h, S(k, 256, 16), part=S(a, b)),
+               V("gg" if side else "gl", S(HW * h + 16 * a + k, HW * h + 16 * b, 16)), V("rg" if side else "rl"))
+            if k % 2:
+                join(2)
+                chain("x")
 
-    def hd_mm(h):
-        o = 2048 * h
-        for k in range(16):
-            mm(V("pG", h, S(128 + k, 256, 16)), V("gh", S(o + k, o + 2048, 16)), r8(3), False, False)
-            mm(V("pB", S(256 * h + 128 + k, 256 * h + 256, 16)), V("gh", S(o + k, o + 2048, 16)), r8(6), False, False)
+    def m_mm(side, h, j, a=0, b=128):
+        for k in range(j, 16, 4):
+            mm(V("pG", h, S(384 + k, 512, 16), part=S(a, b)) if side else V("pL", h, S(k, 128, 16), part=S(a, b)),
+               gm(side, h, k, 16, a, b), V("rm", S(8 * side, 8 * side + 8)))
+        join(4)
 
-    def hg_mm(h):
-        o = 4096 + 2048 * h
-        for k in range(16):
-            mm(V("pG", h, S(k, 256, 16)), V("gh", S(o + k, o + 2048, 16)), r8(5, 2), False, k == 15)
-        for k in range(16):
-            mm(V("pB", S(256 * h + k, 256 * h + 128, 16)), V("gh", S(o + k, o + 2048, 16)), r8(6), False, False)
+    def side_mm(side, h, a=0, b=128):
+        for j in range(4):
+            g_max(side, h, j, a, b)
+        x_mm(side, h, range(0, 8), a, b)
+        m_mm(side, h, 0, a, b)
+        x_mm(side, h, range(8, 12), a, b)
+        m_mm(side, h, 1, a, b)
+        x_mm(side, h, range(12, 16), a, b)
+        m_mm(side, h, 2, a, b)
+        m_mm(side, h, 3, a, b)
 
-    both = S(0, 2)
+    cuts = lambda c: [(0, c), (c, 128)] if c < 128 else [(0, 128)]
+
     Lp, Dp = V("pL", both, S(128, 256)), V("pL", both, S(0, 128))
-    L15 = V("pL", both, S(143, 256, 16))
-    S15 = V("ss", S(15, 256, 16))
-    SG, SL = V("sg", both, S(15, 128, 16)), V("sg", both, S(143, 256, 16))
-    scr = V("pS", S(0, 256))
+    wcol = V("qc", S(80, 96))
+    scr, ss = V("pA", S(256, 512)), V("ss", S(0, 256))
+    scr15 = V("pA", S(271, 512, 16))
+    vx = V("vx")
 
-    def l_side():
+    def l_clean():
+        if CFG["pur"] == "act":
+            lin(V("y1"), Lp, 1.0, R4096)
+            lin(V("y2"), V("y1"), 1.0, -R4096)
+        else:
+            ts(V("y2"), Lp, R4096, A.add, -R4096, A.add)
+        tt(Lp, Lp, V("y2"), A.subtract)
+
+    def l_rename():
         tt(scr, Lp, V("urep"), A.mult)
+        name("times")
+        mov(V("lq"), Lp, on="act")
         tt(V("ia"), V("ck"), scr, A.subtract)
         ts(V("rr"), V("ia"), 5, A.arith_shift_right, 2047, A.bitwise_and)
-        tt(V("kf", S(0, 256)), Dp, V("rr"), A.min)
-        scan(V("ss"), V("stp"), V("kf", S(0, 256)), 0.0, A.add, A.max)
-        tt(scr, Lp, V("ss"), A.max)
-        ops[-1]["early"] = EARLY[2]
-        lin(sm(3), S15, 4096.0, 4096.0)
-        act(sm(8), S15, FN.Relu, bias=4096.0)
-        lin(sm(9), sm(8), 1.0, 2048.0)
-        ts(sm(5), V("pS", S(15, 256, 16)), -1.0, A.mult)
+
+    def l_pick():
+        tt(V("kf"), Dp, V("rr"), A.min)
+        name("fail")
+        scan(ss, V("stp"), V("kf"), 0.0, A.add, A.max)
+        tt(scr, Lp, ss, A.max)
+        act(V("qc", S(64, 80)), scr15, FN.Abs)
+        ts(wcol, V("qc", S(64, 80)), 2047, A.bitwise_and)
         tt(V("nw"), scr, V("rr"), A.min)
-        tt(qi(4), sm(5), S15, A.max)
-        tt(sm(3), sm(3), V("zl"), A.min)
-        ts(qi(5), qi(4), 2047, A.bitwise_and)
-        tt(sm(4), sm(5), sm(3), A.max)
-        cp(sm(2), qi(5))
 
-    def newk_mm():
-        for h in range(2):
-            hs = S(128 * h, 128 * h + 128)
-            mm(V("pC", hs), V("nw", hs), V("ident"), True, True)
+    def halve(name, win, off, ps):
+        mov(V(name), ind(V(win), V(off)), -16.0, 0.5, "act")
 
-    def halve(hname, off, out):
-        tt(V(hname), ind(V("tab", S(XO, ZO + K)), V(off)), V("zb"), A.add)
-        ts(out, V(hname), 0.5, A.mult, -1024.0, A.add)
+    def halve_mm(name, v, ps, stop):
+        mm(ps, V("idh"), V("z%d" % v), True)
+        mm(ps, V("idq"), V(name))
+        mm(ps, V("idb"), V("cst", S(0, 256)), False, True)
+        join(2)
 
-    Ep, Fp = V("pG", both, S(0, 128)), V("pG", both, S(128, 256))
-
-    def g_square():
-        act(V("sq"), Fp, FN.Square, scale=512.0)
-        act(V("pen", S(0, 256)), Ep, FN.Relu, bias=BIG, scale=-1.0)
-        act(V("pen", S(256, 512)), V("sq"), FN.Relu, bias=BIG, scale=-1.0)
-        for h in range(2):
-            for i in range(2):
-                for wh in range(2):
-                    mm(V("pB", S(256 * h + 128 * wh, 256 * h + 128 * wh + 128)), V("idn"),
-                       V("pen", S(256 * i + 128 * h, 256 * i + 128 * h + 128)), False, h + i + wh == 3)
-
-    def g_side():
-        for h in range(2):
-            scan(V("sg", h), V("seg"), V("pB", S(256 * h, 256 * h + 256)), 0.0, A.mult, A.max)
-        tt(qi(0), SG, V("zl"), A.max)
-        tt(qi(1), SG, SL, A.max)
-        ts(qi(3), qi(0), 4095, A.bitwise_and)
-        tt(qi(2), SG, SL, A.min)
-        e_op("ez", qi(3))
-        w_mm("ez", "pC", 256)
-        tt(V("nm"), SG, sm(9), A.is_le)
-        ts(qi(4, 2), qi(1, 2), 2047, A.bitwise_and)
-        ts(sm(5), V("nm"), col(7), A.mult)
-        cp(V("lb", S(16, 32)), qi(5))
-        tt(sm(6), qi(4), sm(5), A.max)
-        cp(V("oz"), V("pC", S(256, 272)))
-        u_op("uh", sm(6))
-        tt(V("lb", S(0, 16)), qi(5), V("lb", S(16, 32)), A.subtract)
-        act(V("ul"), ind(V("lb"), V("exl")), FN.Copy)
-
-    def lo_mm():
-        for h in range(2):
-            mm(V("pL", 0, S(128 * h, 128 * h + 128)), V("ul", S(128 * h, 128 * h + 128)), V("idb"), True, True)
+    def g_pen(h):
+        Ep, Fp = V("pG", h, S(384, 512)), V("pG", h, S(256, 384))
+        p1, p2 = V("pen", h, S(0, 128)), V("pen", h, S(128, 256))
+        either(lambda: ts(p1, Ep, 0.0, A.is_lt, SINK, A.mult), lambda: act(p1, Ep, FN.Relu, scale=-SINK * 8 / BIG))
+        if CFG["pen"][1 - h] == "act":
+            act(half("sq", h), Fp, FN.Abs, scale=SINK)
+            act(p2, half("sq", h), FN.Relu, bias=SINK, scale=-1.0)
+        else:
+            ts(p2, Fp, 0.0, A.is_equal, SINK, A.mult)
+        mov(half("gq", h), V("pG", h, S(128, 256)), on="act")
+        kl, kg = V("pL", h, S(0, 128)), V("pL", h, S(128, 256))
+        mm(V("pL", h), V("ones"), V("og1", S(0, 256)), True)
+        mm(kl, V("idf"), half("lq", h))
+        mm(kl, V("idn"), half("fp", h))
+        join(3)
+        for p in (p1, p2):
+            mm(kl, V("idn"), p)
+            mm(kg, V("idn"), p)
+        join(4)
+        mm(kg, V("ident"), half("gq", h))
+        scan(V("sg", S(256 * h, 256 * h + 256)), V("rs2"), V("pL", h), 0.0, A.min, A.max)
 
     def count_merges():
+        act(V("sgn"), V("sg", S(15, 512, 16)), FN.Sign, bias=0.5)
+        ps, y = V("pL", 0, S(0, 128), part=S(0, 8)), V("qa", part=S(0, 8))
         for h in range(2):
-            mm(V("pC", S(384, 512), part=S(0, 8)), V("nm", S(8 * h, 8 * h + 8)), V("ones"), h == 0, h == 1)
-        ps, y1, y2 = V("pC", S(384, 512), part=S(0, 8)), V("fo", part=S(0, 8)), V("tf", S(0, 128), part=S(0, 8))
-        act(y1, ps, FN.Identity, bias=16 - 15 / 32, scale=-1 / 16)
-        act(V("a15", S(0, 128), part=S(0, 8)), ps, FN.Identity, bias=256.0, scale=-1.0)
-        act(y2, y1, FN.Identity, bias=ROUND)
-        act(V("a15", S(128, 256), part=S(0, 8)), y2, FN.Identity, bias=16 * ROUND, scale=-16.0)
+            mm(ps, V("sgn", S(16 * h, 16 * h + 8)), V("ones"), h == 0)
+        join(2)
+        mov(y, ps, 8 - 15 / 32, 1 / 32, "act")
+        mov(V("a15", S(0, 128), part=S(0, 8)), ps, 128.0, 0.5, "act")
+        mov(V("a15", S(128, 256), part=S(0, 8)), y, 0.0, -16.0, "act")
 
-    def scatter_b(a, b):
-        for c in range(b - 1, a - 1, -1):
-            cp(ind(V("bt"), V("o2", S(2 * c, 2 * c + 1))), V("nk", S(16 * c, 16 * c + 16)))
+    def contest(o, n, places):
+        for i, c in ((0, 15), (1, 47)):
+            s, p = dict(V("s4", S(i, 16 * n, 2)), reg=[("s4", i, i + 1)]), V("pr", S(o + c, o + 384 * n, 48))
+            either(lambda: ts(s, p, 0.0, A.is_equal, col(14 + i), A.mult), lambda: act(s, p, FN.Relu, bias=col(14 + i), scale=-4096.0))
+        tt(V("s3", S(0, 16 * n)), places, dict(V("s4", S(0, 16 * n)), reg=[("s4", 0, 2)]), A.max)
 
-    def scatter_x():
-        for c in range(15, -1, -1):
-            cp(ind(V("tab", S(XO, ZO)), V("o2", S(32 + 2 * c, 33 + 2 * c))), V("vx", S(16 * c, 16 * c + 16)))
-
-    def scatter_f():
+    def rounds32(win, val, off="o1", o=0):
         for r in range(7, -1, -1):
-            cp(ind(V("tab", S(0, XO)), V("o1", S(2 * r, 2 * r + 2))), V("vf", S(32 * r, 32 * r + 32)))
+            cp(ind(win, V(off, S(o + 2 * r, o + 2 * r + 2))), V(val, S(32 * r, 32 * r + 32)))
 
-    def contest_f():
-        scan(V("prf"), V("pB", S(0, 392)), V("rsf"), 1.0, A.mult, A.add)
-        ts(dict(V("s4", S(0, 16, 2)), reg=[("s4", 0, 1)]), V("prf", S(14, 256, 32)), 0.0, A.is_equal, col(9), A.mult)
-        ts(dict(V("s4", S(1, 16, 2)), reg=[("s4", 1, 2)]), V("prf", S(30, 256, 32)), 0.0, A.is_equal, col(15), A.mult)
-        ts(V("s3", S(16, 24)), V("prf", S(271, 392, 17)), 0.0, A.is_equal, col(15), A.mult)
-        tt(V("s3", S(0, 16)), V("pC", S(272, 288)), V("s4"), A.max)
-        tt(V("s3", S(1, 16, 2)), V("s3", S(1, 16, 2)), V("s3", S(16, 24)), A.max)
-        cp(V("o1", S(0, 16)), V("s3", S(0, 16)))
-
-    def dif_f():
-        for name, rhs, far in (("uh", "ri", "ri2"), ("eh", "re_", "re2")):
-            for h in range(2):
-                hs = S(128 * h, 128 * h + 128)
-                mm(V("pB", hs), V(name, hs), V(rhs), False, False)
-                mm(V("pB", S(256 + 68 * h, 324 + 68 * h)), V(name, hs), V(far), False, name == "eh" and h == 1)
-
-    XS, ZP, ZA = SPLIT
+    first_x()
+    forwards(0)
+    w_gather(0, CFG["w0dve"], XW)
     for v in range(VISITS):
         last = v == VISITS - 1
-        XS = SPLIT[0] if v else RATE[4]
-        z = V("z%d" % v)
+        named.clear()
         if v > 0:
             arrive("l%d" % v, "al%d" % v, v)
             arrive("z%d" % v, "az%d" % v, v)
-        spread_z(v, range(0, ZP), "pool")
-        spread_z(v, range(ZP, ZA), "act")
-        cell_mm(v)
-        cell_act()
-        fw_mm(True)
-        if v > 0:
-            scatter_b(8, 16)
-        cp(V("fw16"), V("pD", S(0, 128)))
-        xf_part(XS, W, "act")
-        if v > 0:
-            scatter_b(0, 8)
-        spread_z(v, range(ZA, 16), "dve")
-        cell_small()
-        if XS:
-            xf_part(0, XS, "dve")
-        e_op("ec", sm(0))
-        for j in (0, 2, 1, 3):
-            h_mm(j)
-            h_cp(j)
-        w_mm("ec", "pD", 320)
+            forwards(v)
+        gather(v, 0, 1)
+        cell_part(v)
+        e_op("ec", V("qc", S(32, 48)))
+        w_mm("ec", 160)
+        mov(V("oc"), V("pD", S(160, 176)))
+        mov(V("bc"), ind(BW if v else V("bt"), V("oc")))
+        early("bc")
+        open_z(v)
         open_l(v)
-        g_max(v, 0, 0)
-        cp(V("oc"), V("pD", S(320, 336)))
-        ops[-1]["early"] = 0.0 if v else EARLY[0]
-        cp(V("bc"), ind(V("bt", S(0, W)), V("oc")))
-        ops[-1]["early"] = EARLY[0] if v else 0.0
-        g_h(v, 0, 0)
-        m_mm(0, 0)
-        open_g(v)
-        g_max(v, 0, 1)
         if v == 0:
             late_constants()
-        act(V("urep"), ind(sm(1), V("ex")), FN.Identity, bias=32.0, scale=0.5)
-        u_op("uc", sm(0))
-        g_h(v, 0, 1)
-        m_mm(0, 1)
-        hl_mm(0)
-        hd_mm(0)
-        dif_open("pA", 512)
-        dif_mm("ec", "uc", "pA", 0, False)
-        g_max(v, 1, 0)
-        act(V("zb"), z, FN.Identity, bias=2047.5)
-        act(V("tab", S(ZO, ZO + K)), z, FN.Copy)
-        g_h(v, 1, 0)
-        m_mm(1, 0)
-        hl_mm(1)
-        hd_mm(1)
-        n0 = len(ops)
-        g_max(v, 1, 1)
-        n1 = len(ops)
-        l_side()
-        if WEAVE:
-            pieces, steps = ops[n0:n1], ops[n1:]
-            for o in steps[:len(pieces)]:
-                o["chain"] = "gm"
-            ops[n0:] = [o for pair in zip(steps, pieces) for o in pair] + steps[len(pieces):]
-        g_h(v, 1, 1)
-        m_mm(1, 1)
-        hg_mm(0)
-        newk_mm()
-        hg_mm(1)
-        u_op("uw", sm(2))
-        e_op("ew", sm(2))
-        e_op("ev", sm(4))
-        g_square()
-        act(V("nk"), V("pC", S(0, 256)), FN.Abs)
-        if not last:
-            cp(V("ls%d" % v), V("nk"))
-            send("ls%d" % v, "l%d" % (v + 1), "al%d" % (v + 1), v + 1)
-            ops[-1]["early"] = 0.0 if v else EARLY[6]
-        w_mm("ev", "pD", 352)
-        w_mm("ew", "pD", 336)
-        dif_mm("ew", "uw", "pA", 256, True)
-        if last:
-            dma("sync", T.yl[:], V("nk"))
-            contest("pA", 2, V("pD", S(320, 352)), col(9))
-            cp(V("o2", S(0, 64, 2)), V("s2", S(32, 64)))
-            scatter_b(0, 16)
             for j in range(4):
-                js = S(512 * j, 512 * j + 512)
-                for i in range(2):
-                    half = S(512 * j + 256 * i, 512 * j + 256 * i + 256)
-                    cp(V("bf", half), V("bt", half))
-                dma("sync", T.yb[:, js], V("bf", js))
-                ops[-1]["early"] = EARLY[3]
-        g_side()
-        e_op("eh", sm(6))
-        halve("h1", "oz", V("zs%d" % v))
+                mov(V("xb", S(BO + 512 * j, BO + 512 * j + 512)), V("bt", S(512 * j, 512 * j + 512)))
         if last:
-            ops[-2]["early"] = EARLY[5]
+            for a in range(0, W, 512):
+                mov(V("xh", S(a, a + 512)), V("xb", S(a, a + 512)), 1024.0, 1 / 64, "act")
+                mov(V("xin", S(a, a + 512)), V("xh", S(a, a + 512)), -1024.0)
+            w_gather(v + 1, 0, V("num"))
+        gather(v, 0, 0)
+        mov(V("urep"), ind(V("qc", S(48, 64)), V("ex")), 32.0, 0.5, "act")
+        u_op("uc", V("qc", S(32, 48)))
+        dif("ec", "uc", 0, "pG", 0)
+        if last:
+            contest(0, 1, V("pD", S(160, 176)))
+            mov(V("o3", S(0, 16)), V("s3", S(0, 16)))
+        side_mm(0, 1)
+        for a, b in cuts(CFG["cut"][0]):
+            x_mm(0, 0, range(16), a, b)
+        gather(v, 1, 1)
+        for j in range(4):
+            g_max(0, 0, j)
+            m_mm(0, 0, j)
+        l_clean()
+        l_rename()
+        for h in (1, 0):
+            open_g(v, h)
+        l_pick()
+        gather(v, 1, 0)
+        side_mm(1, 1)
+        act(V("fp"), ss, FN.Relu, bias=SINK, scale=SINK / 32768)
+        for h in (1, 0):
+            mm(V("pG", h, S(256, 384)), V("idq"), half("lq", h))
+            mm(V("pG", h, S(256, 384)), V("idb"), half("y2", h))
+            join(2)
+        for h in range(2):
+            mm(V("pC", S(128 * h, 128 * h + 128)), half("nw", h), V("idq"), True)
+        join(2)
+        nk = V("nl")
+        act(nk, V("pC", S(0, 256)), FN.Abs)
         if not last:
-            send("zs%d" % v, "z%d" % (v + 1), "az%d" % (v + 1), v + 1)
-            ops[-1]["early"] = EARLY[1]
+            mov(V("ls%d" % v), nk, on="act")
+            send("ls%d" % v, "l%d" % (v + 1), "al%d" % (v + 1), v + 1)
+            early("sendl")
         else:
-            dma("act", T.yz[:], V("zs%d" % v))
-        mm(V("pB", S(0, 392)), V("idb"), V("mbf"), True, False)
-        dif_f()
-        w_mm("eh", "pC", 272)
-        lo_mm()
-        act(V("vf"), V("pL", 0), FN.Copy)
-        cp(V("ov"), V("pD", S(352, 368)))
+            rounds32(V("xb", S(BO, 2 * BO)), "nl", "o3")
+            dma(T.yb[:], BW)
+            dma(T.yl[:], nk)
+        own_mm("ev", 0, "ss", 192, "selv", 16, func=FN.Sign, bias=0.5)
+        mov(V("ov"), V("pD", S(192, 208)), col(10))
+        u_op("uw", wcol)
+        e_op("ew", wcol)
+        name("ew")
+        w_mm("ew", 176)
+        dif("ew", "uw", 384, "pA")
+        px = V("pC", S(256, 512))
+        halve("hx", "gl", "ov", px)
+        halve_mm("hx", v, px, last)
+        if last:
+            mov(V("vxo"), px, -ROUND, 1 / 64, "act")
+        else:
+            mov(V("wq", S(0, 256, 16)), wcol, -16.0, 1 / 64, "act")
+            mm(px, V("idb"), V("cst", S(256, 512)), False, True)
+            for h in range(2):
+                mm(V("pC", S(256 + 128 * h, 384 + 128 * h)), half("wq", h), V("idq"))
+            join(3)
+            mov(vx, px, on="act")
+        if last:
+            contest(384, 1, V("pD", S(176, 192)))
+            mov(V("o3", S(16, 32)), V("s3", S(0, 16)))
+            rounds32(V("xin"), "vxo", "o3", 16)
+            dma(T.yx[:], V("xin", S(0, W)))
+        else:
+            contest(0, 2, V("pD", S(160, 192)))
+            mov(V("o3"), V("s3"))
+            rounds32(V("xb", S(0, BO)), "vx", "o3", 16)
+            rounds32(V("xb", S(BO, 2 * BO)), "nl", "o3")
+            w_gather(v + 1, CFG["wdve"], XW)
+        g_pen(1)
+        for a, b in cuts(CFG["cut"][1]):
+            side_mm(1, 0, a, b)
+        g_pen(0)
+        own_mm("ez", 1, "sg", 208, "sel", 0, scale=-1 / RANK, bias=1040.5 - 2.0 ** -10)
+        mov(V("oz"), V("pD", S(208, 224)), col(20))
+        mov(V("qi"), V("sg", S(15, 512, 16)))
+        ts(V("qj"), V("qi"), 4095, A.bitwise_and)
+        tt(sm(6), V("qj", both, 0), V("qj", both, 1), A.max)
+        tt(sm(7), V("qj", both, 0), V("qj", both, 1), A.min)
+        e_op("eh", sm(6))
+        u_op("uh", sm(6))
+        own_mm("el", 2, "sm", 240)
+        w_mm("eh", 224)
+        mov(V("ol"), V("pD", S(240, 256)))
+        pzz = V("pC", S(0, 256))
+        halve("hz", "gg", "oz", pzz)
+        halve_mm("hz", v, pzz, True)
+        if not last:
+            mov(V("zs%d" % v), pzz, -R64, on="act")
+            send("zs%d" % v, "z%d" % (v + 1), "az%d" % (v + 1), v + 1)
+            early("sendz")
+        else:
+            mov(V("zs%d" % v), pzz, -ROUND, 1 / 64, "act")
+            dma(T.yz[:], V("zs%d" % v))
+        mov(V("vw"), ind(V("num") if last else XW, V("ol")), on="act")
+        dif("eh", "uh", 0, "pA")
+        contest(0, 1, V("pD", S(224, 240)))
+        mov(V("o1"), V("s3", S(0, 16)))
+        rounds32(V("w%d" % ((v + 1) % 2)), "vw")
         if not last:
             count_merges()
-            contest("pA", 2, V("pD", S(320, 352)), col(9))
-            cp(V("o2", S(0, 64, 2)), V("s2", S(32, 64)))
-            ops[-1]["early"] = EARLY[4]
-        halve("h2", "ov", V("vx"))
-        ops[-1]["early"] = EARLY[4]
-        scatter_x()
-        contest_f()
-        scatter_f()
-    dma("act", T.yx[:], XW)
-    fw_mm(False)
-    cp(V("fo"), V("pD", S(0, 128)))
-    dma("sync", T.yf[:], V("fo"))
+            if CFG["ftab"]:
+                mov(V("vf"), ind(V("ipart"), V("ol")), on="act")
+                rounds32(V("ft"), "vf")
+    dma(T.yf[:], V("w%d" % (VISITS % 2), S(0, W), part=S(0, 128, 16)))
 
     def meet(a, b):
         return a[0] == b[0] and a[1] < b[2] and b[1] < a[2]
@@ -672,14 +736,17 @@ def rank_program(g, core, T, topo):
                 ps = SCRATCH[reg[0]][0] == "psum"
                 for j, reg2, wr2 in seen.get(reg[0], []):
                     if j != i and meet(reg, reg2) and not (o.get("apart") and ops[j].get("apart")):
-                        same = ops[j]["eng"] == o["eng"]
+                        same = ops[j]["eng"] == o["eng"] and "alt" not in o and "alt" not in ops[j]
                         if same and o["eng"] == "pe":
-                            pre[i][j] = 0.0
+                            if (wr or wr2) and not (o["adds"] and ops[j]["adds"]):
+                                pre[i][j] = 0.0
+                        elif same and wr and wr2 and not SAME_QUEUE_WAW:
+                            pre[i].setdefault(j, 0.0)
                         elif wr or wr2 or (ps and not same):
                             pre[i][j] = LAT
             for reg, wr in [(r, False) for r in o["r"]] + [(r, True) for r in o["w"]]:
                 old = seen.get(reg[0], [])
-                if wr and not o.get("apart"):
+                if wr and not o.get("apart") and not o.get("adds"):
                     old = [e for e in old if not (reg[1] <= e[1][1] and e[1][2] <= reg[2])]
                 seen[reg[0]] = old + [(i, reg, wr)]
             if o.get("chain"):
@@ -688,67 +755,124 @@ def rank_program(g, core, T, topo):
                 lastq[o["chain"]] = i
             if o["ext"]:
                 pre[i][sends[o["sem"]]] = 0.0
-            elif o["sem"] is not None:
-                if o["eng"] in lastq:
-                    pre[i].setdefault(lastq[o["eng"]], None)
-                lastq[o["eng"]] = i
-                if o["sem"] == "":
-                    sends[o["to"]] = i
+            elif o["sem"] == "":
+                sends[o["to"]] = i
+        steps, count = {}, {}
+        for i, o in enumerate(ops):
+            o["at"] = i
+            if o["ext"] and o["sem"].startswith("al"):
+                count = {}
+            what = tuple([o["eng"]] + [r[0].rstrip("0123") for r in o["w"][:1] + o["r"][:2]])
+            count[what] = count.get(what, 0) + 1
+            o["step"] = steps.setdefault((what, count[what]), len(steps))
+        for i, o in enumerate(ops):
+            for p in o.get("behind", []):
+                pre[i].setdefault(p["at"], 0.0)
         suc = [[] for _ in range(n)]
         for i in range(n):
             for j in pre[i]:
                 suc[j].append(i)
+        hold = [100.0 if o["sem"] == "" else o["cost"] for o in ops]
+        lead = [DMA[0] if o["eng"] == "sync" else 0.0 for o in ops]
+        tail = [DMA[1] if o["eng"] == "sync" else o["cost"] - h for o, h in zip(ops, hold)]
+        gap = [{j: d + tail[j] + lead[i] for j, d in pre[i].items()} for i in range(n)]
+        back = [{k: gap[k][i] for k in suc[i]} for i in range(n)]
+
+        def place(before, after, first, key):
+            left = [len(p) for p in before]
+            at = list(first)
+            ready = sorted(((-key[i], i) for i in range(n) if not left[i]))
+            busy = {e: ([], []) for e in set(eng)}
+            while ready:
+                i = ready.pop()[1]
+                t, h = at[i], hold[i]
+                if h:
+                    starts, ends = busy[eng[i]]
+                    lo, hi = 0, len(ends)
+                    m = hi
+                    while lo < hi:
+                        mid = (lo + hi) // 2
+                        if ends[mid] <= t:
+                            lo = mid + 1
+                        else:
+                            hi = mid
+                    while lo < m and starts[lo] < t + h:
+                        t = ends[lo]
+                        lo += 1
+                    starts.insert(lo, t)
+                    ends.insert(lo, t + h)
+                    at[i] = t
+                new = False
+                for k, d in after[i].items():
+                    if t + h + d > at[k]:
+                        at[k] = t + h + d
+                    left[k] -= 1
+                    if not left[k]:
+                        ready.append((-key[k], k))
+                        new = True
+                if new:
+                    ready.sort()
+            return at
+
+        def there_and_back(key):
+            at = place(gap, back, lead, key)
+            late = place(back, gap, tail, [-(a + h) for a, h in zip(at, hold)])
+            at2 = place(gap, back, lead, [-(a + h) for a, h in zip(late, hold)])
+            return min((max(a + h + t for a, h, t in zip(x, hold, tail)), x) for x in (at, at2)) + (list(eng),)
+
+        def swap(s):
+            for i in either_of[s]:
+                o = ops[i] if eng[i] != ops[i]["eng"] else ops[i]["alt"]
+                eng[i], hold[i] = o["eng"], o["cost"]
+
+        either_of = {}
+        for i, o in enumerate(ops):
+            if "alt" in o:
+                either_of.setdefault(o["step"], []).append(i)
+        free = sorted(either_of)
+
+        eng = [o["eng"] for o in ops]
         rest = [0.0] * n
-        for i in range(n - 1, -1, -1):
-            rest[i] = ops[i]["cost"] + ops[i].get("early", 0.0) + max([0.0] + [rest[k] + (pre[k][i] or 0.0) - (ops[i]["cost"] if pre[k][i] is None else 0.0) for k in suc[i]])
-        left = [len(p) for p in pre]
-        ready_at = [0.0] * n
-        ready = {}
-        for i in range(n):
-            if not left[i]:
-                ready.setdefault(ops[i]["eng"], []).append(i)
-        free, wires, order = {}, [0.0], []
-        while len(order) < n:
-            best = None
-            for e, lst in ready.items():
-                if lst:
-                    t = max(free.get(e, 0.0), min(ready_at[i] for i in lst))
-                    if best is None or t < best[0]:
-                        best = (t, e)
-            t, e = best
-            wait = None
-            for now in sorted((i for i in ready[e] if ready_at[i] <= t), key=lambda i: (-rest[i], i)):
-                soon = [i for i in ready[e] if t < ready_at[i] < t + min(HOLD * ops[now]["cost"], 600.0)
-                        and rest[i] > rest[now] + AHEAD and e != "ext"]
-                if not soon:
-                    break
-                wait = wait or soon
+        at = place(gap, back, [0.0] * n, list(range(n)))
+        for i in sorted(range(n), key=lambda i: (-at[i], -i)):
+            rest[i] = hold[i] + max([tail[i]] + [rest[k] + d for k, d in back[i].items()])
+        best = now = there_and_back([-r for r in rest])
+        rng = np.random.RandomState(0)
+        step = np.array([o["step"] for o in ops])
+        for _ in range(PASSES):
+            at = np.array(now[1])
+            if rng.rand() < 0.5:
+                shake = rng.randn(n) * (abs(at - rng.rand() * now[0]) < SHAKE[1])
             else:
-                now = max(wait, key=lambda i: rest[i])
-                t = ready_at[now]
-            ready[e].remove(now)
-            order.append(now)
-            o = ops[now]
-            if o["sem"] is None or o["ext"]:
-                end = t + o["cost"]
-                free[e] = end if not o["ext"] else 0.0
-            else:
-                free[e] = t + 100.0
-                if o["sem"]:
-                    wires[0] = max(wires[0], t + 1000.0) + o["cost"] - 2000.0
-                    end = wires[0] + 1000.0
-                else:
-                    end = t + o["cost"]
-            for k in suc[now]:
-                ready_at[k] = max(ready_at[k], t if pre[k][now] is None else end + pre[k][now])
-                left[k] -= 1
-                if not left[k]:
-                    ready.setdefault(ops[k]["eng"], []).append(k)
-        return order
+                shake = (rng.randn(n) * (rng.rand(n) < SHAKE[2]))[step]
+            other = free[rng.randint(len(free))] if rng.rand() < SHAKE[4] else None
+            if other is not None:
+                swap(other)
+                shake = shake * (rng.rand() < 0.5)
+            got = there_and_back((at + SHAKE[0] * shake).tolist())
+            if got[0] <= now[0] - SHAKE[3] * np.log(rng.rand()):
+                now = got
+                best = min(best, now)
+            elif other is not None:
+                swap(other)
+        MEMO["span"] = best[0]
+        return sorted(range(n), key=lambda i: (best[1][i], i)), best[2]
 
     if "order" not in MEMO:
         MEMO["order"] = arrange(ops)
-    ops = [ops[i] for i in MEMO["order"]]
+    for o, e in zip(ops, MEMO["order"][1]):
+        if e != o["eng"]:
+            o.update(o["alt"])
+    ops = [ops[i] for i in MEMO["order"][0]]
+
+    lastmm = {}
+    for o in ops:
+        for reg in o["r"] + (o["w"] if o.get("start", True) else []):
+            for bank, end in lastmm.items():
+                if meet(reg, bank):
+                    end[0] = True
+        if "end" in o:
+            lastmm[o["w"][0]] = o["end"]
 
     hist = {}
     for i, o in enumerate(ops):
@@ -762,7 +886,7 @@ def rank_program(g, core, T, topo):
                 p = ops[j]
                 same = own and p["sem"] is None and p["eng"] == o["eng"]
                 if same:
-                    need = o["eng"] != "pe" and ((wr2 and not wr) or (SAME_QUEUE_WAW and (wr or wr2)))
+                    need = o["eng"] != "pe" and (wr != wr2 or (SAME_QUEUE_WAW and wr))
                 else:
                     need = wr or wr2 or ps
                 if need and j != i:

@@ -24,7 +24,7 @@ def _sb(dtype, **kw):
 _sb(BF16, ft=WW + 8, ipart=W, ilo=W, vf=K, xin=BO, i512=1024, vxo=256, fl=256, zin=K,
     z0=K, z1=K, z2=K, z3=K, zs0=K, zs1=K, zs2=K, zs3=K, y2=256, fp=256, cst=512,
     ones=128, idb=128, idn=128, idh=128, i64=128, dq=128, rz=256, r8=16, pen=(2, 256), selz=144, rst=384, sd=384, pr=768,
-    ol1=512, ol2=128, og1=512, og2=384, sgn=32, a15=256, blkn=128, cu=32, cb=32)
+    ol1=512, ol2=256, og1=256, og2=384, sgn=32, a15=128, blkn=128, cu=32, cb=32)
 _sb(F32, xb=2 * BO, w0=WW, w1=WW, gl=2 * HW, gg=2 * HW, nl=256, vx=256, vw=256, ident=128, blk=128, maske=256,
     rl=16, rg=24, rs2=256, stp=256, ck=256, cols=32, tf=256, urep=256, kf=256, ss=264, num=W, sel0=144, g8=8,
     sg=520, gq=256, y1=256, sq=256, sm=136, s3=32, s4=32)
@@ -37,10 +37,12 @@ _sb(F16, ri=192, lq=256, wq=256, uw=256, uh=256, uc=256, gm=8192, nw=256, idq=12
 SEMAPHORES = (["pe", "dve", "act", "pool", "sent"] + ["d%d" % i for i in range(24)]
               + ["al%d" % i for i in range(1, VISITS)] + ["az%d" % i for i in range(1, VISITS)])
 SAME_QUEUE_WAW = True
-LAT, PASSES, SHAKE = 170.0, 6000, (1000.0, 3000.0, 0.05, 60.0, 0.3)
+LAT, PASSES, SHAKE = 150.0, 13000, (1000.0, 1000.0, 0.015, 200.0, 0.3)
 DMA = (1300.0, 700.0, 100.0, 200.0)
-RATE = (0.85, 40.0, 1.25, 2.6)
-CFG = {"gp": (64, 32, 32, 32), "gdve": (64, 0, 0, 0), "cut": (128, 128), "wp": 512, "wdve": 1024, "w0dve": 1024, "pur": "dve", "pen": ("act", "dve"), "gq": ("act", "act"), "early": {}, "first": (), "ftab": True}
+RATE = (0.9, 35.0, 1.25, 2.6, 10.0, 4500.0)
+OTHER = ({"plain": 1.15, "pe": 1.25, "gather": 0.8, "scatter": 0.7, "wait": 0.6, "remote": 0.8},
+         {"plain": 0.95, "pe": 1.0, "gather": 1.3, "scatter": 1.5, "wait": 1.5, "remote": 1.5})
+CFG = {"gp": (64, 64, 64, 32), "gdve": (64, 0, 0, 0), "cut": (128, 128), "wp": 512, "wdve": 1024, "w0dve": 1024, "pur": "dve", "pen": ("dve", "dve"), "gq": ("act", "act"), "early": {}, "first": (), "ftab": True}
 MEMO = {}
 A = AluOpType
 FN = ActivationFunctionType
@@ -91,25 +93,26 @@ def rank_program(g, core, T, topo):
         if ext:
             cost = 0.0
         elif sem == "":
-            cost = 4000.0
+            cost = RATE[5]
         elif sem is not None:
             cost = DMA[2] + sides[0]["n"] * sides[0]["rows"] * sides[0]["size"] / DMA[3]
         elif eng == "pe":
-            cost = 8.0 + max(min(64, ins[0]["n"]), ins[1]["n"]) * (4 if ins[1]["size"] == 4 else 1) * RATE[0] / 2
+            cost = RATE[4] + max(min(64, ins[0]["n"]), ins[1]["n"]) * (4 if ins[1]["size"] == 4 else 1) * RATE[0] / 2
         elif eng == "pool":
             cost = 170.0 + 2 * n * RATE[0]
         elif outs[0]["also"]:
             cost = 50.0 + RATE[3] * n
         elif any(x["also"] for x in sides):
-            cost = 55.0 + RATE[2] * n
+            cost = (65.0 if eng == "act" else 50.0) + RATE[2] * n
         else:
             full = [x for x in ins if isinstance(x, dict) and x["n"] == n]
             if eng == "dve" and all(x["size"] == 2 for x in outs + full):
                 n = n / 2
             if two and SCRATCH[full[0]["reg"][0][0]][0] == SCRATCH[full[1]["reg"][0][0]][0]:
                 n = 2 * n
-            cost = RATE[1] + max(64, n) * RATE[0]
-        ops.append({"eng": eng, "fn": fn, "w": w, "r": r, "sem": sem, "count": count, "ext": ext, "cost": cost, "to": to})
+            cost = RATE[1] + (15.0 if eng == "act" else 0.0) + max(64, n) * RATE[0]
+        kind = "dma" if sem is not None else "pe" if eng == "pe" else "scatter" if outs[0]["also"] else "gather" if any(x["also"] for x in sides) else "plain"
+        ops.append({"eng": eng, "fn": fn, "w": w, "r": r, "sem": sem, "count": count, "ext": ext, "cost": cost, "to": to, "kind": kind})
 
     def ap(x):
         return x["ap"] if isinstance(x, dict) else x
@@ -198,7 +201,7 @@ def rank_program(g, core, T, topo):
                 named[b].setdefault("behind", []).append(named[a])
 
     def lin(o, a, scale, bias=0.0):
-        act(o, a, FN.Identity, bias=bias, scale=scale)
+        mov(o, a, bias, scale, "act")
 
     def either(first, second):
         first()
@@ -213,7 +216,7 @@ def rank_program(g, core, T, topo):
             d = lambda: ts(o, a, bias, A.add)
         else:
             d = lambda: cp(o, a)
-        s = lambda: lin(o, a, scale, bias)
+        s = lambda: act(o, a, FN.Identity, bias, scale)
         either(*((d, s) if on == "dve" else (s, d)))
 
     def fill(o, c):
@@ -287,14 +290,18 @@ def rank_program(g, core, T, topo):
     ts(V("ti", S(3, 4)), V("ti", S(0, 1)), 8064, A.bitwise_and)
     cp(V("cols", S(12, 14)), V("ti", S(2, 4)))
     ts(col(12), col(12), 0.5, A.add)
+    swap = V("gq", S(0, 128))
+    asel(swap, V("ones"), [[-2, 64], [1, 2]], A.is_equal, 0.0, -1, 1)
+    mm(V("pD", S(256, 258)), swap, V("cols", S(12, 14)), True)
+    ts(V("ol2", S(0, 128)), swap, V("pD", S(256, 257)), A.mult, -BIG, A.mult)
+    ts(V("ol2", S(128, 256)), V("ident"), col(13), A.mult, -BIG, A.mult)
+    tt(V("ol1", S(0, 128)), V("ol2", S(0, 128)), V("ol2", S(128, 256)), A.add)
+    lin(V("ol1", S(256, 384)), V("ol1", S(0, 128)), 1.0)
     for h in range(2):
-        ts(V("ol1", S(256 * h, 256 * h + 128)), V("ident"), col(13), A.mult, -BIG, A.mult)
         lin(V("ol1", S(256 * h + 128, 256 * h + 256)), V("ident"), -1024.0)
-    ts(V("ol2"), V("ident"), col(12), A.mult, -BIG, A.mult)
     lin(V("og2", S(256, 384)), V("ol1", S(0, 128)), -1.0)
     lin(V("og2", S(0, 128)), V("ident"), 1024.0)
     lin(V("og2", S(128, 256)), V("ident"), 1024.0)
-    lin(V("og1", S(256, 384)), V("ol2"), -1.0)
     lin(V("og1", S(0, 128)), V("ident"), col(11))
     lin(V("og1", S(128, 256)), V("ident"), col(11))
     lin(V("idn"), V("ident"), -1.0)
@@ -304,14 +311,17 @@ def rank_program(g, core, T, topo):
         cp(V("idq"), V("ident"))
         lin(V("ck"), kk, 613.0 * 32)
         lin(V("idh"), V("ident"), 0.5)
-        fill(V("tf", S(0, 192)), 1)
-        asel(V("y1", S(0, 192)), V("tf", S(0, 192)), [[-32, 4], [-16, 3], [1, 16]], A.is_equal, 0.0, -15, 1)
-        asel(V("sq", S(0, 192)), V("tf", S(0, 192)), [[-32, 4], [-16, 3], [1, 16]], A.is_equal, 0.0, 17, 1)
-        for j in range(4):
-            lin(V("ri", S(48 * j, 48 * j + 32)), V("y1", S(48 * j, 48 * j + 32)), 1.0)
-            lin(V("ri", S(48 * j + 32, 48 * j + 48)), V("sq", S(48 * j + 32, 48 * j + 48)), 1.0)
-            lin(V("re_", S(48 * j, 48 * j + 32)), V("blk", S(32 * j, 32 * j + 32)), -1.0)
-            lin(V("re_", S(48 * j + 32, 48 * j + 48)), V("blk", S(32 * j + 16, 32 * j + 32)), -1.0)
+        t0, t1 = V("tf", S(0, 192)), V("y1", S(0, 192))
+        iota(t0, [[0, 4], [1, 3], [0, 16]], 0, 0)
+        ts(t0, t0, 1.5, A.is_gt)
+        iota(t1, [[32, 4], [16, 3], [-1, 16]], 15, -1)
+        ts(V("sq", S(0, 192)), t0, 32.0, A.mult)
+        tt(V("ri"), t1, V("sq", S(0, 192)), A.is_equal)
+        iota(t1, [[2, 4], [1, 3], [0, 16]], 0, 0)
+        tt(t1, t1, t0, A.subtract)
+        ts(V("ib", S(3, 4)), V("ia", S(0, 1)), 4, A.arith_shift_right)
+        cp(col(27), V("ib", S(3, 4)))
+        ts(V("re_"), t1, col(27), A.is_equal, -1.0, A.mult)
         iota(V("pr", S(0, 384)), [[0, 24], [-1, 16]], 15, 0)
         ts(V("rst"), V("pr", S(0, 384)), col(0), A.is_equal, 4096.0, A.mult)
         asel(V("rst"), V("rst"), [[0, 8], [1, 3], [0, 16]], A.not_equal, 0.0, -2, 0)
@@ -334,7 +344,6 @@ def rank_program(g, core, T, topo):
         lin(V("sel", S(112, 128)), V("maske", S(0, 16)), 1.0)
         lin(V("selv"), V("sel"), col(21))
         ts(V("ib", S(2, 3)), V("ia", S(0, 1)), 7, A.bitwise_and)
-        ts(V("ib", S(3, 4)), V("ia", S(0, 1)), 4, A.arith_shift_right)
         ts(V("ib", S(4, 5)), V("ia", S(0, 1)), 3, A.arith_shift_right, 1, A.bitwise_and)
         tt(col(24), V("ib", S(2, 3)), V("ib", S(3, 4)), A.is_equal)
         cp(col(25), V("ib", S(4, 5)))
@@ -345,8 +354,6 @@ def rank_program(g, core, T, topo):
         lin(V("ss", S(256, 264)), blk8, 0.0, -0.5)
         lin(V("sg", S(512, 520)), blk8, 0.0)
         lin(V("sm", S(128, 136)), blk8, 0.0)
-        lin(V("sel0"), V("kf", S(0, 144)), 0.0)
-        lin(V("sel0", S(15, 143, 16)), blk8, col(8))
         lin(col(23), col(7), 2.0, W + 2 - RANK)
         fill(V("rs2"), 2 ** 23)
         lin(V("rs2"), V("rs2"), 4.0)
@@ -444,22 +451,17 @@ def rank_program(g, core, T, topo):
         d = [V("pL", h, S(0, 128)) for h in range(2)]
         mm(V("pL"), V("ones"), V("ol1"), True)
         for h in range(2):
-            mm(d[h], V("ones"), V("ol2"))
-        join(3)
-        for h in range(2):
             mm(d[h], half("z%d" % v, h), V("rz", S(0, 128)))
         join(2)
         if v > 0:
             for h in range(2):
-                for i in range(2):
-                    mm(d[h], V("a15", S(128 * i, 128 * i + 128), part=S(0, 8)), V("blkn", part=S(0, 8)))
-            join(4)
+                mm(d[h], V("a15", part=S(0, 8)), V("blkn", part=S(0, 8)))
+            join(2)
 
     def open_g(v, h):
         mm(V("pG", h, S(128, 512)), V("ones"), V("og2"), True)
-        mm(V("pG", h, S(384, 512)), V("ones"), V("og1", S(256, 384)))
         mm(V("pG", h, S(384, 512)), half("z%d" % v, h), V("rz", S(128, 256)))
-        join(3)
+        join(2)
 
     def gather(v, side, h):
         n = CFG["gp"][2 * side + 1 - h]
@@ -576,9 +578,9 @@ def rank_program(g, core, T, topo):
         for h in range(2):
             mm(ps, V("sgn", S(16 * h, 16 * h + 8)), V("ones"), h == 0)
         join(2)
-        mov(y, ps, 8 - 15 / 32, 1 / 32, "act")
-        mov(V("a15", S(0, 128), part=S(0, 8)), ps, 128.0, 0.5, "act")
-        mov(V("a15", S(128, 256), part=S(0, 8)), y, 0.0, -16.0, "act")
+        mov(y, ps, 128.0, 0.5, "act")
+        ts(y, y, 15, A.bitwise_and)
+        mov(V("a15", part=S(0, 8)), y, on="act")
 
     def contest(o, n, places):
         for i, c in ((0, 15), (1, 47)):
@@ -612,7 +614,7 @@ def rank_program(g, core, T, topo):
         if v == 0:
             late_constants()
             for j in range(4):
-                mov(V("xb", S(BO + 512 * j, BO + 512 * j + 512)), V("bt", S(512 * j, 512 * j + 512)))
+                asel(V("xb", S(BO + 512 * j, BO + 512 * j + 512)), V("bt", S(512 * j, 512 * j + 512)), [[0, 512]], A.is_ge, 0.0, 0, 0)
         if last:
             for a in range(0, W, 512):
                 mov(V("xh", S(a, a + 512)), V("xb", S(a, a + 512)), 1024.0, 1 / 64, "act")
@@ -647,10 +649,9 @@ def rank_program(g, core, T, topo):
         for h in range(2):
             mm(V("pC", S(128 * h, 128 * h + 128)), half("nw", h), V("idq"), True)
         join(2)
-        nk = V("nl")
+        nk = V("nl" if last else "ls%d" % v)
         act(nk, V("pC", S(0, 256)), FN.Abs)
         if not last:
-            mov(V("ls%d" % v), nk, on="act")
             send("ls%d" % v, "l%d" % (v + 1), "al%d" % (v + 1), v + 1)
             early("sendl")
         else:
@@ -685,7 +686,7 @@ def rank_program(g, core, T, topo):
             contest(0, 2, V("pD", S(160, 192)))
             mov(V("o3"), V("s3"))
             rounds32(V("xb", S(0, BO)), "vx", "o3", 16)
-            rounds32(V("xb", S(BO, 2 * BO)), "nl", "o3")
+            rounds32(V("xb", S(BO, 2 * BO)), "ls%d" % v, "o3")
             w_gather(v + 1, CFG["wdve"], XW)
         g_pen(1)
         for a, b in cuts(CFG["cut"][1]):
@@ -815,10 +816,36 @@ def rank_program(g, core, T, topo):
             return at
 
         def there_and_back(key):
-            at = place(gap, back, lead, key)
-            late = place(back, gap, tail, [-(a + h) for a, h in zip(at, hold)])
-            at2 = place(gap, back, lead, [-(a + h) for a, h in zip(late, hold)])
-            return min((max(a + h + t for a, h, t in zip(x, hold, tail)), x) for x in (at, at2)) + (list(eng),)
+            late = place(back, gap, tail, [-(a + h) for a, h in zip(key, hold)])
+            at = place(gap, back, lead, [-(a + h) for a, h in zip(late, hold)])
+            span = max(a + h + t for a, h, t in zip(at, hold, tail))
+            if span < limit[0]:
+                order = sorted(range(n), key=lambda i: at[i])
+                limit[1] = span
+                span = (span + sum(replay(order, *m) for m in others)) / (1 + len(others))
+            else:
+                span = 1e9
+            return span, at, list(eng)
+
+        def replay(order, times, gaps, tails):
+            end, busy, last = [0.0] * n, {e: 0.0 for e in set(eng)}, 0.0
+            for i in order:
+                t = busy[eng[i]] if hold[i] else 0.0
+                for j, d in gaps[i]:
+                    if end[j] + d > t:
+                        t = end[j] + d
+                t = max(t, lead[i]) + hold[i] * times[i]
+                end[i] = t
+                if hold[i]:
+                    busy[eng[i]] = t
+                last = max(last, t + tails[i])
+            return last
+
+        others, limit = [], [1e9, 0.0]
+        for m in OTHER:
+            tails = [t * m["remote"] if o["sem"] == "" else t for o, t in zip(ops, tail)]
+            others.append(([m.get(o["kind"], 1.0) for o in ops],
+                           [[(j, d * m["wait"] + tails[j] + lead[i]) for j, d in pre[i].items()] for i in range(n)], tails))
 
         def swap(s):
             for i in either_of[s]:
@@ -829,17 +856,18 @@ def rank_program(g, core, T, topo):
         for i, o in enumerate(ops):
             if "alt" in o:
                 either_of.setdefault(o["step"], []).append(i)
-        free = sorted(either_of)
+        free = [s for s in sorted(either_of) for _ in either_of[s]]
 
         eng = [o["eng"] for o in ops]
         rest = [0.0] * n
         at = place(gap, back, [0.0] * n, list(range(n)))
         for i in sorted(range(n), key=lambda i: (-at[i], -i)):
             rest[i] = hold[i] + max([tail[i]] + [rest[k] + d for k, d in back[i].items()])
-        best = now = there_and_back([-r for r in rest])
+        best = now = there_and_back(place(gap, back, lead, [-r for r in rest]))
         rng = np.random.RandomState(0)
         step = np.array([o["step"] for o in ops])
-        for _ in range(PASSES):
+        for k in range(PASSES):
+            warm = SHAKE[3] * (1 - k / PASSES)
             at = np.array(now[1])
             if rng.rand() < 0.5:
                 shake = rng.randn(n) * (abs(at - rng.rand() * now[0]) < SHAKE[1])
@@ -850,9 +878,10 @@ def rank_program(g, core, T, topo):
                 swap(other)
                 shake = shake * (rng.rand() < 0.5)
             got = there_and_back((at + SHAKE[0] * shake).tolist())
-            if got[0] <= now[0] - SHAKE[3] * np.log(rng.rand()):
+            if got[0] <= now[0] - warm * np.log(rng.rand()):
                 now = got
                 best = min(best, now)
+                limit[0] = limit[1] + 4 * warm + 300.0
             elif other is not None:
                 swap(other)
         MEMO["span"] = best[0]

import numpy as np
from concourse.bass import DstId, RemoteDMATransfer
from concourse.mybir import dt, AluOpType, AxisListType, ActivationFunctionType

W, K, VISITS = 2048, 256, 4
BIG = float(2 ** 20)
ROUND = 1.5 * 2 ** 23
R64, R4096 = 64 * ROUND, 4096 * ROUND
RANK, SINK = float(2 ** 20), float(2 ** 33)
BO, WW, HW = W + 72, W + 72, W + 256
F32, BF16, I32, U16, F16 = "float32", "bfloat16", "int32", "uint16", "float16"

SCRATCH = {
    "pz": ("psum", [128, 2, 512], F32), "pL": ("psum", [128, 2, 256], F32), "pG": ("psum", [128, 2, 512], F32),
    "pA": ("psum", [128, 512], F32), "pC": ("psum", [128, 512], F32), "pD": ("psum", [128, 512], F32),
}


def _sb(dtype, **kw):
    for n, s in kw.items():
        SCRATCH[n] = ("sbuf", [128] + (list(s) if isinstance(s, tuple) else [s]), dtype)


_sb(BF16, ft=WW + 8, ipart=W, ilo=W, vf=K, xin=BO, i512=1024, vxo=256, fl=256, zin=K,
    z0=K, z1=K, z2=K, z3=K, zs0=K, zs1=K, zs2=K, zs3=K, y2=256, fp=256, cst=512,
    ones=128, idb=128, idn=128, idh=128, i64=128, dq=128, rz=256, r8=16, pen=(2, 256), selz=144, rst=384, sd=384, pr=768,
    ol1=512, ol2=256, og1=256, og2=384, sgn=32, a15=128, blkn=128, cu=32, cb=32)
_sb(F32, xb=2 * BO, w0=WW, w1=WW, gl=2 * HW, gg=2 * HW, nl=256, vx=256, vw=256, ident=128, blk=128, maske=256,
    rl=16, rg=24, rs2=256, stp=256, ck=256, cols=32, tf=256, urep=256, kf=256, ss=264, num=W, sel0=144, g8=8,
    sg=520, gq=256, y1=256, sq=256, sm=136, s3=32, s4=32)
_sb(I32, bt=W, fi2=128, li=K, ti=8, ia=256, ib=256, rr=256, qi=32, qc=96, qa=128, qj=(2, 2, 8))
_sb(U16, l0=K, l1=K, l2=K, l3=K, ls0=K, ls1=K, ls2=K, fw16=128, bc=K, o1=16, o3=32, lists=80, own=24)
LISTS = ("ex", "oc", "oz", "ov", "ol")
_sb(F16, ri=192, lq=256, wq=256, uw=256, uh=256, uc=256, gm=8192, nw=256, idq=128, idf=128, ec=256, ew=256, ev=128, eh=256, el=128, ez=128, rm=16, re_=192, rw=8,
    sel=240, selv=240, hx=K, hz=K, xh=W)

SEMAPHORES = (["pe", "dve", "act", "pool", "sent"] + ["d%d" % i for i in range(24)]
              + ["al%d" % i for i in range(1, VISITS)] + ["az%d" % i for i in range(1, VISITS)])
SAME_QUEUE_WAW = True
LAT, PASSES, SHAKE = 150.0, 13000, (1000.0, 1000.0, 0.015, 200.0, 0.3)
DMA = (1300.0, 700.0, 100.0, 200.0)
RATE = (0.9, 35.0, 1.25, 2.6, 10.0, 4500.0)
OTHER = ({"plain": 1.15, "pe": 1.25, "gather": 0.8, "scatter": 0.7, "wait": 0.6, "remote": 0.8},
         {"plain": 0.95, "pe": 1.0, "gather": 1.3, "scatter": 1.5, "wait": 1.5, "remote": 1.5})
CFG = {"gp": (64, 64, 64, 32), "gdve": (64, 0, 0, 0), "cut": (128, 128), "wp": 512, "wdve": 1024, "w0dve": 1024, "pur": "dve", "pen": ("dve", "dve"), "gq": ("act", "act"), "early": {}, "first": (), "ftab": True}
MEMO = {}
A = AluOpType
FN = ActivationFunctionType


def rank_program(g, core, T, topo):
    rank = T.rank_of(core)
    if rank is None:
        return
    n_ranks = len(T.cores)
    ops = []
    ndma = [0]

    def V(name, *idx, part=slice(None)):
        if name in LISTS:
            return V("lists", slice(16 * LISTS.index(name), 16 * LISTS.index(name) + 16))
        shape = SCRATCH[name][1][1:]
        full = list(idx) + [slice(None)] * (len(shape) - len(idx))
        lo = hi = 0
        stride = n = 1
        for d in range(len(shape) - 1, -1, -1):
            r = range(shape[d])[full[d]]
            if isinstance(r, int):
                lo += r * stride; hi += r * stride
            else:
                lo += r[0] * stride; hi += r[-1] * stride; n *= len(r)
            stride *= shape[d]
        if SCRATCH[name][0] == "psum":
            lo, hi = lo // 512 * 512, hi // 512 * 512 + 511
        return {"ap": T[name][(part,) + tuple(full)], "reg": [(name, lo, hi + 1)], "also": [], "n": n,
                "rows": len(range(128)[part]), "size": 4 if SCRATCH[name][2] in (F32, I32) else 2}

    def S(a, b, s=1):
        return slice(a, b, s)

    def ind(win, off):
        return dict(win, ap=win["ap"].indirect(off["ap"]), also=off["reg"], n=16 * off["n"])

    def rec(eng, fn, outs, ins, sem=None, count=1, ext=False, two=False, to=None):
        w, r = [], []
        for o in outs:
            w += o["reg"]; r += o["also"]
        for i in ins:
            if isinstance(i, dict):
                r += i["reg"] + i["also"]
        sides = [x for x in outs + ins if isinstance(x, dict)]
        n = max([x["n"] for x in outs] + [0])
        if ext:
            cost = 0.0
        elif sem == "":
            cost = RATE[5]
        elif sem is not None:
            cost = DMA[2] + sides[0]["n"] * sides[0]["rows"] * sides[0]["size"] / DMA[3]
        elif eng == "pe":
            cost = RATE[4] + max(min(64, ins[0]["n"]), ins[1]["n"]) * (4 if ins[1]["size"] == 4 else 1) * RATE[0] / 2
        elif eng == "pool":
            cost = 170.0 + 2 * n * RATE[0]
        elif outs[0]["also"]:
            cost = 50.0 + RATE[3] * n
        elif any(x["also"] for x in sides):
            cost = (65.0 if eng == "act" else 50.0) + RATE[2] * n
        else:
            full = [x for x in ins if isinstance(x, dict) and x["n"] == n]
            if eng == "dve" and all(x["size"] == 2 for x in outs + full):
                n = n / 2
            if two and SCRATCH[full[0]["reg"][0][0]][0] == SCRATCH[full[1]["reg"][0][0]][0]:
                n = 2 * n
            cost = RATE[1] + (15.0 if eng == "act" else 0.0) + max(64, n) * RATE[0]
        kind = "dma" if sem is not None else "pe" if eng == "pe" else "scatter" if outs[0]["also"] else "gather" if any(x["also"] for x in sides) else "plain"
        ops.append({"eng": eng, "fn": fn, "w": w, "r": r, "sem": sem, "count": count, "ext": ext, "cost": cost, "to": to, "kind": kind})

    def ap(x):
        return x["ap"] if isinstance(x, dict) else x

    def tt(o, a, b, op):
        rec("dve", lambda: g.vector.tensor_tensor(ap(o), ap(a), ap(b), op), [o], [a, b], two=True)

    def ts(o, a, s1, op0, s2=None, op1=None):
        if op1 is None:
            rec("dve", lambda: g.vector.tensor_scalar(ap(o), ap(a), ap(s1), None, op0), [o], [a, s1])
        else:
            rec("dve", lambda: g.vector.tensor_scalar(ap(o), ap(a), ap(s1), ap(s2), op0, op1), [o], [a, s1, s2])

    def cp(o, a):
        rec("dve", lambda: g.vector.tensor_copy(ap(o), ap(a)), [o], [a])

    def ms(o, c):
        rec("dve", lambda: g.vector.memset(ap(o), c), [o], [])

    def scan(o, d0, d1, init, op0, op1):
        rec("dve", lambda: g.vector.tensor_tensor_scan(ap(o), ap(d0), ap(d1), init, op0, op1), [o], [d0, d1])

    def act(o, a, func=FN.Identity, bias=0.0, scale=1.0):
        rec("act", lambda: g.scalar.activation(ap(o), ap(a), func, bias=ap(bias), scale=ap(scale)), [o], [a, bias, scale])

    def mm(o, l, r, start=False, strict=False):
        end = [False]
        rec("pe", lambda: g.tensor.matmul(ap(o), ap(l), ap(r), start, end[0]), [o], [l, r])
        ops[-1].update(end=end, start=start, adds=not (start or strict))

    def join(k):
        part = ops[-k:]
        del ops[-k:]
        for a, b in zip(part, part[1:]):
            a["end"][0] = b["start"]
        ops.append(dict(part[-1], fn=lambda: [o["fn"]() for o in part][-1], r=[x for o in part for x in o["r"]],
                        cost=sum(o["cost"] for o in part), start=part[0]["start"], adds=all(o["adds"] for o in part)))

    def iota(o, pat, base, cm):
        small = SCRATCH[o["reg"][0][0]][2] != I32
        if small:
            rec("pool", lambda: g.iota(ap(o), pat, base, cm, allow_small_or_imprecise_dtypes=True), [o], [])
        else:
            rec("pool", lambda: g.iota(ap(o), pat, base, cm), [o], [])

    def asel(o, a, pat, op, fill, base, cm):
        rec("pool", lambda: g.affine_select(ap(o), ap(a), pat, op, fill, base, cm), [o], [a])

    def dma(o, a):
        sem = "d%d" % ndma[0]
        ndma[0] += 1
        rec("sync", lambda: g.sync.dma_start(ap(o), ap(a)), [o] if isinstance(o, dict) else [], [a], sem=sem, count=16)

    def lanes_mask(src, dst):
        eng = [e for e in topo.engines(src, dst) if all(e in topo.engines(src, c) for c in T.cores if c != src)]
        return sum(1 << e for e in eng), len(eng)

    nsent = [0]

    def send(src, land, sem, v):
        s = 1 + (v - 1) % (n_ranks - 1)
        dst = T.cores[(rank + s) % n_ranks]
        rid, pid, _ = topo.addr(dst)
        mask, n = lanes_mask(core, dst)
        nsent[0] += n
        rec("pool", lambda: g.remote_dma(T[land][:], T[src][:], T.sem[sem], T.sem.sent, pid, rid, mask), [], [V(src)], sem="", to=sem)

    def arrive(land, sem, v):
        s = 1 + (v - 1) % (n_ranks - 1)
        n = lanes_mask(T.cores[(rank - s) % n_ranks], core)[1]
        rec("ext", None, [V(land)], [], sem=sem, count=n, ext=True)

    def early(name, n=1):
        for o in ops[-n:]:
            o["early"] = CFG["early"].get(name, 0.0)

    def chain(name):
        ops[-1]["chain"] = name

    named = {}

    def name(n):
        named[n] = ops[-1]
        for a, b in CFG["first"]:
            if n in (a, b) and a in named and b in named:
                named[b].setdefault("behind", []).append(named[a])

    def lin(o, a, scale, bias=0.0):
        mov(o, a, bias, scale, "act")

    def either(first, second):
        first()
        second()
        b = ops.pop()
        ops[-1]["alt"] = {k: b[k] for k in ("eng", "fn", "cost")}

    def mov(o, a, bias=0.0, scale=1.0, on="dve"):
        if scale != 1.0:
            d = lambda: ts(o, a, scale, A.mult, bias, A.add)
        elif isinstance(bias, dict) or bias:
            d = lambda: ts(o, a, bias, A.add)
        else:
            d = lambda: cp(o, a)
        s = lambda: act(o, a, FN.Identity, bias, scale)
        either(*((d, s) if on == "dve" else (s, d)))

    def fill(o, c):
        iota(o, [[0, o["n"]]], c, 0)

    col = lambda i: V("cols", S(i, i + 1))
    sm = lambda i, n=1: V("sm", S(16 * i, 16 * (i + n)))
    both = S(0, 2)
    half = lambda name, h: V(name, S(128 * h, 128 * h + 128))

    dma(V("fi2"), T.fw[:])
    for a in (0, W // 2):
        dma(V("xin", S(a, a + W // 2)), T.x[:, a:a + W // 2])
    dma(V("zin"), T.zz[:])
    dma(V("li"), T.la[:])
    dma(V("ti", S(0, 1)), T.th[:])
    ms(V("ft", S(0, W)), 0.0)

    iota(V("ia", S(0, 1)), [[0, 1]], 0, 1)
    ms(V("ident"), 1.0)
    ms(V("ones"), 1.0)
    asel(V("blk"), V("ident"), [[-16, 8], [0, 16]], A.is_ge, 0.0, 0, 1)
    asel(V("blk"), V("blk"), [[16, 8], [0, 16]], A.is_ge, 0.0, 15, -1)
    asel(V("ident"), V("ident"), [[-1, 128]], A.is_equal, 0.0, 0, 1)
    iota(V("i512", S(0, 512)), [[16, 32], [0, 16]], 0, 0)
    iota(V("i512", S(512, 1024)), [[0, 32], [1, 16]], 0, 0)
    cp(V("fl", S(128, 256)), V("fi2"))
    tt(V("fl", S(0, 128)), V("fi2"), V("fl", S(128, 256)), A.subtract)
    dma(V("ft", S(0, W), part=S(8, 128, 16)), V("fl", S(0, 128)))
    dma(V("ft", S(0, W), part=S(9, 128, 16)), V("fl", S(128, 256)))
    ops[-1]["apart"] = ops[-2]["apart"] = True
    dma(V("bt"), T.bk[:])
    ts(V("ib", S(0, 1)), V("ia", S(0, 1)), 15, A.bitwise_and)
    cp(col(0), V("ib", S(0, 1)))
    ts(col(1), col(0), 0.0, A.is_equal)
    ts(col(2), col(0), 7.5, A.is_gt)
    ts(col(3), col(0), 9.5, A.is_lt)
    tt(col(2), col(2), col(3), A.mult)
    blk8 = V("blk", S(0, 128, 16))
    ms(V("selz"), 0.0)
    ts(V("selz", S(15, 143, 16)), blk8, col(2), A.mult)
    ts(V("dq"), V("ident"), col(1), A.mult, 1 / 64, A.mult)
    lin(V("i64"), V("ident"), 64.0)
    for j in range(4):
        lin(col(16 + j), col(1), 8.0 * j - 16)
    iota(V("ia", S(16, 32)), [[1, 16]], 0, 0)
    iota(V("kf"), [[0, 16], [1, 16]], 0, 0)
    iota(V("cu"), [[255, 2], [0, 16]], 255, 0)
    lin(V("z0"), V("zin"), 64.0)
    lin(col(5), col(0), 14.0 / 64, 39.0 / 64)
    lin(col(6), col(0), 20.0 / 64, 10.0 / 64)
    lin(col(8), col(1), 64.0)
    lin(col(11), col(0), -RANK, 15 * RANK)
    lin(V("rz", S(0, 128)), V("blk"), -BIG / 64)
    lin(V("rz", S(128, 256)), V("blk"), BIG / 64)
    ts(V("rm", S(0, 8)), blk8, BIG / 32, A.mult)
    ts(V("rm", S(8, 16)), blk8, -BIG / 32, A.mult)
    lin(V("rl", S(0, 8)), blk8, -BIG / 64)
    lin(V("rg", S(16, 24)), blk8, BIG / 64)
    lin(V("rg", S(8, 16)), blk8, col(8))
    lin(V("rg", S(0, 8)), blk8, col(8))
    lin(V("rl", S(8, 16)), V("rg", S(8, 16)), -1.0)
    cp(V("idb"), V("ident"))
    ts(V("r8", S(0, 8)), blk8, col(5), A.mult)
    ts(V("r8", S(8, 16)), blk8, col(6), A.mult)
    cp(V("l0"), V("li"))
    cp(V("ex"), V("ia", S(16, 32)))
    cp(V("rw"), blk8)
    ts(V("maske"), V("kf"), col(0), A.is_equal)
    ts(V("ti", S(2, 3)), V("ti", S(0, 1)), 127, A.bitwise_and)
    ts(V("ti", S(3, 4)), V("ti", S(0, 1)), 8064, A.bitwise_and)
    cp(V("cols", S(12, 14)), V("ti", S(2, 4)))
    ts(col(12), col(12), 0.5, A.add)
    swap = V("gq", S(0, 128))
    asel(swap, V("ones"), [[-2, 64], [1, 2]], A.is_equal, 0.0, -1, 1)
    mm(V("pD", S(256, 258)), swap, V("cols", S(12, 14)), True)
    ts(V("ol2", S(0, 128)), swap, V("pD", S(256, 257)), A.mult, -BIG, A.mult)
    ts(V("ol2", S(128, 256)), V("ident"), col(13), A.mult, -BIG, A.mult)
    tt(V("ol1", S(0, 128)), V("ol2", S(0, 128)), V("ol2", S(128, 256)), A.add)
    lin(V("ol1", S(256, 384)), V("ol1", S(0, 128)), 1.0)
    for h in range(2):
        lin(V("ol1", S(256 * h + 128, 256 * h + 256)), V("ident"), -1024.0)
    lin(V("og2", S(256, 384)), V("ol1", S(0, 128)), -1.0)
    lin(V("og2", S(0, 128)), V("ident"), 1024.0)
    lin(V("og2", S(128, 256)), V("ident"), 1024.0)
    lin(V("og1", S(0, 128)), V("ident"), col(11))
    lin(V("og1", S(128, 256)), V("ident"), col(11))
    lin(V("idn"), V("ident"), -1.0)

    def late_constants():
        kk = V("kf")
        cp(V("idq"), V("ident"))
        lin(V("ck"), kk, 613.0 * 32)
        lin(V("idh"), V("ident"), 0.5)
        t0, t1 = V("tf", S(0, 192)), V("y1", S(0, 192))
        iota(t0, [[0, 4], [1, 3], [0, 16]], 0, 0)
        ts(t0, t0, 1.5, A.is_gt)
        iota(t1, [[32, 4], [16, 3], [-1, 16]], 15, -1)
        ts(V("sq", S(0, 192)), t0, 32.0, A.mult)
        tt(V("ri"), t1, V("sq", S(0, 192)), A.is_equal)
        iota(t1, [[2, 4], [1, 3], [0, 16]], 0, 0)
        tt(t1, t1, t0, A.subtract)
        ts(V("ib", S(3, 4)), V("ia", S(0, 1)), 4, A.arith_shift_right)
        cp(col(27), V("ib", S(3, 4)))
        ts(V("re_"), t1, col(27), A.is_equal, -1.0, A.mult)
        iota(V("pr", S(0, 384)), [[0, 24], [-1, 16]], 15, 0)
        ts(V("rst"), V("pr", S(0, 384)), col(0), A.is_equal, 4096.0, A.mult)
        asel(V("rst"), V("rst"), [[0, 8], [1, 3], [0, 16]], A.not_equal, 0.0, -2, 0)
        fill(V("stp"), 4096)
        lin(V("wq"), kk, 0.0)
        lin(V("idf"), V("ident"), -1.0)
        fill(V("stp", S(0, 256, 16)), -16000000)
        asel(V("blkn"), V("ones"), [[-1, 8], [0, 16]], A.is_equal, 0.0, 0, 1)
        lin(V("blkn"), V("blkn"), -BIG)
        cp(col(4), V("ia", S(0, 1)))
        ts(V("ib", S(1, 2)), V("ia", S(0, 1)), 31, A.bitwise_and)
        cp(col(7), V("ib", S(1, 2)))
        lin(col(14), col(0), 2.0, float(W + 2))
        lin(col(15), col(0), 2.0, float(W + 34))
        lin(col(10), col(0), 9.0, W / 2 + 8)
        lin(col(20), col(0), 16.0, 15.0 - 8 * 1040)
        lin(col(21), col(4), -7.0, W / 2 - 7)
        lin(col(22), col(21), -2 * RANK)
        lin(V("sel"), V("kf", S(0, 240)), 0.0)
        lin(V("sel", S(112, 128)), V("maske", S(0, 16)), 1.0)
        lin(V("selv"), V("sel"), col(21))
        ts(V("ib", S(2, 3)), V("ia", S(0, 1)), 7, A.bitwise_and)
        ts(V("ib", S(4, 5)), V("ia", S(0, 1)), 3, A.arith_shift_right, 1, A.bitwise_and)
        tt(col(24), V("ib", S(2, 3)), V("ib", S(3, 4)), A.is_equal)
        cp(col(25), V("ib", S(4, 5)))
        for i, (first, per_g, per_h, filler) in enumerate(((15, 16, 128, 256), (143, 16, 256, 512), (112, 1, 8, 128))):
            lin(col(26), col(25), float(per_h), float(first - filler))
            lin(V("g8"), V("kf", S(0, 8)), float(per_g), col(26))
            ts(V("own", S(8 * i, 8 * i + 8)), V("g8"), col(24), A.mult, float(filler), A.add)
        lin(V("ss", S(256, 264)), blk8, 0.0, -0.5)
        lin(V("sg", S(512, 520)), blk8, 0.0)
        lin(V("sm", S(128, 136)), blk8, 0.0)
        lin(col(23), col(7), 2.0, W + 2 - RANK)
        fill(V("rs2"), 2 ** 23)
        lin(V("rs2"), V("rs2"), 4.0)
        lin(V("rs2", S(0, 128, 16)), blk8, 0.0, col(23))
        lin(V("rs2", S(128, 256, 16)), blk8, 0.0, col(22))
        iota(V("cb", S(0, 16)), [[HW, 2], [256, 8]], 0, 0)
        iota(V("cb", S(16, 32)), [[HW, 2], [144, 8]], 0, 0)
        for i, c in enumerate((R64, -R64)):
            lin(V("cst", S(256 * i, 256 * i + 256)), V("maske"), 0.0, c)
        iota(V("num"), [[1, W]], 0, 0)
        if CFG["ftab"]:
            iota(V("ipart"), [[16, 128], [0, 16]], 0, 0)
            iota(V("ilo"), [[0, 128], [1, 16]], 0, 0)
            dma(V("ipart", part=S(8, 128, 16)), V("ilo", part=S(8, 128, 16)))

    XW, BW = V("xb", S(0, W)), V("xb", S(BO, BO + W))

    def first_x():
        banks = [V("pA"), V("pC"), V("pG", 0), V("pG", 1)]
        for j in range(4):
            mm(banks[j], V("dq"), V("i512", S(0, 512)), True, False)
            mm(banks[j], V("dq"), V("i512", S(512, 1024)), False, False)
        for j in range(4):
            js = S(512 * j, 512 * j + 512)
            mm(banks[j], V("i64"), V("xin", js), False, True)
            mov(V("xb", js), banks[j], col(16 + j), on="act" if j % 2 else "dve")

    def forwards(v):
        ps = V("pC" if v else "pD", S(0, 128))
        v = 0 if CFG["ftab"] else v
        for p in range(16):
            mm(ps, V("sel0" if v else "selz", S(15 - p, 143 - p)), V("w%d" % (v % 2) if v else "ft", S(p, W, 16)), p == 0)
            if p % 2:
                join(2)
                chain("f")
        if v:
            mov(V("fi2"), ps, 1024.0)
            ts(V("fi2"), V("fi2"), 2047, A.bitwise_and)
        mov(V("fw16"), V("fi2") if v else ps)

    def w_gather(v, by_dve, table):
        for a in range(0, W, CFG["wp"]):
            b = a + CFG["wp"]
            o, src = V("w%d" % (v % 2), S(a, b)), ind(table, V("fw16", S(a // 16, b // 16)))
            mov(o, src, on="dve" if a < by_dve else "act")

    def cell_part(v):
        ps = V("pD", S(128, 160))
        mm(ps, V("idb"), V("cu"), True, False)
        for wh in range(2):
            for h in range(2):
                o = 128 + 16 * wh + 8 * h
                mm(V("pD", S(o, o + 8)), half("z%d" % v, h), V("r8", S(8 * wh, 8 * wh + 8)))
        join(5)
        mov(V("qc", S(0, 32)), ps)
        ts(V("qc", S(32, 64)), V("qc", S(0, 32)), 2047, A.bitwise_and)

    def e_op(name, src):
        tt(V(name), ind(src, V("ex")), V("maske"), A.mult)

    def u_op(name, src):
        mov(V(name), ind(src, V("ex")), on="act")

    def w_mm(name, o):
        for h in range(2):
            mm(V("pD", S(o + 8 * h, o + 8 * h + 8)), half(name, h), V("rw"), True)
        join(2)

    def own_mm(name, i, win, o, sel="sel", base=None, **kw):
        act(V(name), ind(V(win), V("own", S(8 * i, 8 * i + 8))), **kw)
        if base is not None:
            mm(V("pD", S(o, o + 16)), V("idb"), V("cb", S(base, base + 16)), True)
        for j in range(8):
            mm(V("pD", S(o, o + 16)), V(sel, S(112 - 16 * j, 240 - 16 * j)), V(name, S(16 * j, 16 * j + 16)), base is None and j == 0)
        join(8 if base is None else 9)

    def dif(e, u, o, *bank):
        for h in range(2):
            mm(V(*bank, S(192 * h, 192 * h + 192)), half(e, h), V("re_"), True)
            mm(V(*bank, S(192 * h, 192 * h + 192)), half(u, h), V("ri"))
        join(4)
        act(V("sd"), V(*bank, S(0, 384)), FN.Abs)
        scan(V("pr", S(o, o + 384)), V("sd"), V("rst"), 1.0, A.min, A.max)

    def open_z(v):
        for h in range(2):
            for j in range(4):
                mm(V("pz", h, S(j, 512, 4)), V("idb"), half("z%d" % v, h), True)
            join(4)
        for name in ("gl", "gg"):
            for h in range(2):
                asel(V(name, S(HW * h + W + 1, HW * h + HW, 2)), half("z%d" % v, h), [[0, 128]], A.is_ge, 0.0, 0, 0)

    def open_l(v):
        d = [V("pL", h, S(0, 128)) for h in range(2)]
        mm(V("pL"), V("ones"), V("ol1"), True)
        for h in range(2):
            mm(d[h], half("z%d" % v, h), V("rz", S(0, 128)))
        join(2)
        if v > 0:
            for h in range(2):
                mm(d[h], V("a15", part=S(0, 8)), V("blkn", part=S(0, 8)))
            join(2)

    def open_g(v, h):
        mm(V("pG", h, S(128, 512)), V("ones"), V("og2"), True)
        mm(V("pG", h, S(384, 512)), half("z%d" % v, h), V("rz", S(128, 256)))
        join(2)

    def gather(v, side, h):
        n = CFG["gp"][2 * side + 1 - h]
        for a in range(0, 128, n):
            o = V("gg" if side else "gl", S(HW * h + 16 * a, HW * h + 16 * (a + n)))
            src = ind(V("w%d" % (v % 2), S(0, W)), V("bc" if side else "l%d" % v, S(128 * h + a, 128 * h + a + n)))
            if a < CFG["gdve"][2 * side + 1 - h]:
                mov(o, src)
            else:
                act(o, src, FN.Copy)
                chain("gh")

    def gm(side, h, k, step, a=0, b=128):
        o = 4096 * side + 2048 * h
        i = 2 * (8 * side + 4 * h + k % 4)
        return dict(V("gm", S(o + 16 * a + k, o + 16 * b, step)), reg=[("gm", i + (a > 0), i + 1 + (b == 128))])

    def g_max(side, h, j, a=0, b=128):
        tt(gm(side, h, j, 4, a, b), V("gg" if side else "gl", S(HW * h + 16 * a + j, HW * h + 16 * b, 4)), V("pz", h, S(4 * a, 4 * b)), A.max)
        chain("gm")
        name("max%d%d%d" % (side, h, j))

    def x_mm(side, h, ks, a=0, b=128):
        for k in ks:
            mm(V("pG", h, S(128 + k, 512, 16), part=S(a, b)) if side else V("pL", h, S(k, 256, 16), part=S(a, b)),
               V("gg" if side else "gl", S(HW * h + 16 * a + k, HW * h + 16 * b, 16)), V("rg" if side else "rl"))
            if k % 2:
                join(2)
                chain("x")

    def m_mm(side, h, j, a=0, b=128):
        for k in range(j, 16, 4):
            mm(V("pG", h, S(384 + k, 512, 16), part=S(a, b)) if side else V("pL", h, S(k, 128, 16), part=S(a, b)),
               gm(side, h, k, 16, a, b), V("rm", S(8 * side, 8 * side + 8)))
        join(4)

    def side_mm(side, h, a=0, b=128):
        for j in range(4):
            g_max(side, h, j, a, b)
        x_mm(side, h, range(0, 8), a, b)
        m_mm(side, h, 0, a, b)
        x_mm(side, h, range(8, 12), a, b)
        m_mm(side, h, 1, a, b)
        x_mm(side, h, range(12, 16), a, b)
        m_mm(side, h, 2, a, b)
        m_mm(side, h, 3, a, b)

    cuts = lambda c: [(0, c), (c, 128)] if c < 128 else [(0, 128)]

    Lp, Dp = V("pL", both, S(128, 256)), V("pL", both, S(0, 128))
    wcol = V("qc", S(80, 96))
    scr, ss = V("pA", S(256, 512)), V("ss", S(0, 256))
    scr15 = V("pA", S(271, 512, 16))
    vx = V("vx")

    def l_clean():
        if CFG["pur"] == "act":
            lin(V("y1"), Lp, 1.0, R4096)
            lin(V("y2"), V("y1"), 1.0, -R4096)
        else:
            ts(V("y2"), Lp, R4096, A.add, -R4096, A.add)
        tt(Lp, Lp, V("y2"), A.subtract)

    def l_rename():
        tt(scr, Lp, V("urep"), A.mult)
        name("times")
        mov(V("lq"), Lp, on="act")
        tt(V("ia"), V("ck"), scr, A.subtract)
        ts(V("rr"), V("ia"), 5, A.arith_shift_right, 2047, A.bitwise_and)

    def l_pick():
        tt(V("kf"), Dp, V("rr"), A.min)
        name("fail")
        scan(ss, V("stp"), V("kf"), 0.0, A.add, A.max)
        tt(scr, Lp, ss, A.max)
        act(V("qc", S(64, 80)), scr15, FN.Abs)
        ts(wcol, V("qc", S(64, 80)), 2047, A.bitwise_and)
        tt(V("nw"), scr, V("rr"), A.min)

    def halve(name, win, off, ps):
        mov(V(name), ind(V(win), V(off)), -16.0, 0.5, "act")

    def halve_mm(name, v, ps, stop):
        mm(ps, V("idh"), V("z%d" % v), True)
        mm(ps, V("idq"), V(name))
        mm(ps, V("idb"), V("cst", S(0, 256)), False, True)
        join(2)

    def g_pen(h):
        Ep, Fp = V("pG", h, S(384, 512)), V("pG", h, S(256, 384))
        p1, p2 = V("pen", h, S(0, 128)), V("pen", h, S(128, 256))
        either(lambda: ts(p1, Ep, 0.0, A.is_lt, SINK, A.mult), lambda: act(p1, Ep, FN.Relu, scale=-SINK * 8 / BIG))
        if CFG["pen"][1 - h] == "act":
            act(half("sq", h), Fp, FN.Abs, scale=SINK)
            act(p2, half("sq", h), FN.Relu, bias=SINK, scale=-1.0)
        else:
            ts(p2, Fp, 0.0, A.is_equal, SINK, A.mult)
        mov(half("gq", h), V("pG", h, S(128, 256)), on="act")
        kl, kg = V("pL", h, S(0, 128)), V("pL", h, S(128, 256))
        mm(V("pL", h), V("ones"), V("og1", S(0, 256)), True)
        mm(kl, V("idf"), half("lq", h))
        mm(kl, V("idn"), half("fp", h))
        join(3)
        for p in (p1, p2):
            mm(kl, V("idn"), p)
            mm(kg, V("idn"), p)
        join(4)
        mm(kg, V("ident"), half("gq", h))
        scan(V("sg", S(256 * h, 256 * h + 256)), V("rs2"), V("pL", h), 0.0, A.min, A.max)

    def count_merges():
        act(V("sgn"), V("sg", S(15, 512, 16)), FN.Sign, bias=0.5)
        ps, y = V("pL", 0, S(0, 128), part=S(0, 8)), V("qa", part=S(0, 8))
        for h in range(2):
            mm(ps, V("sgn", S(16 * h, 16 * h + 8)), V("ones"), h == 0)
        join(2)
        mov(y, ps, 128.0, 0.5, "act")
        ts(y, y, 15, A.bitwise_and)
        mov(V("a15", part=S(0, 8)), y, on="act")

    def contest(o, n, places):
        for i, c in ((0, 15), (1, 47)):
            s, p = dict(V("s4", S(i, 16 * n, 2)), reg=[("s4", i, i + 1)]), V("pr", S(o + c, o + 384 * n, 48))
            either(lambda: ts(s, p, 0.0, A.is_equal, col(14 + i), A.mult), lambda: act(s, p, FN.Relu, bias=col(14 + i), scale=-4096.0))
        tt(V("s3", S(0, 16 * n)), places, dict(V("s4", S(0, 16 * n)), reg=[("s4", 0, 2)]), A.max)

    def rounds32(win, val, off="o1", o=0):
        for r in range(7, -1, -1):
            cp(ind(win, V(off, S(o + 2 * r, o + 2 * r + 2))), V(val, S(32 * r, 32 * r + 32)))

    first_x()
    forwards(0)
    w_gather(0, CFG["w0dve"], XW)
    for v in range(VISITS):
        last = v == VISITS - 1
        named.clear()
        if v > 0:
            arrive("l%d" % v, "al%d" % v, v)
            arrive("z%d" % v, "az%d" % v, v)
            forwards(v)
        gather(v, 0, 1)
        cell_part(v)
        e_op("ec", V("qc", S(32, 48)))
        w_mm("ec", 160)
        mov(V("oc"), V("pD", S(160, 176)))
        mov(V("bc"), ind(BW if v else V("bt"), V("oc")))
        early("bc")
        open_z(v)
        open_l(v)
        if v == 0:
            late_constants()
            for j in range(4):
                asel(V("xb", S(BO + 512 * j, BO + 512 * j + 512)), V("bt", S(512 * j, 512 * j + 512)), [[0, 512]], A.is_ge, 0.0, 0, 0)
        if last:
            for a in range(0, W, 512):
                mov(V("xh", S(a, a + 512)), V("xb", S(a, a + 512)), 1024.0, 1 / 64, "act")
                mov(V("xin", S(a, a + 512)), V("xh", S(a, a + 512)), -1024.0)
            w_gather(v + 1, 0, V("num"))
        gather(v, 0, 0)
        mov(V("urep"), ind(V("qc", S(48, 64)), V("ex")), 32.0, 0.5, "act")
        u_op("uc", V("qc", S(32, 48)))
        dif("ec", "uc", 0, "pG", 0)
        if last:
            contest(0, 1, V("pD", S(160, 176)))
            mov(V("o3", S(0, 16)), V("s3", S(0, 16)))
        side_mm(0, 1)
        for a, b in cuts(CFG["cut"][0]):
            x_mm(0, 0, range(16), a, b)
        gather(v, 1, 1)
        for j in range(4):
            g_max(0, 0, j)
            m_mm(0, 0, j)
        l_clean()
        l_rename()
        for h in (1, 0):
            open_g(v, h)
        l_pick()
        gather(v, 1, 0)
        side_mm(1, 1)
        act(V("fp"), ss, FN.Relu, bias=SINK, scale=SINK / 32768)
        for h in (1, 0):
            mm(V("pG", h, S(256, 384)), V("idq"), half("lq", h))
            mm(V("pG", h, S(256, 384)), V("idb"), half("y2", h))
            join(2)
        for h in range(2):
            mm(V("pC", S(128 * h, 128 * h + 128)), half("nw", h), V("idq"), True)
        join(2)
        nk = V("nl" if last else "ls%d" % v)
        act(nk, V("pC", S(0, 256)), FN.Abs)
        if not last:
            send("ls%d" % v, "l%d" % (v + 1), "al%d" % (v + 1), v + 1)
            early("sendl")
        else:
            rounds32(V("xb", S(BO, 2 * BO)), "nl", "o3")
            dma(T.yb[:], BW)
            dma(T.yl[:], nk)
        own_mm("ev", 0, "ss", 192, "selv", 16, func=FN.Sign, bias=0.5)
        mov(V("ov"), V("pD", S(192, 208)), col(10))
        u_op("uw", wcol)
        e_op("ew", wcol)
        name("ew")
        w_mm("ew", 176)
        dif("ew", "uw", 384, "pA")
        px = V("pC", S(256, 512))
        halve("hx", "gl", "ov", px)
        halve_mm("hx", v, px, last)
        if last:
            mov(V("vxo"), px, -ROUND, 1 / 64, "act")
        else:
            mov(V("wq", S(0, 256, 16)), wcol, -16.0, 1 / 64, "act")
            mm(px, V("idb"), V("cst", S(256, 512)), False, True)
            for h in range(2):
                mm(V("pC", S(256 + 128 * h, 384 + 128 * h)), half("wq", h), V("idq"))
            join(3)
            mov(vx, px, on="act")
        if last:
            contest(384, 1, V("pD", S(176, 192)))
            mov(V("o3", S(16, 32)), V("s3", S(0, 16)))
            rounds32(V("xin"), "vxo", "o3", 16)
            dma(T.yx[:], V("xin", S(0, W)))
        else:
            contest(0, 2, V("pD", S(160, 192)))
            mov(V("o3"), V("s3"))
            rounds32(V("xb", S(0, BO)), "vx", "o3", 16)
            rounds32(V("xb", S(BO, 2 * BO)), "ls%d" % v, "o3")
            w_gather(v + 1, CFG["wdve"], XW)
        g_pen(1)
        for a, b in cuts(CFG["cut"][1]):
            side_mm(1, 0, a, b)
        g_pen(0)
        own_mm("ez", 1, "sg", 208, "sel", 0, scale=-1 / RANK, bias=1040.5 - 2.0 ** -10)
        mov(V("oz"), V("pD", S(208, 224)), col(20))
        mov(V("qi"), V("sg", S(15, 512, 16)))
        ts(V("qj"), V("qi"), 4095, A.bitwise_and)
        tt(sm(6), V("qj", both, 0), V("qj", both, 1), A.max)
        tt(sm(7), V("qj", both, 0), V("qj", both, 1), A.min)
        e_op("eh", sm(6))
        u_op("uh", sm(6))
        own_mm("el", 2, "sm", 240)
        w_mm("eh", 224)
        mov(V("ol"), V("pD", S(240, 256)))
        pzz = V("pC", S(0, 256))
        halve("hz", "gg", "oz", pzz)
        halve_mm("hz", v, pzz, True)
        if not last:
            mov(V("zs%d" % v), pzz, -R64, on="act")
            send("zs%d" % v, "z%d" % (v + 1), "az%d" % (v + 1), v + 1)
            early("sendz")
        else:
            mov(V("zs%d" % v), pzz, -ROUND, 1 / 64, "act")
            dma(T.yz[:], V("zs%d" % v))
        mov(V("vw"), ind(V("num") if last else XW, V("ol")), on="act")
        dif("eh", "uh", 0, "pA")
        contest(0, 1, V("pD", S(224, 240)))
        mov(V("o1"), V("s3", S(0, 16)))
        rounds32(V("w%d" % ((v + 1) % 2)), "vw")
        if not last:
            count_merges()
            if CFG["ftab"]:
                mov(V("vf"), ind(V("ipart"), V("ol")), on="act")
                rounds32(V("ft"), "vf")
    dma(T.yf[:], V("w%d" % (VISITS % 2), S(0, W), part=S(0, 128, 16)))

    def meet(a, b):
        return a[0] == b[0] and a[1] < b[2] and b[1] < a[2]

    def arrange(ops):
        n = len(ops)
        pre = [dict() for _ in range(n)]
        seen, lastq, sends = {}, {}, {}
        for i, o in enumerate(ops):
            for reg, wr in [(r, False) for r in o["r"]] + [(r, True) for r in o["w"]]:
                ps = SCRATCH[reg[0]][0] == "psum"
                for j, reg2, wr2 in seen.get(reg[0], []):
                    if j != i and meet(reg, reg2) and not (o.get("apart") and ops[j].get("apart")):
                        same = ops[j]["eng"] == o["eng"] and "alt" not in o and "alt" not in ops[j]
                        if same and o["eng"] == "pe":
                            if (wr or wr2) and not (o["adds"] and ops[j]["adds"]):
                                pre[i][j] = 0.0
                        elif same and wr and wr2 and not SAME_QUEUE_WAW:
                            pre[i].setdefault(j, 0.0)
                        elif wr or wr2 or (ps and not same):
                            pre[i][j] = LAT
            for reg, wr in [(r, False) for r in o["r"]] + [(r, True) for r in o["w"]]:
                old = seen.get(reg[0], [])
                if wr and not o.get("apart") and not o.get("adds"):
                    old = [e for e in old if not (reg[1] <= e[1][1] and e[1][2] <= reg[2])]
                seen[reg[0]] = old + [(i, reg, wr)]
            if o.get("chain"):
                if o["chain"] in lastq:
                    pre[i].setdefault(lastq[o["chain"]], 0.0)
                lastq[o["chain"]] = i
            if o["ext"]:
                pre[i][sends[o["sem"]]] = 0.0
            elif o["sem"] == "":
                sends[o["to"]] = i
        steps, count = {}, {}
        for i, o in enumerate(ops):
            o["at"] = i
            if o["ext"] and o["sem"].startswith("al"):
                count = {}
            what = tuple([o["eng"]] + [r[0].rstrip("0123") for r in o["w"][:1] + o["r"][:2]])
            count[what] = count.get(what, 0) + 1
            o["step"] = steps.setdefault((what, count[what]), len(steps))
        for i, o in enumerate(ops):
            for p in o.get("behind", []):
                pre[i].setdefault(p["at"], 0.0)
        suc = [[] for _ in range(n)]
        for i in range(n):
            for j in pre[i]:
                suc[j].append(i)
        hold = [100.0 if o["sem"] == "" else o["cost"] for o in ops]
        lead = [DMA[0] if o["eng"] == "sync" else 0.0 for o in ops]
        tail = [DMA[1] if o["eng"] == "sync" else o["cost"] - h for o, h in zip(ops, hold)]
        gap = [{j: d + tail[j] + lead[i] for j, d in pre[i].items()} for i in range(n)]
        back = [{k: gap[k][i] for k in suc[i]} for i in range(n)]

        def place(before, after, first, key):
            left = [len(p) for p in before]
            at = list(first)
            ready = sorted(((-key[i], i) for i in range(n) if not left[i]))
            busy = {e: ([], []) for e in set(eng)}
            while ready:
                i = ready.pop()[1]
                t, h = at[i], hold[i]
                if h:
                    starts, ends = busy[eng[i]]
                    lo, hi = 0, len(ends)
                    m = hi
                    while lo < hi:
                        mid = (lo + hi) // 2
                        if ends[mid] <= t:
                            lo = mid + 1
                        else:
                            hi = mid
                    while lo < m and starts[lo] < t + h:
                        t = ends[lo]
                        lo += 1
                    starts.insert(lo, t)
                    ends.insert(lo, t + h)
                    at[i] = t
                new = False
                for k, d in after[i].items():
                    if t + h + d > at[k]:
                        at[k] = t + h + d
                    left[k] -= 1
                    if not left[k]:
                        ready.append((-key[k], k))
                        new = True
                if new:
                    ready.sort()
            return at

        def there_and_back(key):
            late = place(back, gap, tail, [-(a + h) for a, h in zip(key, hold)])
            at = place(gap, back, lead, [-(a + h) for a, h in zip(late, hold)])
            span = max(a + h + t for a, h, t in zip(at, hold, tail))
            if span < limit[0]:
                order = sorted(range(n), key=lambda i: at[i])
                limit[1] = span
                span = (span + sum(replay(order, *m) for m in others)) / (1 + len(others))
            else:
                span = 1e9
            return span, at, list(eng)

        def replay(order, times, gaps, tails):
            end, busy, last = [0.0] * n, {e: 0.0 for e in set(eng)}, 0.0
            for i in order:
                t = busy[eng[i]] if hold[i] else 0.0
                for j, d in gaps[i]:
                    if end[j] + d > t:
                        t = end[j] + d
                t = max(t, lead[i]) + hold[i] * times[i]
                end[i] = t
                if hold[i]:
                    busy[eng[i]] = t
                last = max(last, t + tails[i])
            return last

        others, limit = [], [1e9, 0.0]
        for m in OTHER:
            tails = [t * m["remote"] if o["sem"] == "" else t for o, t in zip(ops, tail)]
            others.append(([m.get(o["kind"], 1.0) for o in ops],
                           [[(j, d * m["wait"] + tails[j] + lead[i]) for j, d in pre[i].items()] for i in range(n)], tails))

        def swap(s):
            for i in either_of[s]:
                o = ops[i] if eng[i] != ops[i]["eng"] else ops[i]["alt"]
                eng[i], hold[i] = o["eng"], o["cost"]

        either_of = {}
        for i, o in enumerate(ops):
            if "alt" in o:
                either_of.setdefault(o["step"], []).append(i)
        free = [s for s in sorted(either_of) for _ in either_of[s]]

        eng = [o["eng"] for o in ops]
        rest = [0.0] * n
        at = place(gap, back, [0.0] * n, list(range(n)))
        for i in sorted(range(n), key=lambda i: (-at[i], -i)):
            rest[i] = hold[i] + max([tail[i]] + [rest[k] + d for k, d in back[i].items()])
        best = now = there_and_back(place(gap, back, lead, [-r for r in rest]))
        rng = np.random.RandomState(0)
        step = np.array([o["step"] for o in ops])
        for k in range(PASSES):
            warm = SHAKE[3] * (1 - k / PASSES)
            at = np.array(now[1])
            if rng.rand() < 0.5:
                shake = rng.randn(n) * (abs(at - rng.rand() * now[0]) < SHAKE[1])
            else:
                shake = (rng.randn(n) * (rng.rand(n) < SHAKE[2]))[step]
            other = free[rng.randint(len(free))] if rng.rand() < SHAKE[4] else None
            if other is not None:
                swap(other)
                shake = shake * (rng.rand() < 0.5)
            got = there_and_back((at + SHAKE[0] * shake).tolist())
            if got[0] <= now[0] - warm * np.log(rng.rand()):
                now = got
                best = min(best, now)
                limit[0] = limit[1] + 4 * warm + 300.0
            elif other is not None:
                swap(other)
        MEMO["span"] = best[0]
        return sorted(range(n), key=lambda i: (best[1][i], i)), best[2]

    if "order" not in MEMO:
        MEMO["order"] = arrange(ops)
    for o, e in zip(ops, MEMO["order"][1]):
        if e != o["eng"]:
            o.update(o["alt"])
    ops = [ops[i] for i in MEMO["order"][0]]

    lastmm = {}
    for o in ops:
        for reg in o["r"] + (o["w"] if o.get("start", True) else []):
            for bank, end in lastmm.items():
                if meet(reg, bank):
                    end[0] = True
        if "end" in o:
            lastmm[o["w"][0]] = o["end"]

    hist = {}
    for i, o in enumerate(ops):
        deps = set()
        own = o["sem"] is None
        for reg, wr in [(r, False) for r in o["r"]] + [(r, True) for r in o["w"]]:
            ps = SCRATCH[reg[0]][0] == "psum"
            for j, reg2, wr2 in hist.get(reg[0], []):
                if not meet(reg, reg2) or (o.get("apart") and ops[j].get("apart")):
                    continue
                p = ops[j]
                same = own and p["sem"] is None and p["eng"] == o["eng"]
                if same:
                    need = o["eng"] != "pe" and (wr != wr2 or (SAME_QUEUE_WAW and wr))
                else:
                    need = wr or wr2 or ps
                if need and j != i:
                    deps.add(j)
        o["deps"] = deps
        for reg, wr in [(r, False) for r in o["r"]] + [(r, True) for r in o["w"]]:
            hist.setdefault(reg[0], []).append((i, reg, wr))
        for j in deps:
            ops[j]["inc"] = True
    tally = {}
    for o in ops:
        if o["sem"] is None:
            if o.get("inc"):
                tally[o["eng"]] = tally.get(o["eng"], 0) + 1
            o["tick"] = (o["eng"], tally.get(o["eng"], 0))
        else:
            o["tick"] = (o["sem"], o["count"])
    queue = {"pe": g.tensor, "dve": g.vector, "act": g.scalar, "pool": g, "sync": g.sync}
    known = {e: {} for e in queue}
    for o in ops:
        if o["ext"]:
            o["clock"] = {}
            continue
        kn = known[o["eng"]]
        for j in sorted(o["deps"], reverse=True):
            p = ops[j]
            s, n = p["tick"]
            if s == "" or kn.get(s, 0) >= n:
                continue
            queue[o["eng"]].wait_ge(T.sem[s], n)
            kn[s] = n
            for s2, n2 in p["clock"].items():
                if kn.get(s2, 0) < n2:
                    kn[s2] = n2
        o["clock"] = dict(kn)
        ins = o["fn"]()
        if o["sem"] is None:
            if o.get("inc"):
                ins.then_inc(T.sem[o["eng"]], 1)
        elif o["sem"]:
            ins.then_inc(T.sem[o["sem"]], 16)
    for e, n in tally.items():
        g.wait_ge(T.sem[e], n)
    for i in range(ndma[0]):
        g.wait_ge(T.sem["d%d" % i], 16)
    g.wait_ge(T.sem.sent, nsent[0])
